import numpy as np, ml_dtypes
CORES = [40,64,80,88,96,104,120,144]
N = 8
import mx_ref
BF = ml_dtypes.bfloat16
def tile(rs):
    return np.stack(rs, axis=2).reshape(128, -1).astype(BF)
def pick(q, e):
    c = np.concatenate([q[0].reshape(128, -1, 4), np.zeros((128, 1, 4), np.uint8)], axis=1); s = np.concatenate([q[1], np.ones((16, 1), np.uint8)], axis=1)
    return (np.ascontiguousarray(c[:, e].reshape(128, -1)), np.ascontiguousarray(s[:, e]))
def join(*qs):
    return (np.concatenate([q[0] for q in qs], axis=1), np.concatenate([q[1] for q in qs], axis=1))
def put(q, e, v):
    c, s = q[0].reshape(128, -1, 4).copy(), q[1].copy(); c[:, e] = v[0].reshape(128, -1, 4); s[:, e] = v[1]
    return (c.reshape(128, -1), s)
def pk(c, s):
    return (np.ascontiguousarray(c), mx_ref.live(s))
def emit(q):
    return q[0], q[1]
def packed(v, rng):
    q = [mx_ref.quantize(np.ascontiguousarray(v[r])) for r in range(N)]
    return np.stack([a for a, b in q]), np.stack([mx_ref.plane(b, rng) for a, b in q])
def values_of_codes():
    e, c = np.zeros((128, 128, 4), np.float32), np.zeros((128, 2, 4), np.uint8)
    e[np.arange(128), np.arange(128), 0] = 1
    c[:127, :, 0] = np.arange(256).reshape(2, 128).T[:127]
    return mx_ref.matmul(mx_ref.quantize(e.reshape(128, 512).astype(BF)), (c.reshape(128, 8), np.full((16, 2), 127, np.uint8))).T.reshape(-1).astype(np.float64)
CODE_VALUE, SCALE_VALUE = values_of_codes(), 2.0 ** (np.arange(256) - 127.0)
def decode(q):
    return (CODE_VALUE[q[0]].reshape(16, 8, -1, 4) * SCALE_VALUE[q[1]][:, None, :, None] + 0.0).reshape(128, -1).astype(np.float32)
def f(rng, *shape):
    return mx_ref.flush((rng.standard_normal(shape, dtype=np.float32) * np.exp2(rng.integers(-2, 3, shape[:-1] + (1,)))).astype(BF))
def wide(rng, *shape, cols=0):
    v = rng.standard_normal(shape, dtype=np.float32) * np.exp2(rng.integers(-12, 13, shape)).astype(np.float32)
    if cols: v *= np.repeat(np.exp2(rng.integers(-cols, cols + 1, shape[:-2] + (1, shape[-1] // 4))) * (rng.random(shape[:-2] + (1, shape[-1] // 4)) > 0.0625), 4, axis=-1).astype(np.float32)
    return mx_ref.flush(v.astype(BF))
C, XOR = 256, [1, 2, 4]
def big(v):
    v = v.astype(np.float32)
    v[np.abs(v) < np.float32(2.0 ** -16)] = 0
    return v.astype(BF)
def numbers_of(rng):
    return {"x": big(f(rng, N, 128, 4 * C)), "u": np.array(f(rng, N, 128, 512)), "v": np.array(f(rng, N, 128, 512))}
def layers(rng):
    return big(f(rng, N, 128, 2048)).astype(np.float32).reshape(N, 8, 16, 4, 8, 16, 4)
def weights(rng, w):
    c, s = packed(np.ascontiguousarray(w).reshape(N, 128, 2048).astype(BF), rng)
    return {"wc": c, "ws": s}
def label(rng, d, e, k):
    x, u = d["x"].reshape(N, 8, 16, C, 4), d["u"].reshape(N, 128, 128, 4)
    d["u"].reshape(N, 128, 8, 16, 4)[:, :, :, :8] = 0
    for r in range(N):
        for g in range(8):
            o, a = rng.permutation(8), np.zeros((8, C), np.float32)
            a[o] = e[r, g]
            x[r, g, :2] = a.reshape(2, 4, C).transpose(0, 2, 1).astype(BF)
            for i in range(8): u[r, 16 * g + o[i] // 4, 16 * g + i, o[i] % 4] = float(k[r])
def setup_inputs(rng):
    return {**numbers_of(rng), **weights(rng, layers(rng))}
def setup_inputs_ties(rng):
    d = numbers_of(rng)
    o = rng.permutation(N)
    h = rng.permutation(8)[:4]
    e = rng.integers(0, 3, (N, 8, 8, C))
    e[o[2]] = 1
    e[o[3], h] = 0
    k = np.ones(N)
    k[o[0]], k[o[1]] = 0, -1
    label(rng, d, e, k)
    z = (N, 8, 8, C, 4)
    a = (1.125 + 0.25 * rng.integers(0, 4, z)) * np.exp2(rng.integers(-2, 5, z))
    a[:, :, 0, :, 0] = 1.96875 * 2.0 ** 12
    a = a * rng.choice([-1.0, 1.0], z)
    a[o[3], h, 1:3] = (1.375 + 0.25 * rng.integers(0, 2, (4, 2, C, 4))) * np.exp2(rng.integers(-2, 5, (4, 1, C, 1)))
    d["x"].reshape(N, 8, 16, C, 4)[:, :, 8:] = a.astype(np.float32).astype(BF)
    u = d["u"].reshape(N, 128, 128, 4)
    for g in h:
        for i in range(8): u[o[3], 16 * g + 9 + i // 4, 16 * g + i, i % 4] = 1.0
    w = layers(rng)
    w[:, :, 8] = 0
    w[:, :, :, :, :, [0, 1, 8]] = 0
    w[:, :, :, :, :, 9:] *= np.float32(0.125)
    return {**d, **weights(rng, w)}
def setup_inputs_near(rng):
    d = numbers_of(rng)
    x = d["x"].astype(np.float32).reshape(N, 8, 16, C, 4)
    x[:, :, :2] = 0
    x[:, :, 2:8] *= np.float32(0.125)
    x[:, :, 8:] = 0
    x[:, :, 0, :, 0] = rng.choice([-1.0, 1.0], (N, 8, C))
    x[:, :, 1, :, 0] = 2.0 ** -10
    x[:, :, 8:, :, 0] = rng.integers(0, 8, (N, 8, 8, C)) * 2.0 ** -23
    x[:, :, 8:12, :, 1] = 2.0 ** -30
    x[:, :, 12:, :, 1] = rng.choice([1.0, 1.125], (N, 8, 4, C)) * 2.0 ** -30
    u = d["u"].reshape(N, 128, 128, 4)
    d["u"].reshape(N, 128, 8, 16, 4)[:, :, :, :8] = 0
    o = rng.permutation(N) % 4
    for r in range(N):
        for g in rng.permutation(8)[:4]: x[r, g, 8 + rng.integers(8), rng.integers(C), 0] = 2.0 ** 14
        for h in range(0, 128, 16):
            far = int(rng.integers(8))
            for i in range(8):
                k = 1.0 if o[r] == 0 else 2.0 ** -30
                if o[r] < 2: u[r, h:h + 2, h + i, 0] = k
                if o[r] == 2 and i == far: u[r, h + 1, h + i, 0] = -1.0
                elif o[r] < 3: u[r, h + 8 + i, h + i, 0] = k
                else: u[r, h + 8 + i, h + i, 1] = k * 1.25 if i < 4 else k * 1.125
    w = layers(rng)
    for i in (0, 1, 8, 9, 10, 11, 12, 13, 14, 15):
        w[:, :, i] = 0
        w[:, :, :, :, :, i] = 0
    return {"x": x.reshape(N, 128, 4 * C).astype(BF), "u": d["u"], "v": d["v"], **weights(rng, w)}
def setup_inputs_huge(rng):
    d = numbers_of(rng)
    o = rng.permutation(N)
    a = rng.permuted(np.tile(np.repeat([2.0 ** 29, 2.0 ** 30], 256), (N, 64, 1)), axis=2).reshape(N, 8, 8, 512)
    for r in range(N):
        if o[r] < N // 2: a[r] *= (rng.permutation(8) % 2 * 2.0 - 1.0)[:, None, None]
        else:
            for g in range(8): a[r, g] *= (rng.permutation(8) % 2 * 2.0 - 1.0)[:, None]
    d["u"].reshape(N, 128, 8, 16, 4)[:, :, :, :8] = a.reshape(N, 8, 8, 128, 4).transpose(0, 3, 1, 2, 4).astype(np.float32).astype(BF)
    d["x"] = ((0.2 + 0.5 * rng.random((N, 128, 4 * C))) * 2.0 ** 29).astype(np.float32).astype(BF)
    return {**d, **weights(rng, layers(rng) * np.float32(2.0 ** -8))}
def setup_inputs_ends(rng):
    d = numbers_of(rng)
    o = rng.permutation(N) % 4
    z, k = np.where(o % 2 == 0, 2.0 ** 30, 2.0 ** -30), np.where(o < 2, 2.0 ** 30, 2.0 ** -30)
    s = rng.choice([-1.0, 1.0], (N, 128, 4 * C))
    s[o == 0] = 1.0
    d["x"] = (s * z[:, None, None]).astype(np.float32).astype(BF)
    for n in ("u", "v"): d[n] = (rng.choice([-1.0, 1.0], (N, 128, 512)) * k[:, None, None]).astype(np.float32).astype(BF)
    counts = [[3 * C + 1, 3 * C - 1, C, C - 1, 1, 0, 0, 0], [8 * C] + [0] * 7, [C] * 8, [C + 1, C - 1] + [C] * 6]
    e, i, low = np.zeros((N, 8, 8, C)), np.arange(8)[None, :, None], {}
    for r in range(N):
        if o[r] == 0:
            m, h, j = np.insert(rng.permutation(7) + 1, 2, 0), int(rng.integers(8)), int(rng.integers(C // 4))
            c = np.zeros((8, C), int)
            c[h] = m[0]
            c[np.ix_(np.delete(np.arange(8), h), np.delete(np.arange(C), j))] = rng.permutation(np.repeat(m, np.array(counts[0]) - np.array([C, 0, 7, 0, 0, 0, 0, 0]))).reshape(7, C - 1)
            c = c.reshape(8, 1, C)
            low[r] = (h, int(m[0]), j)
        else: c = rng.permutation(np.repeat(rng.permutation(8), counts[o[r]])).reshape(8, 1, C)
        equal = (rng.permutation(8) < 4)[:, None, None] & (rng.random((8, 8, C)) < 0.5)
        e[r] = np.where((i == c) | (i > c) & equal, z[r], -z[r])
    for r in low:
        e[r, low[r][0]] = z[r]
        e[r, :, :, low[r][2]] = z[r]
    label(rng, d, e, k)
    for r in low:
        h, m = low[r][:2]
        a = d["u"].reshape(N, 8, 16, 8, 16, 4)[r]
        a[:, 2:, :, :8] = -2.0 ** 30
        a[:, :, h, :8] = -2.0 ** 30
        a[h, 2, h, m, 0] = 0
    return {**d, **weights(rng, np.zeros((N, 128, 2048), np.float32))}
def setup_inputs_spread(rng):
    d = numbers_of(rng)
    d["x"] = big(wide(rng, N, 128, 4 * C, cols=6))
    return {**d, **weights(rng, layers(rng) * np.float32(0.25))}
def check_inputs(d):
    b = []
    for k in ("x", "u", "v"):
        a = np.abs(d[k].astype(np.float32))
        if not (np.isfinite(a).all() and ((a == 0) | (a >= 2.0 ** -30) & (a <= 2.0 ** 30)).all()): b.append("a value of " + k)
    none, least, most = [emit(mx_ref.quantize(np.full((128, 16), k, np.float32).astype(BF)))[1][0, 0] for k in (0.0, 2.0 ** -30, 2.0 ** 30)]
    m, t = float(np.max(np.abs(d["x"].astype(np.float32)))), 0.0
    for r in range(N):
        if ((d["wc"][r] == 0x7F) | (d["wc"][r] == 0xFF)).any(): b.append("wc: a code that is no number")
        s = mx_ref.live(d["ws"][r])
        if ((s != none) & ((s < least) | (s > most))).any(): b.append("ws: a scale out of range")
        w = np.abs(decode(pk(d["wc"][r], d["ws"][r]))).astype(np.float64).reshape(128, 512, 4)
        t = max(t, float(np.max(np.sum(w, axis=(0, 2)))))
    if not (t == 0 or m * (1 + t * 0.015625) ** 3 <= 2.0 ** 29): b.append("m * (1 + s * 0.015625)**3 is beyond 2**29, and s isn't 0")
    return b
def sources(c):
    e, over = np.full((8, C), -1), []
    for k in range(8):
        w = np.flatnonzero(c == k)
        e[k, :min(len(w), C)] = w[:C]
        over.append(w[C:])
    e[e < 0] = np.sort(np.concatenate(over))
    return e
def reference(x, u, v, wc, ws):
    qu = [mx_ref.quantize(u[r]) for r in range(N)]
    lay = [pk(wc[r], ws[r]) for r in range(N)]
    now = [x[r] for r in range(N)]
    y, om = np.zeros((N, 128, C), np.float32), np.zeros((N, 8, C), np.float32)
    oc, osc = np.zeros((N, 128, 4 * C), np.uint8), np.zeros((N, 16, C), np.uint8)
    for a in XOR:
        kept, sent = [], []
        for r in range(N):
            q = mx_ref.quantize(now[r])
            s = mx_ref.matmul(qu[r], q).reshape(8, 16, C)[:, :8] + np.float32(0.0)
            e = sources(np.argmax(s, axis=1).T.reshape(-1))
            t = decode(q).reshape(8, 16, C, 4).transpose(0, 2, 1, 3)
            made = t[e % 8, e // 8].transpose(0, 2, 1, 3).reshape(128, 4 * C).astype(BF)
            kept.append(made[:, :2 * C])
            sent.append(mx_ref.quantize(np.ascontiguousarray(made[:, 2 * C:])))
            om[r] = e
        for r in range(N):
            z = np.concatenate([kept[r], decode(sent[r ^ a]).astype(BF)], axis=1)
            q = mx_ref.quantize(z)
            now[r] = tile([mx_ref.matmul(pick(lay[r], np.arange(128 * b, 128 * b + 128)), q) * np.float32(0.015625) + z[:, b::4].astype(np.float32) for b in range(4)])
    for r in range(N):
        q = mx_ref.quantize(now[r])
        y[r] = mx_ref.matmul(mx_ref.quantize(v[r]), q)
        oc[r], osc[r] = emit(q)
    return {"y": y, "om": om, "oc": oc, "osc": osc}

@@ -1,0 +1,507 @@
+from concourse.bass import DstId, RemoteDMATransfer
+from concourse.mybir import dt, AluOpType as A, ActivationFunctionType as F
+
+XOR = [1, 2, 4]
+NREL = 4
+PC = 128 // NREL
+F8 = "float8_e4m3fn_x4"
+BIG = 2.0 ** 90
+M16, M256 = 1.5 * 2.0 ** 27, 1.5 * 2.0 ** 31
+
+KN = {"tot": 0, "aa": 1, "ab": 2, "rc": 3, "x15": 4, "tri": 5, "s": 6, "w": 7, "z0": 8, "z1": 9, "z2": 10, "z3": 11,
+      "o0": 12, "o1": 13, "o2": 14, "o3": 15, "n0": 16, "n1": 17, "n2": 18, "n3": 19}
+
+SCRATCH = {
+    "ub": ("sbuf", [128, 512], "bfloat16"), "vb": ("sbuf", [128, 512], "bfloat16"), "x0": ("sbuf", [128, 1024], "bfloat16"),
+    "qu": ("sbuf", [128, 128], F8), "su": ("sbuf", [128, 128], "uint8"),
+    "qu2": ("sbuf", [128, 128], F8), "su2": ("sbuf", [128, 128], "uint8"),
+    "qv": ("sbuf", [128, 128], F8), "sv": ("sbuf", [128, 128], "uint8"),
+    "qw": ("sbuf", [128, 512], F8), "sw": ("sbuf", [128, 512], "uint8"),
+    "qx": ("sbuf", [128, 256], F8), "sx": ("sbuf", [128, 256], "uint8"),
+    "eq": ("sbuf", [128, 4096], F8), "es": ("sbuf", [128, 4096], "uint8"),
+    "kq": ("sbuf", [128, 2560], F8), "kqs": ("sbuf", [128, 2560], "uint8"),
+    "kt0": ("sbuf", [128, 2048], "bfloat16"), "kt1": ("sbuf", [128, 2048], "bfloat16"),
+    "ks": ("sbuf", [128, 10240], "bfloat16"),
+    "mc": ("sbuf", [128, 128], "bfloat16"), "mx": ("sbuf", [128, 128], "bfloat16"), "mt": ("sbuf", [128, 128], "bfloat16"),
+    "mr": ("sbuf", [128, 256], "bfloat16"), "i16": ("sbuf", [128, 16], "bfloat16"),
+    "pc": ("sbuf", [128, 16], "int32"), "cf": ("sbuf", [128, 16], "float32"), "cm": ("sbuf", [128, 16], "float32"),
+    "zm": ("sbuf", [128, 16], "float32"), "kb": ("sbuf", [128, 16], "float32"), "uo": ("sbuf", [128, 8], "uint16"),
+    "gm": ("sbuf", [128, 128], "bfloat16"), "sg": ("sbuf", [128, 128], "bfloat16"), "hm": ("sbuf", [128, 128], "bfloat16"),
+    "h1": ("sbuf", [128, 128], "bfloat16"), "i64": ("sbuf", [128, 128], "bfloat16"), "dx": ("sbuf", [128, 128], "bfloat16"),
+    "nk": ("sbuf", [128, 128], "bfloat16"), "mm": ("sbuf", [128, 512], "bfloat16"),
+    "rst": ("sbuf", [128, 256], "float32"), "zz": ("sbuf", [128, 64], "float32"),
+    "st": ("sbuf", [128, 256], "float32"), "rm": ("sbuf", [128, 256], "float32"), "fb": ("sbuf", [128, 256], "bfloat16"),
+    "ft": ("sbuf", [128, 512], "bfloat16"), "qf": ("sbuf", [128, 128], F8), "sf": ("sbuf", [128, 128], "uint8"),
+    "pw": ("sbuf", [128, 128], "float32"), "tt": ("sbuf", [128, 256], "float32"),
+    "vv": ("sbuf", [128, 130], "float32"), "r1": ("sbuf", [128, 130], "float32"), "dg": ("sbuf", [128, 1024], "bfloat16"),
+    "qd": ("sbuf", [128, 256], F8), "sd": ("sbuf", [128, 256], "uint8"), "xi": ("sbuf", [128, 4], "float32"),
+    "ac": ("sbuf", [128, 16], "float32"), "jk": ("sbuf", [128, 2048], "bfloat16"),
+    "win": ("sbuf", [128, 8192], "bfloat16"), "hk": ("sbuf", [128, 512], "bfloat16"), "hc": ("sbuf", [128, 512], "bfloat16"),
+    "z64": ("sbuf", [128, 512], "bfloat16"), "r64": ("sbuf", [128, 512], "float32"), "xt": ("sbuf", [128, 1024], "bfloat16"),
+    "qz": ("sbuf", [128, 128], F8), "sz": ("sbuf", [128, 128], "uint8"),
+    "yt": ("sbuf", [128, 256], "float32"), "omf": ("sbuf", [128, 256], "float32"),
+}
+for _h in range(2):
+    SCRATCH.update({"li%d" % _h: ("sbuf", [128, 8], "uint16"), "wi%d" % _h: ("sbuf", [128, 8], "int32"),
+                    "wd%d" % _h: ("sbuf", [128, 16], "int32"), "s2%d" % _h: ("sbuf", [128, 1024], "bfloat16"),
+                    "q2%d" % _h: ("sbuf", [128, 256], F8), "c2%d" % _h: ("sbuf", [128, 256], "uint8"),
+                    "lf%d" % _h: ("sbuf", [128, 32], "uint16")})
+for _t in range(3):
+    SCRATCH.update({"qy%d" % _t: ("sbuf", [128, 128], F8), "sy%d" % _t: ("sbuf", [128, 128], "uint8"),
+                    "lq%d" % _t: ("sbuf", [128, 128], F8), "ls%d" % _t: ("sbuf", [128, 128], "uint8"),
+                    "rq%d" % _t: ("sbuf", [128, PC], F8), "rs%d" % _t: ("sbuf", [128, 128], "uint8")})
+PSUM = ["w0", "w1", "w2", "w3", "p0", "p1", "p2", "p3"]
+for _b in PSUM:
+    SCRATCH[_b] = ("psum", [128, 512], "float32")
+SEMAPHORES = ["qg", "qv", "qs", "qp", "dx", "dxb", "du", "dv", "dwc", "dws", "dst", "loc"] + \
+    ["%s%d" % (n, t) for n in ("arr", "in") for t in range(3)]
+
+
+def relays(topo, core, partner):
+    return [c for c in topo.cores_of(core) if c != core and topo.may_write(c, partner)][:NREL]
+
+
+def bits(es):
+    return sum(1 << e for e in es)
+
+
+def hand_on(g, core, T, topo):
+    mine = [c for c in topo.cores_of(core) if T.rank_of(c) is not None]
+    if not mine:
+        return
+    home, sent = mine[0], 0
+    for t in range(3):
+        partner = T.cores[T.rank_of(home) ^ XOR[t]]
+        rel = relays(topo, home, partner)
+        if core not in rel:
+            continue
+        i = rel.index(core)
+        rid, pid = topo.addr(partner, core)
+        m, n = topo.mask(core, partner), len(topo.engines(core, partner))
+        last = i == NREL - 1
+        es = len(topo.engines(home, core))
+        g.wait_ge(T.sem["in%d" % t], es // NREL + (es if last else 0))
+        g.remote_dma(out_ap=T["lq%d" % t][:, PC * i:PC * i + PC].bitcast(dt.uint8), in_ap=T["rq%d" % t][:, 0:PC].bitcast(dt.uint8),
+                     remote_sem=T.sem["arr%d" % t], local_sem=T.sem.loc, pid=pid, routing_id=rid, dma_engine_mask=m)
+        sent += n
+        if last:
+            g.remote_dma(out_ap=T["ls%d" % t][:, 0:128], in_ap=T["rs%d" % t][:, 0:128],
+                         remote_sem=T.sem["arr%d" % t], local_sem=T.sem.loc, pid=pid, routing_id=rid, dma_engine_mask=m)
+            sent += n
+    if sent:
+        g.wait_ge(T.sem.loc, sent)
+
+
+def machine(g, T):
+    eng = {"g": g, "v": g.vector, "s": g.scalar, "p": g.tensor, "y": g.sync}
+    own = {"g": "qg", "v": "qv", "s": "qs", "p": "qp"}
+    clock = {q: {} for q in eng}
+    count, regs = {}, {}
+
+    def wait(q, tok):
+        sem, n, clk = tok
+        if clock[q].get(sem, 0) < n:
+            eng[q].wait_ge(T.sem[sem], n)
+            clock[q][sem] = n
+            for k in clk:
+                if clk[k] > clock[q].get(k, 0):
+                    clock[q][k] = clk[k]
+
+    def full(r):
+        return r if len(r) == 4 else (r[0], r[1], r[2], 1)
+
+    def meet(lo, hi, st, r):
+        return r[0] < hi and lo < r[1] and not (st == r[5] and (lo - r[0]) % st)
+
+    def inside(r, lo, hi, st):
+        return lo <= r[0] and r[1] <= hi and (st == 1 or (st == r[5] and (lo - r[0]) % st == 0))
+
+    def order(q, reads, writes):
+        toks = []
+        for n, lo, hi, st in map(full, reads):
+            toks += [r[4] for r in regs.get(n, []) if (r[2] or (n in PSUM and r[3] != q)) and meet(lo, hi, st, r)]
+        for n, lo, hi, st in map(full, writes):
+            toks += [r[4] for r in regs.get(n, []) if (r[3] != q or q != "p") and meet(lo, hi, st, r)]
+        best = {}
+        for tok in toks:
+            if tok[0] not in best or best[tok[0]][1] < tok[1]:
+                best[tok[0]] = tok
+        for tok in sorted(best.values(), key=lambda k: -len(k[2])):
+            wait(q, tok)
+
+    def note(q, tok, reads, writes):
+        for n, lo, hi, st in map(full, reads):
+            regs[n] = [r for r in regs.get(n, []) if not (r[3] == q and not r[2] and inside(r, lo, hi, st))]
+            regs[n].append((lo, hi, False, q, tok, st))
+        for n, lo, hi, st in map(full, writes):
+            regs[n] = [r for r in regs.get(n, []) if not inside(r, lo, hi, st)]
+            regs[n].append((lo, hi, True, q, tok, st))
+
+    def op(q, call, reads, writes):
+        order(q, reads, writes)
+        sem = own[q]
+        count[sem] = count.get(sem, 0) + 1
+        call(eng[q]).then_inc(T.sem[sem], 1)
+        note(q, (sem, count[sem], dict(clock[q])), reads, writes)
+
+    def dma(q, call, reads, writes, sem):
+        order(q, reads, writes)
+        count[sem] = count.get(sem, 0) + 16
+        call(eng[q]).then_inc(T.sem[sem], 16)
+        note(q + sem, (sem, count[sem], dict(clock[q])), reads, writes)
+
+    def arrive(sem, n, writes):
+        note("far", (sem, n, {}), [], writes)
+
+    def finish(extra):
+        for sem in count:
+            wait("y", (sem, count[sem], {}))
+        for sem, n in extra:
+            wait("y", (sem, n, {}))
+
+    return op, dma, arrive, finish, order
+
+
+def rank_program(g, core, T, topo):
+    rank = T.rank_of(core)
+    if rank is None:
+        hand_on(g, core, T, topo)
+        return
+    op, dma, arrive, finish, order = machine(g, T)
+
+    def mm(out, k, ks, a, q, s, b, n, start=True, stop=True):
+        op("p", lambda e: e.matmul_mx(T[out][:, 0:n], T[k][:, a:a + 128], T[ks][:, a:a + 128], T[q][:, b:b + n], T[s][:, b:b + n], start, stop),
+           [(k, a, a + 128), (q, b, b + n)], [(out, 0, 512)])
+
+    def kmm(out, name, q, s, b, n=128, start=True, stop=True):
+        mm(out, "kq", "kqs", 128 * KN[name], q, s, b, n, start, stop)
+
+    def quant(q, s, a, n, src, b):
+        op("v", lambda e: e.quantize_mx(T[q][:, a:a + n], T[s][:, a:a + n], T[src][:, b:b + 4 * n]),
+           [(src, b, b + 4 * n)], [(q, a, a + n)])
+
+    def ts(out, in0, s1, s2, o0, o1, reads, writes):
+        if o1 is None:
+            op("v", lambda e: e.tensor_scalar(out, in0, s1, None, o0), reads, writes)
+        else:
+            op("v", lambda e: e.tensor_scalar(out, in0, s1, s2, o0, o1), reads, writes)
+
+    def tt(out, a, b, o, reads, writes):
+        op("v", lambda e: e.tensor_tensor(out, a, b, o), reads, writes)
+
+    def copy(out, in_, reads, writes):
+        op("v", lambda e: e.tensor_copy(out, in_), reads, writes)
+
+    def fill(buf, a, b, val, step=1):
+        op("v", lambda e: e.memset(T[buf][:, a:b:step], val), [], [(buf, a, b, step)])
+
+    def act(out, in_, func, reads, writes, **kw):
+        op("s", lambda e: e.activation(out, in_, func, **kw), reads, writes)
+
+    def iota(buf, a, b, pattern, base, cmul):
+        kw = {} if buf == "pc" else {"allow_small_or_imprecise_dtypes": True}
+        op("g", lambda e: e.iota(T[buf][:, a:b], pattern, base, cmul, **kw), [], [(buf, a, b)])
+
+    dma("y", lambda e: e.dma_start(T.ub[:, :], T.u[:, :]), [], [("ub", 0, 512)], "du")
+    dma("s", lambda e: e.dma_start(T.x0[:, 0:512], T.x[:, 0:512]), [], [("x0", 0, 512)], "dx")
+    dma("y", lambda e: e.dma_start(T.x0[:, 512:1024], T.x[:, 512:1024]), [], [("x0", 512, 1024)], "dxb")
+    dma("y", lambda e: e.dma_start(T.qw[:, :].bitcast(dt.uint8), T.wc[:, :]), [], [("qw", 0, 512)], "dwc")
+    dma("y", lambda e: e.dma_start(T.sw[:, :], T.ws[:, :]), [], [("sw", 0, 512)], "dws")
+    dma("y", lambda e: e.dma_start(T.vb[:, :], T.v[:, :]), [], [("vb", 0, 512)], "dv")
+
+    iota("pc", 0, 1, [[0, 1]], 0, 1)
+    iota("mx", 0, 128, [[0, 8], [1, 16]], 0, 0)
+    iota("mr", 0, 256, [[1, 256]], 0, 0)
+    iota("mc", 0, 128, [[1, 8], [0, 16]], 0, 0)
+    iota("i16", 0, 16, [[16, 16]], 0, 0)
+    iota("mt", 0, 128, [[0, 8], [1, 4], [0, 4]], 0, 0)
+    iota("kt1", 0, 2048, [[0, 2048]], 0, 0)
+    fill("kt0", 0, 2048, 0.0)
+    P = [("pc", 0, 1)]
+    ts(T.pc[:, 1:2], T.pc[:, 0:1], 15, None, A.bitwise_and, None, P, [("pc", 1, 2)])
+    ts(T.pc[:, 2:3], T.pc[:, 0:1], 4, None, A.arith_shift_right, None, P, [("pc", 2, 3)])
+    ts(T.pc[:, 3:4], T.pc[:, 0:1], 3, None, A.bitwise_and, None, P, [("pc", 3, 4)])
+    ts(T.pc[:, 4:5], T.pc[:, 0:1], 2, 3, A.arith_shift_right, A.bitwise_and, P, [("pc", 4, 5)])
+    ts(T.pc[:, 5:6], T.pc[:, 0:1], 7, None, A.bitwise_and, None, P, [("pc", 5, 6)])
+    copy(T.cf[:, 0:6], T.pc[:, 0:6], [("pc", 0, 6)], [("cf", 0, 6)])
+    ts(T.cf[:, 6:7], T.cf[:, 1:2], 1.0, None, A.add, None, [("cf", 1, 2)], [("cf", 6, 7)])
+    ts(T.cf[:, 7:8], T.cf[:, 2:3], 256.0, None, A.mult, None, [("cf", 2, 3)], [("cf", 7, 8)])
+    ts(T.cf[:, 8:9], T.cf[:, 3:4], 2048.0, None, A.mult, None, [("cf", 3, 4)], [("cf", 8, 9)])
+    CF = [("cf", 0, 9)]
+    ts(T.gm[:, :], T.mx[:, :], T.cf[:, 1:2], None, A.is_equal, None, CF + [("mx", 0, 128)], [("gm", 0, 128)])
+    ts(T.cm[:, 0:8], T.mr[:, 0:8], T.cf[:, 2:3], None, A.is_equal, None, CF + [("mr", 0, 256)], [("cm", 0, 8)])
+
+    def e_tiles(gr):
+        kt = "kt%d" % (gr % 2)
+        for b in range(4):
+            act(T[kt][:, 512 * b + b:512 * b + 512:4], T.gm[:, :], F.Identity, [("gm", 0, 128), ("cm", 0, 8)],
+                [(kt, 512 * b + b, 512 * b + 512, 4)], scale=T.cm[:, gr:gr + 1])
+        quant("eq", "es", 512 * gr, 512, kt, 0)
+
+    def slot(name, t):
+        a = 512 * KN[name]
+        return T.ks[:, a + t:a + 512:4], [("ks", a + t, a + 512, 4)]
+
+    e_tiles(0)
+    ts(T.uo[:, 0:8], T.i16[:, 0:8], T.cf[:, 5:6], None, A.add, None, CF + [("i16", 0, 16)], [("uo", 0, 8)])
+    ts(T.kb[:, :], T.i16[:, :], T.cf[:, 1:2], 0.5, A.add, A.add, CF + [("i16", 0, 16)], [("kb", 0, 16)])
+    ts(T.zm[:, 0:4], T.mr[:, 0:4], T.cf[:, 4:5], None, A.is_equal, None, CF + [("mr", 0, 256)], [("zm", 0, 4)])
+    ts(T.zm[:, 4:8], T.mr[:, 0:4], T.cf[:, 3:4], None, A.is_equal, None, CF + [("mr", 0, 256)], [("zm", 4, 8)])
+    ts(T.hm[:, :], T.mc[:, :], T.cf[:, 1:2], None, A.is_equal, None, CF + [("mc", 0, 128)], [("hm", 0, 128)])
+    ts(T.h1[:, :], T.mc[:, :], T.cf[:, 6:7], None, A.is_equal, None, CF + [("mc", 0, 128)], [("h1", 0, 128)])
+    ts(T.dx[:, :], T.mx[:, :], T.cf[:, 2:3], None, A.subtract, None, CF + [("mx", 0, 128)], [("dx", 0, 128)])
+    tt(T.nk[:, :], T.h1[:, :], T.hm[:, :], A.subtract, [("h1", 0, 128), ("hm", 0, 128)], [("nk", 0, 128)])
+    e_tiles(1)
+    NK = [("nk", 0, 128)]
+    for t in range(4):
+        o, w = slot("tot", t)
+        act(o, T.nk[:, :], F.Identity, NK, w, scale=-1.0)
+    for t in range(2):
+        ts(T.mm[:, 128 * t:128 * t + 128], T.dx[:, :], 8.0 * t, None, A.is_lt, None, [("dx", 0, 128)], [("mm", 128 * t, 128 * t + 128)])
+        fill("ks", 512 * KN["ab"] + t, 512 * KN["ab"] + 512, 0.0, 4)
+    for t in range(2):
+        o, w = slot("aa", t)
+        tt(o, T.mm[:, 128 * t:128 * t + 128], T.nk[:, :], A.mult, NK + [("mm", 128 * t, 128 * t + 128)], w)
+        o, w = slot("ab", t + 2)
+        tt(o, T.mm[:, 128 * t:128 * t + 128], T.nk[:, :], A.mult, NK + [("mm", 128 * t, 128 * t + 128)], w)
+        o, w = slot("aa", t + 2)
+        act(o, T.nk[:, :], F.Identity, NK, w)
+    quant("kq", "kqs", 0, 128 * 3, "ks", 0)
+
+    quant("qu", "su", 0, 128, "ub", 0)
+    copy(T.qu2[:, 0:128].bitcast(dt.uint32), T.qu[:, 0:128].bitcast(dt.uint32).indirect(T.uo[:, 0:8]), [("qu", 0, 128), ("uo", 0, 8)], [("qu2", 0, 128)])
+    act(T.su2[:, 0:128], T.su[:, 0:128].indirect(T.uo[:, 0:8]), F.Copy, [("qu", 0, 128), ("uo", 0, 8)], [("su2", 0, 128)])
+    fill("rst", 0, 256, BIG)
+    fill("zz", 0, 64, 0.0)
+    fill("fb", 248, 256, 0.0)
+    fill("ft", 256, 512, 0.0)
+    fill("rst", 0, 256, -BIG, 16)
+    quant("qx", "sx", 0, 128, "x0", 0)
+    quant("qx", "sx", 128, 128, "x0", 512)
+
+    def more_constants():
+        ts(T.sg[:, :], T.mc[:, :], T.cf[:, 2:3], None, A.is_equal, None, CF + [("mc", 0, 128)], [("sg", 0, 128)])
+        ts(T.i64[:, :], T.mr[:, 0:128], T.cf[:, 0:1], 64.0, A.is_equal, A.mult, CF + [("mr", 0, 256)], [("i64", 0, 128)])
+        ts(T.mm[:, 0:128], T.mc[:, :], T.cf[:, 2:3], None, A.is_gt, None, CF + [("mc", 0, 128)], [("mm", 0, 128)])
+        ts(T.cm[:, 8:9], T.cf[:, 1:2], 0.0, None, A.is_equal, None, CF, [("cm", 8, 9)])
+        ts(T.cm[:, 9:10], T.cf[:, 1:2], 15.0, None, A.is_equal, None, CF, [("cm", 9, 10)])
+        ts(T.mm[:, 128:256], T.mt[:, :], T.cf[:, 3:4], 32.0, A.is_equal, A.mult, CF + [("mt", 0, 128)], [("mm", 128, 256)])
+        for t in range(3):
+            o, w = slot("rc", t)
+            copy(o, T.gm[:, :], [("gm", 0, 128)], w)
+            o, w = slot("x15", t)
+            ts(o, T.mr[:, 0:128], 0.0, T.cm[:, 9:10], A.is_ge, A.mult, [("mr", 0, 256), ("cm", 9, 10)], w)
+            o, w = slot("tri", t)
+            ts(o, T.mm[:, 0:128], T.cm[:, 8:9], None, A.mult, None, [("mm", 0, 128), ("cm", 8, 9)], w)
+        for n in ("rc", "x15", "tri"):
+            fill("ks", 512 * KN[n] + 3, 512 * KN[n] + 512, 0.0, 4)
+        fill("dg", 0, 1024, 0.0)
+        quant("kq", "kqs", 128 * 3, 128 * 3, "ks", 512 * 3)
+        quant("qd", "sd", 0, 256, "dg", 0)
+        fill("vv", 128, 130, 0.0)
+
+    def list_constants():
+        for t in range(4):
+            a = 256 + 128 * (t % 2)
+            ts(T.mm[:, a:a + 128], T.mt[:, :], float(t), None, A.is_equal, None, [("mt", 0, 128)], [("mm", a, a + 128)])
+            o, w = slot("s", t)
+            tt(o, T.mm[:, a:a + 128], T.sg[:, :], A.mult, [("mm", a, a + 128), ("sg", 0, 128)], w)
+        a = 512 * KN["w"]
+        fill("ks", a, a + 512, 0.0)
+        for h in range(2):
+            fill("s2%d" % h, 0, 1024, 0.0)
+        o, w = slot("w", 0)
+        tt(o, T.mm[:, 128:256], T.sg[:, :], A.mult, [("mm", 128, 256), ("sg", 0, 128)], w)
+        for h in range(2):
+            quant("q2%d" % h, "c2%d" % h, 0, 256, "s2%d" % h, 0)
+        quant("kq", "kqs", 128 * 6, 256, "ks", 512 * 6)
+
+    def layer_constants():
+        a = 512 * KN["z0"]
+        fill("ks", a, a + 2048, 0.0)
+        for b in range(4):
+            o, w = slot("z%d" % b, b)
+            copy(o, T.i64[:, :], [("i64", 0, 128)], w)
+        quant("kq", "kqs", 128 * KN["z0"], 512, "ks", a)
+
+    def om_constants():
+        a = 512 * KN["o0"]
+        fill("ks", a, a + 4096, 0.0)
+        for t in range(4):
+            o, w = slot("o%d" % t, t)
+            copy(o, T.sg[:, :], [("sg", 0, 128)], w)
+            o, w = slot("n%d" % t, 0)
+            ts(o, T.sg[:, :], T.zm[:, 4 + t:5 + t], 32.0, A.mult, A.mult, [("sg", 0, 128), ("zm", 0, 8)], w)
+        quant("kq", "kqs", 128 * KN["o0"], 512, "ks", a)
+        quant("kq", "kqs", 128 * KN["n0"], 512, "ks", a + 2048)
+        quant("qv", "sv", 0, 128, "vb", 0)
+
+    def one_round(t):
+        steps = [(gr, b) for gr in range(8) for b in range(4)]
+        at = [0]
+
+        def pump(n, who="s"):
+            for gr, b in steps[at[0]:at[0] + n]:
+                bank = "w%d" % (at[0] % 4)
+                mm(bank, "eq", "es", 512 * gr + 128 * b, "qx", "sx", 0, 256)
+                a = 2048 * b + gr
+                o, i, w = T.win[:, a:2048 * b + 2048:8], T[bank][:, 0:256], [("win", a, 2048 * b + 2048, 8)]
+                if who == "s":
+                    act(o, i, F.Copy, [(bank, 0, 512)], w)
+                else:
+                    copy(o, i, [(bank, 0, 512)], w)
+                at[0] += 1
+
+        order("p", [("su2", 0, 128)], [])
+        mm("p0", "qu2", "su2", 0, "qx", "sx", 0, 256)
+        if t == 0:
+            e_tiles(2)
+        pump(8)
+        op("v", lambda e: e.transpose(T.st[:, :], T.p0[:, 0:256]), [("p0", 0, 512)], [("st", 0, 256)])
+        op("v", lambda e: e.tensor_tensor_scan(T.rm[:, :], T.rst[:, :], T.st[:, :], 0.0, A.min, A.max),
+           [("rst", 0, 256), ("st", 0, 256)], [("rm", 0, 256)])
+        tt(T.fb[:, 0:248], T.rm[:, 0:248], T.rm[:, 8:256], A.is_ge, [("rm", 0, 256)], [("fb", 0, 248)])
+        op("v", lambda e: e.transpose(T.ft[:, 0:256], T.fb[:, :]), [("fb", 0, 256)], [("ft", 0, 256)])
+        quant("qf", "sf", 0, 128, "ft", 0)
+        kmm("p1", "tot", "qf", "sf", 0)
+        kmm("p2", "aa", "qf", "sf", 0)
+        kmm("p3", "ab", "qf", "sf", 0)
+        if t == 0:
+            for gr in (3, 4):
+                e_tiles(gr)
+            more_constants()
+        pump(8)
+        op("v", lambda e: e.tensor_tensor_scan(T.pw[:, 0:64], T.zz[:, :], T.p1[:, 0:64], 0.0, A.add, A.add),
+           [("zz", 0, 64), ("p1", 0, 512)], [("pw", 0, 64)])
+        tt(T.tt[:, 0:64], T.p2[:, 0:64], T.pw[:, 0:64], A.add, [("p2", 0, 512), ("pw", 0, 64)], [("tt", 0, 64)])
+        tt(T.tt[:, 128:192], T.p3[:, 0:64], T.pw[:, 0:64], A.add, [("p3", 0, 512), ("pw", 0, 64)], [("tt", 128, 192)])
+        ts(T.vv[:, 128:129], T.pw[:, 63:64], 256.0, None, A.min, None, [("pw", 0, 64)], [("vv", 128, 129)])
+        ts(T.vv[:, 0:64], T.tt[:, 0:64], -256.0, 0.0, A.add, A.max, [("tt", 0, 64)], [("vv", 0, 64)])
+        ts(T.vv[:, 64:128], T.tt[:, 128:192], -256.0, 0.0, A.add, A.max, [("tt", 128, 192)], [("vv", 64, 128)])
+        V = [("vv", 0, 130)]
+        ts(T.r1[:, :], T.vv[:, :], M16, -M16, A.add, A.add, V, [("r1", 0, 130)])
+        ts(T.dg[:, 2:520:4], T.vv[:, :], M256, -M256, A.add, A.add, V, [("dg", 2, 520, 4)])
+        tt(T.dg[:, 0:520:4], T.vv[:, :], T.r1[:, :], A.subtract, V + [("r1", 0, 130)], [("dg", 0, 520, 4)])
+        tt(T.dg[:, 1:520:4], T.r1[:, :], T.dg[:, 2:520:4], A.subtract, [("r1", 0, 130), ("dg", 2, 520, 4)], [("dg", 1, 520, 4)])
+        quant("qd", "sd", 0, 130, "dg", 0)
+        kmm("p0", "tri", "qd", "sd", 128)
+        kmm("p1", "x15", "qd", "sd", 64)
+        kmm("p2", "rc", "qd", "sd", 0)
+        if t == 0:
+            for gr in (5, 6, 7):
+                e_tiles(gr)
+            list_constants()
+        pump(8)
+        N = T.pw[:, 63:64]
+        ts(T.xi[:, 0:1], T.p0[:, 0:1], N, T.cf[:, 7:8], A.add, A.subtract, CF + [("p0", 0, 512), ("pw", 0, 64)], [("xi", 0, 1)])
+        XI = [("xi", 0, 1), ("pw", 0, 64)]
+        ts(T.pw[:, 64:128], T.p1[:, 0:64], T.xi[:, 0:1], N, A.add, A.max, XI + [("p1", 0, 512)], [("pw", 64, 128)])
+        ts(T.tt[:, 64:128], T.p2[:, 0:64], T.xi[:, 0:1], N, A.add, A.max, XI + [("p2", 0, 512)], [("tt", 64, 128)])
+        ts(T.tt[:, 192:256], T.p2[:, 64:128], T.xi[:, 0:1], N, A.add, A.max, XI + [("p2", 0, 512)], [("tt", 192, 256)])
+
+        def words(h):
+            for k in range(8 * h, 8 * h + 8):
+                act(T.jk[:, 128 * k:128 * k + 128], T.pw[:, 0:128], F.Sign, [("pw", 0, 128), ("kb", 0, 16)],
+                    [("ac", k, k + 1), ("jk", 128 * k, 128 * k + 128)], bias=T.kb[:, k:k + 1], scale=-1.0, accum_out=T.ac[:, k:k + 1])
+
+        def places(h, bank):
+            li, wi, wd, s2, q2, c2, lf = ["%s%d" % (n, h) for n in ("li", "wi", "wd", "s2", "q2", "c2", "lf")]
+            acc, R = T.ac[:, 8 * h:8 * h + 8], [("ac", 8 * h, 8 * h + 8)]
+            ts(T[li][:, 0:8], acc, 0.5, 64.0, A.mult, A.add, R, [(li, 0, 8)])
+            ts(T[wi][:, 0:8], acc, 0.5, 64.0, A.mult, A.add, R, [(wi, 0, 8)])
+            for i in range(2):
+                tt(T[s2][:, 128 * i:128 * i + 128], T.tt[:, 128 * i:128 * i + 128].indirect(T[li][:, 0:8]), T.mr[:, 128 * h:128 * h + 128],
+                   A.is_le, [("tt", 128 * i, 128 * i + 128), (li, 0, 8), ("mr", 0, 256)], [(s2, 128 * i, 128 * i + 128)])
+                ts(T[wd][:, 8 * i:8 * i + 8], T[wi][:, 0:8], (48, 15)[i], None, A.bitwise_and, None, [(wi, 0, 8)], [(wd, 8 * i, 8 * i + 8)])
+            for z in range(4):
+                ts(T[s2][:, 256 + 4 * z:512:16], T[wd][:, 0:16], T.zm[:, z:z + 1], None, A.mult, None, [(wd, 0, 16), ("zm", 0, 4)],
+                   [(s2, 256 + 4 * z, 512, 16)])
+            quant(q2, c2, 0, 128, s2, 0)
+            for i in range(4):
+                kmm(bank, "ssww"[i], q2, c2, 32 * i, 128, i == 0, i == 3)
+            ts(T[lf][:, 0:32], T[bank][:, 0:32], T.cf[:, 8:9], None, A.add, None, CF + [(bank, 0, 512)], [(lf, 0, 32)])
+
+        def gather(h, dst):
+            lf = "lf%d" % h
+            R = [("win", 0, 8192), (lf, 0, 32)]
+            copy(T[dst][:, 0:256], T.win[:, 0:8192].indirect(T[lf][:, 0:16]), R, [(dst, 0, 256)])
+            act(T[dst][:, 256:512], T.win[:, 0:8192].indirect(T[lf][:, 16:32]), F.Copy, R, [(dst, 256, 512)])
+
+        def om_half(h):
+            for i in range(4):
+                bank = "w%d" % i
+                for j in range(4):
+                    kmm(bank, ("o%d" if j < 2 else "n%d") % i, "q2%d" % h, "c2%d" % h, 32 * j, 128, j == 0, j == 3)
+                act(T.omf[:, 128 * h + i:128 * h + 128:4], T[bank][:, 0:32], F.Copy, [(bank, 0, 512)], [("omf", 128 * h + i, 128 * h + 128, 4)])
+
+        words(1)
+        pump(8, "v")
+        words(0)
+        places(1, "p3")
+        gather(1, "hc")
+        qy, sy = "qy%d" % t, "sy%d" % t
+        quant(qy, sy, 0, 128, "hc", 0)
+        partner = T.cores[rank ^ XOR[t]]
+        rel = relays(topo, core, partner)
+        order("g", [(qy, 0, 128)], [])
+        moves = []
+        for i, c in enumerate(rel):
+            rid, pid = topo.addr(c, core)
+            es = topo.engines(core, c)
+            k = len(es) // NREL
+            moves.append(RemoteDMATransfer(dst_ids=[DstId(rid=rid, pnc=pid)], dma_engine_mask=bits(es[k * i:k * i + k]),
+                                           remote_sem=T.sem["in%d" % t], src=T[qy][:, PC * i:PC * i + PC].bitcast(dt.uint8),
+                                           dst=T["rq%d" % t][:, 0:PC].bitcast(dt.uint8)))
+        g.remote_dma_fused(moves, local_sem=T.sem.loc)
+        c = rel[-1]
+        rid, pid = topo.addr(c, core)
+        g.remote_dma(out_ap=T["rs%d" % t][:, 0:128], in_ap=T[sy][:, 0:128], remote_sem=T.sem["in%d" % t], local_sem=T.sem.loc,
+                     pid=pid, routing_id=rid, dma_engine_mask=topo.mask(core, c))
+        places(0, "p0")
+        gather(0, "hk")
+        quant("qz", "sz", 0, 128, "hk", 0)
+        act(T.z64[:, :], T.hk[:, :], F.Identity, [("hk", 0, 512)], [("z64", 0, 512)], scale=64.0)
+        if t == 0:
+            layer_constants()
+            order("p", [("sw", 0, 512)], [])
+        for b in range(4):
+            mm("w%d" % b, "qw", "sw", 128 * b, "qz", "sz", 0, 128)
+        for b in range(4):
+            r = [("r64", 128 * b, 128 * b + 128)]
+            tt(T.r64[:, 128 * b:128 * b + 128], T["w%d" % b][:, 0:128], T.z64[:, b:512:4], A.add, [("w%d" % b, 0, 512), ("z64", 0, 512)], r)
+            act(T.xt[:, b:512:4], T.r64[:, 128 * b:128 * b + 128], F.Identity, r, [("xt", b, 512, 4)], scale=0.015625)
+        quant("qx", "sx", 0, 128, "xt", 0)
+        if t == 1:
+            om_constants()
+        if t == 2:
+            om_half(1)
+            om_half(0)
+        lq, ls = "lq%d" % t, "ls%d" % t
+        far = [len(topo.engines(c, core)) for c in relays(topo, partner, core)]
+        arrive("arr%d" % t, sum(far) + far[-1], [(lq, 0, 128)])
+        for b in range(4):
+            bank = "p%d" % b
+            mm(bank, "qw", "sw", 128 * b, lq, ls, 0, 128, True, False)
+            kmm(bank, "z%d" % b, lq, ls, 0, 128, False, True)
+            o, i, w = T.xt[:, 512 + b:1024:4], T[bank][:, 0:128], [("xt", 512 + b, 1024, 4)]
+            if b % 2 == 0:
+                act(o, i, F.Identity, [(bank, 0, 512)], w, scale=0.015625)
+            else:
+                ts(o, i, 0.015625, None, A.mult, None, [(bank, 0, 512)], w)
+        quant("qx", "sx", 128, 128, "xt", 512)
+
+    for t in range(3):
+        one_round(t)
+
+    mm("w0", "qv", "sv", 0, "qx", "sx", 0, 256)
+    copy(T.yt[:, 0:256], T.w0[:, 0:256], [("w0", 0, 512)], [("yt", 0, 256)])
+    dma("y", lambda e: e.dma_start(T.om[:, :], T.omf[0:128:16, :]), [("omf", 0, 256)], [], "dst")
+    dma("y", lambda e: e.dma_start(T.oc[:, :], T.qx[:, 0:256].bitcast(dt.uint8)), [("qx", 0, 256)], [], "dst")
+    for k in range(4):
+        dma("s", lambda e: e.dma_start(T.osc[4 * k:4 * k + 4, :], T.sx[32 * k:32 * k + 4, 0:256]), [("qx", 0, 256)], [], "dst")
+    dma("y", lambda e: e.dma_start(T.y[:, :], T.yt[:, :]), [("yt", 0, 256)], [], "dst")
+    n = 0
+    for t in range(3):
+        rel = relays(topo, core, T.cores[rank ^ XOR[t]])
+        n += sum(len(topo.engines(core, c)) // NREL for c in rel) + len(topo.engines(core, rel[-1]))
+    finish([("loc", n)])

@@ -2,63 +2,61 @@ from concourse.bass import DstId, RemoteDMATransfer
 from concourse.mybir import dt, AluOpType as A, ActivationFunctionType as F
 
 XOR = [1, 2, 4]
-NREL = 4
+NREL = 2
 PC = 128 // NREL
 F8 = "float8_e4m3fn_x4"
 BIG = 2.0 ** 90
-M16, M256 = 1.5 * 2.0 ** 27, 1.5 * 2.0 ** 31
+M32 = 1.5 * 2.0 ** 28
+LW = 160
+BY_DMA = {"both": 7, "kept": 7, "came": 5}
+NV = 5
+SEG = 66
 
-KN = {"tot": 0, "aa": 1, "ab": 2, "rc": 3, "x15": 4, "tri": 5, "s": 6, "w": 7, "z0": 8, "z1": 9, "z2": 10, "z3": 11,
-      "o0": 12, "o1": 13, "o2": 14, "o3": 15, "n0": 16, "n1": 17, "n2": 18, "n3": 19}
+KN = {n: i for i, n in enumerate(["tot", "aa", "ab", "oa", "ob", "tri", "all", "ra", "rb", "kd", "kj", "kw", "kn"])}
+REFUSED, CHOSEN, FIRST, LAST, RAW = 0, 64, 128, 256, 384
+DG, FT, FB = 768, 1032, 1288
+
+
+def sb(n, kind="bfloat16"):
+    return ("sbuf", [128, n], kind)
+
 
 SCRATCH = {
-    "ub": ("sbuf", [128, 512], "bfloat16"), "vb": ("sbuf", [128, 512], "bfloat16"), "x0": ("sbuf", [128, 1024], "bfloat16"),
-    "qu": ("sbuf", [128, 128], F8), "su": ("sbuf", [128, 128], "uint8"),
-    "qu2": ("sbuf", [128, 128], F8), "su2": ("sbuf", [128, 128], "uint8"),
-    "qv": ("sbuf", [128, 128], F8), "sv": ("sbuf", [128, 128], "uint8"),
-    "qw": ("sbuf", [128, 512], F8), "sw": ("sbuf", [128, 512], "uint8"),
-    "qx": ("sbuf", [128, 256], F8), "sx": ("sbuf", [128, 256], "uint8"),
-    "eq": ("sbuf", [128, 4096], F8), "es": ("sbuf", [128, 4096], "uint8"),
-    "kq": ("sbuf", [128, 2560], F8), "kqs": ("sbuf", [128, 2560], "uint8"),
-    "kt0": ("sbuf", [128, 2048], "bfloat16"), "kt1": ("sbuf", [128, 2048], "bfloat16"),
-    "ks": ("sbuf", [128, 10240], "bfloat16"),
-    "mc": ("sbuf", [128, 128], "bfloat16"), "mx": ("sbuf", [128, 128], "bfloat16"), "mt": ("sbuf", [128, 128], "bfloat16"),
-    "mr": ("sbuf", [128, 256], "bfloat16"), "i16": ("sbuf", [128, 16], "bfloat16"),
-    "pc": ("sbuf", [128, 16], "int32"), "cf": ("sbuf", [128, 16], "float32"), "cm": ("sbuf", [128, 16], "float32"),
-    "zm": ("sbuf", [128, 16], "float32"), "kb": ("sbuf", [128, 16], "float32"), "uo": ("sbuf", [128, 8], "uint16"),
-    "gm": ("sbuf", [128, 128], "bfloat16"), "sg": ("sbuf", [128, 128], "bfloat16"), "hm": ("sbuf", [128, 128], "bfloat16"),
-    "h1": ("sbuf", [128, 128], "bfloat16"), "i64": ("sbuf", [128, 128], "bfloat16"), "dx": ("sbuf", [128, 128], "bfloat16"),
-    "nk": ("sbuf", [128, 128], "bfloat16"), "mm": ("sbuf", [128, 512], "bfloat16"),
-    "rst": ("sbuf", [128, 256], "float32"), "zz": ("sbuf", [128, 64], "float32"),
-    "st": ("sbuf", [128, 256], "float32"), "rm": ("sbuf", [128, 256], "float32"), "fb": ("sbuf", [128, 256], "bfloat16"),
-    "ft": ("sbuf", [128, 512], "bfloat16"), "qf": ("sbuf", [128, 128], F8), "sf": ("sbuf", [128, 128], "uint8"),
-    "pw": ("sbuf", [128, 128], "float32"), "tt": ("sbuf", [128, 256], "float32"),
-    "vv": ("sbuf", [128, 130], "float32"), "r1": ("sbuf", [128, 130], "float32"), "dg": ("sbuf", [128, 1024], "bfloat16"),
-    "qd": ("sbuf", [128, 256], F8), "sd": ("sbuf", [128, 256], "uint8"), "xi": ("sbuf", [128, 4], "float32"),
-    "ac": ("sbuf", [128, 16], "float32"), "jk": ("sbuf", [128, 2048], "bfloat16"),
-    "win": ("sbuf", [128, 8192], "bfloat16"), "hk": ("sbuf", [128, 512], "bfloat16"), "hc": ("sbuf", [128, 512], "bfloat16"),
-    "z64": ("sbuf", [128, 512], "bfloat16"), "r64": ("sbuf", [128, 512], "float32"), "xt": ("sbuf", [128, 1024], "bfloat16"),
-    "qz": ("sbuf", [128, 128], F8), "sz": ("sbuf", [128, 128], "uint8"),
-    "yt": ("sbuf", [128, 256], "float32"), "omf": ("sbuf", [128, 256], "float32"),
+    "ub": sb(512), "vb": sb(512), "x0": sb(1024),
+    "qu": sb(128, F8), "su": sb(128, "uint8"), "qv": sb(128, F8), "sv": sb(128, "uint8"),
+    "qw": sb(512, F8), "sw": sb(512, "uint8"), "qx": sb(256, F8), "sx": sb(256, "uint8"),
+    "eq": sb(4 * LW, F8), "es": sb(4 * LW, "uint8"), "zq": sb(512, F8), "zs": sb(512, "uint8"),
+    "kq": sb(128 * len(KN), F8), "kqs": sb(128 * len(KN), "uint8"), "ks": sb(512 * len(KN)),
+    "jj": sb(512), "z1": sb(1024), "zz64": sb(528), "one": sb(64),
+    "mx": sb(512), "ct": sb(512), "ct2": sb(512), "mt": sb(128), "mr": sb(256), "i16": sb(16), "zmask": sb(128),
+    "pc": sb(16, "int32"), "cf": sb(24, "float32"), "nk": sb(32, "float32"), "kb": sb(24, "float32"),
+    "qu1": sb(128, F8), "su1": sb(128, "uint8"), "uo": sb(8, "uint16"), "go": sb(8, "uint16"),
+    "rst": sb(256, "float32"), "inj": sb(SEG * NV, "float32"),
+    "st": sb(256, "float32"), "rm": sb(256, "float32"), "fl": sb(1544), "qf": sb(128, F8), "sf": sb(128, "uint8"),
+    "tt": sb(448, "float32"), "free": sb(8, "float32"), "kv": sb(16, "float32"), "m64": sb(192),
+    "qd": sb(130, F8), "sd": sb(130, "uint8"), "r16": sb(16),
+    "jk": sb(2688), "wb": sb(SEG * NV), "q2": sb(320, F8), "c2": sb(320, "uint8"), "q3": sb(256, F8), "c3": sb(256, "uint8"), "lf": sb(64, "uint16"),
+    "win": sb(8192), "hk": sb(512), "hc": sb(512), "z64": sb(512), "x64": sb(512), "xt": sb(1024),
+    "qz": sb(128, F8), "sz": sb(128, "uint8"), "yt": sb(256, "float32"),
+    "omf": sb(144, "float32"),
 }
 for _h in range(2):
-    SCRATCH.update({"li%d" % _h: ("sbuf", [128, 8], "uint16"), "wi%d" % _h: ("sbuf", [128, 8], "int32"),
-                    "wd%d" % _h: ("sbuf", [128, 16], "int32"), "s2%d" % _h: ("sbuf", [128, 1024], "bfloat16"),
-                    "q2%d" % _h: ("sbuf", [128, 256], F8), "c2%d" % _h: ("sbuf", [128, 256], "uint8"),
-                    "lf%d" % _h: ("sbuf", [128, 32], "uint16")})
+    SCRATCH.update({"ac%d" % _h: sb(8 * SEG, "float32"), "li%d" % _h: sb(8, "uint16"), "wd%d" % _h: sb(24, "float32")})
 for _t in range(3):
-    SCRATCH.update({"qy%d" % _t: ("sbuf", [128, 128], F8), "sy%d" % _t: ("sbuf", [128, 128], "uint8"),
-                    "lq%d" % _t: ("sbuf", [128, 128], F8), "ls%d" % _t: ("sbuf", [128, 128], "uint8"),
-                    "rq%d" % _t: ("sbuf", [128, PC], F8), "rs%d" % _t: ("sbuf", [128, 128], "uint8")})
+    SCRATCH.update({"qy%d" % _t: sb(128, F8), "sy%d" % _t: sb(128, "uint8"), "lq%d" % _t: sb(128, F8), "ls%d" % _t: sb(128, "uint8"),
+                    "rq%d" % _t: sb(PC, F8), "rs%d" % _t: sb(128, "uint8")})
 PSUM = ["w0", "w1", "w2", "w3", "p0", "p1", "p2", "p3"]
 for _b in PSUM:
     SCRATCH[_b] = ("psum", [128, 512], "float32")
-SEMAPHORES = ["qg", "qv", "qs", "qp", "dx", "dxb", "du", "dv", "dwc", "dws", "dst", "loc"] + \
+SEMAPHORES = ["qg", "qv", "qs", "qp", "dx", "du", "dv", "dwc", "dws", "dst", "loc", "turn0", "turn1"] + \
     ["%s%d" % (n, t) for n in ("arr", "in") for t in range(3)]
 
 
 def relays(topo, core, partner):
-    return [c for c in topo.cores_of(core) if c != core and topo.may_write(c, partner)][:NREL]
+    able = [c for c in topo.cores_of(core) if c != core and topo.may_write(c, partner)]
+    near = [c for c in able if topo.die(c) == topo.die(core)]
+    far = [c for c in able if topo.die(c) != topo.die(core)]
+    return [near[0], far[0], near[1]]
 
 
 def bits(es):
@@ -78,16 +76,14 @@ def hand_on(g, core, T, topo):
         i = rel.index(core)
         rid, pid = topo.addr(partner, core)
         m, n = topo.mask(core, partner), len(topo.engines(core, partner))
-        last = i == NREL - 1
         es = len(topo.engines(home, core))
-        g.wait_ge(T.sem["in%d" % t], es // NREL + (es if last else 0))
-        g.remote_dma(out_ap=T["lq%d" % t][:, PC * i:PC * i + PC].bitcast(dt.uint8), in_ap=T["rq%d" % t][:, 0:PC].bitcast(dt.uint8),
-                     remote_sem=T.sem["arr%d" % t], local_sem=T.sem.loc, pid=pid, routing_id=rid, dma_engine_mask=m)
+        if i < NREL:
+            out, in_, landed = T["lq%d" % t][:, PC * i:PC * i + PC].bitcast(dt.uint8), T["rq%d" % t][:, 0:PC].bitcast(dt.uint8), es // NREL
+        else:
+            out, in_, landed = T["ls%d" % t][:, 0:128], T["rs%d" % t][:, 0:128], es
+        g.wait_ge(T.sem["in%d" % t], landed)
+        g.remote_dma(out_ap=out, in_ap=in_, remote_sem=T.sem["arr%d" % t], local_sem=T.sem.loc, pid=pid, routing_id=rid, dma_engine_mask=m)
         sent += n
-        if last:
-            g.remote_dma(out_ap=T["ls%d" % t][:, 0:128], in_ap=T["rs%d" % t][:, 0:128],
-                         remote_sem=T.sem["arr%d" % t], local_sem=T.sem.loc, pid=pid, routing_id=rid, dma_engine_mask=m)
-            sent += n
     if sent:
         g.wait_ge(T.sem.loc, sent)
 
@@ -111,6 +107,10 @@ def machine(g, T):
         return r if len(r) == 4 else (r[0], r[1], r[2], 1)
 
     def meet(lo, hi, st, r):
+        if st == 1 and r[5] > 1:
+            return any(lo <= c < hi for c in range(r[0], r[1], r[5]))
+        if r[5] == 1 and st > 1:
+            return any(r[0] <= c < r[1] for c in range(lo, hi, st))
         return r[0] < hi and lo < r[1] and not (st == r[5] and (lo - r[0]) % st)
 
     def inside(r, lo, hi, st):
@@ -144,10 +144,11 @@ def machine(g, T):
         call(eng[q]).then_inc(T.sem[sem], 1)
         note(q, (sem, count[sem], dict(clock[q])), reads, writes)
 
-    def dma(q, call, reads, writes, sem):
+    def dma(q, pairs, reads, writes, sem):
         order(q, reads, writes)
-        count[sem] = count.get(sem, 0) + 16
-        call(eng[q]).then_inc(T.sem[sem], 16)
+        for out, in_ in pairs:
+            count[sem] = count.get(sem, 0) + 16
+            eng[q].dma_start(out, in_).then_inc(T.sem[sem], 16)
         note(q + sem, (sem, count[sem], dict(clock[q])), reads, writes)
 
     def arrive(sem, n, writes):
@@ -169,6 +170,12 @@ def rank_program(g, core, T, topo):
         return
     op, dma, arrive, finish, order = machine(g, T)
 
+    def ap(r):
+        return T[r[0]][:, r[1]:r[2]:r[3]] if len(r) == 4 else T[r[0]][:, r[1]:r[2]]
+
+    def bank(r):
+        return (r[0], 0, 512) if r[0] in PSUM else r
+
     def mm(out, k, ks, a, q, s, b, n, start=True, stop=True):
         op("p", lambda e: e.matmul_mx(T[out][:, 0:n], T[k][:, a:a + 128], T[ks][:, a:a + 128], T[q][:, b:b + n], T[s][:, b:b + n], start, stop),
            [(k, a, a + 128), (q, b, b + n)], [(out, 0, 512)])
@@ -180,272 +187,295 @@ def rank_program(g, core, T, topo):
         op("v", lambda e: e.quantize_mx(T[q][:, a:a + n], T[s][:, a:a + n], T[src][:, b:b + 4 * n]),
            [(src, b, b + 4 * n)], [(q, a, a + n)])
 
-    def ts(out, in0, s1, s2, o0, o1, reads, writes):
+    def kquant(name):
+        quant("kq", "kqs", 128 * KN[name], 128, "ks", 512 * KN[name])
+
+    def source(r, by):
+        return (ap(r), [bank(r)]) if by is None else (ap(r).indirect(ap(by)), [r, by])
+
+    def ts(out, in0, s1, o0, s2=None, o1=None):
+        reads = [bank(r) for r in (in0, s1, s2) if isinstance(r, tuple)]
+        a, b = [ap(r) if isinstance(r, tuple) else r for r in (s1, s2)]
         if o1 is None:
-            op("v", lambda e: e.tensor_scalar(out, in0, s1, None, o0), reads, writes)
+            op("v", lambda e: e.tensor_scalar(ap(out), ap(in0), a, None, o0), reads, [out])
         else:
-            op("v", lambda e: e.tensor_scalar(out, in0, s1, s2, o0, o1), reads, writes)
+            op("v", lambda e: e.tensor_scalar(ap(out), ap(in0), a, b, o0, o1), reads, [out])
 
-    def tt(out, a, b, o, reads, writes):
-        op("v", lambda e: e.tensor_tensor(out, a, b, o), reads, writes)
+    def tt(out, a, b, o, by=None):
+        src, reads = source(a, by)
+        op("v", lambda e: e.tensor_tensor(ap(out), src, ap(b), o), reads + [bank(b)], [out])
 
-    def copy(out, in_, reads, writes):
-        op("v", lambda e: e.tensor_copy(out, in_), reads, writes)
+    def copy(out, in_, by=None):
+        src, reads = source(in_, by)
+        op("v", lambda e: e.tensor_copy(ap(out), src), reads, [out])
 
-    def fill(buf, a, b, val, step=1):
-        op("v", lambda e: e.memset(T[buf][:, a:b:step], val), [], [(buf, a, b, step)])
+    def scan(out, d0, d1, o0, o1, first=0.0):
+        op("v", lambda e: e.tensor_tensor_scan(ap(out), ap(d0), ap(d1), first, o0, o1), [bank(d0), bank(d1)], [out])
 
-    def act(out, in_, func, reads, writes, **kw):
-        op("s", lambda e: e.activation(out, in_, func, **kw), reads, writes)
+    def turn(out, in_):
+        op("v", lambda e: e.transpose(ap(out), ap(in_)), [bank(in_)], [out])
 
-    def iota(buf, a, b, pattern, base, cmul):
-        kw = {} if buf == "pc" else {"allow_small_or_imprecise_dtypes": True}
-        op("g", lambda e: e.iota(T[buf][:, a:b], pattern, base, cmul, **kw), [], [(buf, a, b)])
+    def fill(r, val):
+        op("v", lambda e: e.memset(ap(r), val), [], [r])
 
-    dma("y", lambda e: e.dma_start(T.ub[:, :], T.u[:, :]), [], [("ub", 0, 512)], "du")
-    dma("s", lambda e: e.dma_start(T.x0[:, 0:512], T.x[:, 0:512]), [], [("x0", 0, 512)], "dx")
-    dma("y", lambda e: e.dma_start(T.x0[:, 512:1024], T.x[:, 512:1024]), [], [("x0", 512, 1024)], "dxb")
-    dma("y", lambda e: e.dma_start(T.qw[:, :].bitcast(dt.uint8), T.wc[:, :]), [], [("qw", 0, 512)], "dwc")
-    dma("y", lambda e: e.dma_start(T.sw[:, :], T.ws[:, :]), [], [("sw", 0, 512)], "dws")
-    dma("y", lambda e: e.dma_start(T.vb[:, :], T.v[:, :]), [], [("vb", 0, 512)], "dv")
+    def act(out, in_, func=F.Copy, by=None, **kw):
+        src, reads = source(in_, by)
+        reads += [kw[k] for k in ("scale", "bias") if isinstance(kw.get(k), tuple)]
+        writes = [out] + ([kw["accum_out"]] if "accum_out" in kw else [])
+        args = {k: ap(v) if isinstance(v, tuple) else v for k, v in kw.items()}
+        op("s", lambda e: e.activation(ap(out), src, func, **args), reads, writes)
 
-    iota("pc", 0, 1, [[0, 1]], 0, 1)
-    iota("mx", 0, 128, [[0, 8], [1, 16]], 0, 0)
-    iota("mr", 0, 256, [[1, 256]], 0, 0)
-    iota("mc", 0, 128, [[1, 8], [0, 16]], 0, 0)
-    iota("i16", 0, 16, [[16, 16]], 0, 0)
-    iota("mt", 0, 128, [[0, 8], [1, 4], [0, 4]], 0, 0)
-    iota("kt1", 0, 2048, [[0, 2048]], 0, 0)
-    fill("kt0", 0, 2048, 0.0)
-    P = [("pc", 0, 1)]
-    ts(T.pc[:, 1:2], T.pc[:, 0:1], 15, None, A.bitwise_and, None, P, [("pc", 1, 2)])
-    ts(T.pc[:, 2:3], T.pc[:, 0:1], 4, None, A.arith_shift_right, None, P, [("pc", 2, 3)])
-    ts(T.pc[:, 3:4], T.pc[:, 0:1], 3, None, A.bitwise_and, None, P, [("pc", 3, 4)])
-    ts(T.pc[:, 4:5], T.pc[:, 0:1], 2, 3, A.arith_shift_right, A.bitwise_and, P, [("pc", 4, 5)])
-    ts(T.pc[:, 5:6], T.pc[:, 0:1], 7, None, A.bitwise_and, None, P, [("pc", 5, 6)])
-    copy(T.cf[:, 0:6], T.pc[:, 0:6], [("pc", 0, 6)], [("cf", 0, 6)])
-    ts(T.cf[:, 6:7], T.cf[:, 1:2], 1.0, None, A.add, None, [("cf", 1, 2)], [("cf", 6, 7)])
-    ts(T.cf[:, 7:8], T.cf[:, 2:3], 256.0, None, A.mult, None, [("cf", 2, 3)], [("cf", 7, 8)])
-    ts(T.cf[:, 8:9], T.cf[:, 3:4], 2048.0, None, A.mult, None, [("cf", 3, 4)], [("cf", 8, 9)])
-    CF = [("cf", 0, 9)]
-    ts(T.gm[:, :], T.mx[:, :], T.cf[:, 1:2], None, A.is_equal, None, CF + [("mx", 0, 128)], [("gm", 0, 128)])
-    ts(T.cm[:, 0:8], T.mr[:, 0:8], T.cf[:, 2:3], None, A.is_equal, None, CF + [("mr", 0, 256)], [("cm", 0, 8)])
+    def sfill(r, val):
+        act(r, ("z1", 0, len(range(*r[1:]))), F.Identity, scale=0.0, bias=val)
 
-    def e_tiles(gr):
-        kt = "kt%d" % (gr % 2)
-        for b in range(4):
-            act(T[kt][:, 512 * b + b:512 * b + 512:4], T.gm[:, :], F.Identity, [("gm", 0, 128), ("cm", 0, 8)],
-                [(kt, 512 * b + b, 512 * b + 512, 4)], scale=T.cm[:, gr:gr + 1])
-        quant("eq", "es", 512 * gr, 512, kt, 0)
+    def iota(r, pattern, base, cmul):
+        kw = {} if r[0] == "pc" else {"allow_small_or_imprecise_dtypes": True}
+        op("g", lambda e: e.iota(ap(r), pattern, base, cmul, **kw), [], [r])
 
-    def slot(name, t):
-        a = 512 * KN[name]
-        return T.ks[:, a + t:a + 512:4], [("ks", a + t, a + 512, 4)]
+    def keep(out, in_, pattern, base, cmul):
+        op("g", lambda e: e.affine_select(ap(out), ap(in_), pattern, A.is_ge, 0.0, base, cmul), [in_], [out])
 
-    e_tiles(0)
-    ts(T.uo[:, 0:8], T.i16[:, 0:8], T.cf[:, 5:6], None, A.add, None, CF + [("i16", 0, 16)], [("uo", 0, 8)])
-    ts(T.kb[:, :], T.i16[:, :], T.cf[:, 1:2], 0.5, A.add, A.add, CF + [("i16", 0, 16)], [("kb", 0, 16)])
-    ts(T.zm[:, 0:4], T.mr[:, 0:4], T.cf[:, 4:5], None, A.is_equal, None, CF + [("mr", 0, 256)], [("zm", 0, 4)])
-    ts(T.zm[:, 4:8], T.mr[:, 0:4], T.cf[:, 3:4], None, A.is_equal, None, CF + [("mr", 0, 256)], [("zm", 4, 8)])
-    ts(T.hm[:, :], T.mc[:, :], T.cf[:, 1:2], None, A.is_equal, None, CF + [("mc", 0, 128)], [("hm", 0, 128)])
-    ts(T.h1[:, :], T.mc[:, :], T.cf[:, 6:7], None, A.is_equal, None, CF + [("mc", 0, 128)], [("h1", 0, 128)])
-    ts(T.dx[:, :], T.mx[:, :], T.cf[:, 2:3], None, A.subtract, None, CF + [("mx", 0, 128)], [("dx", 0, 128)])
-    tt(T.nk[:, :], T.h1[:, :], T.hm[:, :], A.subtract, [("h1", 0, 128), ("hm", 0, 128)], [("nk", 0, 128)])
-    e_tiles(1)
-    NK = [("nk", 0, 128)]
-    for t in range(4):
-        o, w = slot("tot", t)
-        act(o, T.nk[:, :], F.Identity, NK, w, scale=-1.0)
-    for t in range(2):
-        ts(T.mm[:, 128 * t:128 * t + 128], T.dx[:, :], 8.0 * t, None, A.is_lt, None, [("dx", 0, 128)], [("mm", 128 * t, 128 * t + 128)])
-        fill("ks", 512 * KN["ab"] + t, 512 * KN["ab"] + 512, 0.0, 4)
-    for t in range(2):
-        o, w = slot("aa", t)
-        tt(o, T.mm[:, 128 * t:128 * t + 128], T.nk[:, :], A.mult, NK + [("mm", 128 * t, 128 * t + 128)], w)
-        o, w = slot("ab", t + 2)
-        tt(o, T.mm[:, 128 * t:128 * t + 128], T.nk[:, :], A.mult, NK + [("mm", 128 * t, 128 * t + 128)], w)
-        o, w = slot("aa", t + 2)
-        act(o, T.nk[:, :], F.Identity, NK, w)
-    quant("kq", "kqs", 0, 128 * 3, "ks", 0)
+    def slot(name):
+        return ("ks", 512 * KN[name], 512 * KN[name] + 512)
 
-    quant("qu", "su", 0, 128, "ub", 0)
-    copy(T.qu2[:, 0:128].bitcast(dt.uint32), T.qu[:, 0:128].bitcast(dt.uint32).indirect(T.uo[:, 0:8]), [("qu", 0, 128), ("uo", 0, 8)], [("qu2", 0, 128)])
-    act(T.su2[:, 0:128], T.su[:, 0:128].indirect(T.uo[:, 0:8]), F.Copy, [("qu", 0, 128), ("uo", 0, 8)], [("su2", 0, 128)])
-    fill("rst", 0, 256, BIG)
-    fill("zz", 0, 64, 0.0)
-    fill("fb", 248, 256, 0.0)
-    fill("ft", 256, 512, 0.0)
-    fill("rst", 0, 256, -BIG, 16)
-    quant("qx", "sx", 0, 128, "x0", 0)
-    quant("qx", "sx", 128, 128, "x0", 512)
+    def pc(i):
+        return ("pc", i, i + 1)
 
-    def more_constants():
-        ts(T.sg[:, :], T.mc[:, :], T.cf[:, 2:3], None, A.is_equal, None, CF + [("mc", 0, 128)], [("sg", 0, 128)])
-        ts(T.i64[:, :], T.mr[:, 0:128], T.cf[:, 0:1], 64.0, A.is_equal, A.mult, CF + [("mr", 0, 256)], [("i64", 0, 128)])
-        ts(T.mm[:, 0:128], T.mc[:, :], T.cf[:, 2:3], None, A.is_gt, None, CF + [("mc", 0, 128)], [("mm", 0, 128)])
-        ts(T.cm[:, 8:9], T.cf[:, 1:2], 0.0, None, A.is_equal, None, CF, [("cm", 8, 9)])
-        ts(T.cm[:, 9:10], T.cf[:, 1:2], 15.0, None, A.is_equal, None, CF, [("cm", 9, 10)])
-        ts(T.mm[:, 128:256], T.mt[:, :], T.cf[:, 3:4], 32.0, A.is_equal, A.mult, CF + [("mt", 0, 128)], [("mm", 128, 256)])
-        for t in range(3):
-            o, w = slot("rc", t)
-            copy(o, T.gm[:, :], [("gm", 0, 128)], w)
-            o, w = slot("x15", t)
-            ts(o, T.mr[:, 0:128], 0.0, T.cm[:, 9:10], A.is_ge, A.mult, [("mr", 0, 256), ("cm", 9, 10)], w)
-            o, w = slot("tri", t)
-            ts(o, T.mm[:, 0:128], T.cm[:, 8:9], None, A.mult, None, [("mm", 0, 128), ("cm", 8, 9)], w)
-        for n in ("rc", "x15", "tri"):
-            fill("ks", 512 * KN[n] + 3, 512 * KN[n] + 512, 0.0, 4)
-        fill("dg", 0, 1024, 0.0)
-        quant("kq", "kqs", 128 * 3, 128 * 3, "ks", 512 * 3)
-        quant("qd", "sd", 0, 256, "dg", 0)
-        fill("vv", 128, 130, 0.0)
+    def cf(i):
+        return ("cf", i, i + 1)
 
-    def list_constants():
-        for t in range(4):
-            a = 256 + 128 * (t % 2)
-            ts(T.mm[:, a:a + 128], T.mt[:, :], float(t), None, A.is_equal, None, [("mt", 0, 128)], [("mm", a, a + 128)])
-            o, w = slot("s", t)
-            tt(o, T.mm[:, a:a + 128], T.sg[:, :], A.mult, [("mm", a, a + 128), ("sg", 0, 128)], w)
-        a = 512 * KN["w"]
-        fill("ks", a, a + 512, 0.0)
+    def run(a, n=64):
+        return ("tt", a, a + n)
+
+    later = []
+
+    def now(calls):
+        for call in calls:
+            call[0](*call[1:])
+
+    def gap(n=1):
+        now(later[:n])
+        del later[:n]
+
+    def until(mark):
+        if (mark,) in later:
+            gap(later.index((mark,)) + 1)
+
+    def counts_ready():
+        pass
+
+    def flags_ready():
+        pass
+
+    def marks_ready():
+        pass
+
+    def first_ready():
+        pass
+
+    def last_ready():
+        pass
+
+    def weights():
+        act(cf(13), cf(11), F.Identity, bias=1024.0)
+        act(cf(12), cf(9), F.Identity, scale=4.0)
+        act(slot("kd"), slot("kn"), F.Identity, scale=cf(13))
+        act(slot("kj"), slot("kn"), F.Identity, scale=cf(12))
+
+    def digits_ready():
+        pass
+
+    def lists_ready():
+        pass
+
+    def weights_ready():
+        pass
+
+    dma("s", [(T.ub[:, :], T.u[:, :])], [], [("ub", 0, 512)], "du")
+    dma("y", [(T.x0[:, :], T.x[:, :])], [], [("x0", 0, 1024)], "dx")
+
+    iota(pc(0), [[0, 1]], 0, 1)
+    iota(("r16", 0, 16), [[1, 16]], 0, 0)
+    iota(("jj", 0, 512), [[1, 512]], 0, -4)
+    iota(("i16", 0, 16), [[16, 16]], 0, 0)
+    iota(("m64", 0, 64), [[1, 16], [-8, 4]], 0, 0)
+    fill(("one", 0, 64), 1.0)
+    ts(pc(1), pc(0), 15, A.bitwise_and)
+    ts(pc(2), pc(0), 4, A.arith_shift_right)
+    ts(pc(3), pc(0), 3, A.bitwise_and)
+    ts(pc(4), pc(0), 2, A.arith_shift_right, 3, A.bitwise_and)
+    ts(pc(5), pc(0), 7, A.bitwise_and)
+    fill(("fl", FB + 248, FB + 256), 0.0)
+    copy(("cf", 0, 6), ("pc", 0, 6))
+    fill(("rst", 0, 128), BIG)
+    ts(("nk", 0, 16), ("r16", 0, 16), cf(1), A.is_equal)
+    ts(("nk", 16, 24), ("r16", 0, 8), -1.0, A.add, cf(1), A.is_equal)
+    fill(("rst", 0, 128, 16), -BIG)
+    tt(("nk", 24, 32), ("nk", 0, 8), ("nk", 16, 24), A.subtract)
+    ts(pc(6), pc(0), cf(2), A.subtract)
+    ts(pc(7), pc(2), -1.0, A.mult, 8.0, A.add)
+    ts(("uo", 0, 8), ("i16", 0, 8), cf(5), A.add)
+    ts(("z1", 0, 512), ("jj", 0, 512), 3.0, A.is_equal)
+    ts(("z1", 512, 4 * LW + 4), ("jj", 0, 4 * LW + 4 - 512), 3.0, A.is_equal)
+    quant("qu1", "su1", 0, 128, "ub", 0)
+    unpacking = [(quant, "eq", "es", LW * b, LW, "z1", 3 - b) for b in range(4)]
+    now(unpacking[:1])
+    act(cf(8), cf(2), F.Identity, scale=4.0)
+    act(cf(16), cf(1), F.Identity, scale=16.0)
+    act(cf(10), cf(3), F.Identity, bias=cf(8))
+
+    def by_group(name, pattern):
+        a = slot(name)[1]
+        for c in range(8):
+            act(("ks", a + 64 * c, a + 64 * c + 64), pattern, F.Identity, scale=("nk", 24 + c, 25 + c))
+
+    by_group("tot", ("one", 0, 64))
+    op("v", lambda e: e.tensor_copy(T.qu[:, 0:128].bitcast(dt.uint32), T.qu1[:, 0:128].bitcast(dt.uint32).indirect(T.uo[:, 0:8])),
+       [("qu1", 0, 128), ("uo", 0, 8)], [("qu", 0, 128)])
+    op("s", lambda e: e.activation(T.su[:, 0:128], T.su1[:, 0:128].indirect(T.uo[:, 0:8]), F.Copy), [("qu1", 0, 128), ("uo", 0, 8)], [("su", 0, 128)])
+    ts(("m64", 64, 128), ("m64", 0, 64), cf(2), A.is_equal)
+    quant("qx", "sx", 0, 256, "x0", 0)
+    ts(("m64", 128, 192), ("m64", 0, 64), 16.0, A.add, cf(2), A.is_equal)
+    ts(("pc", 8, 10), ("pc", 6, 8), 7, A.bitwise_and)
+    act(cf(9), ("nk", 7, 8), F.Identity, bias=("nk", 15, 16))
+    act(("rst", 128, 256), ("rst", 0, 128))
+    by_group("oa", ("m64", 64, 128))
+    iota(("ct2", 0, 512), [[1, 32], [0, 16]], 0, 0)
+    for name, first in (("aa", 0), ("ab", 16)):
+        keep(slot(name), slot("tot"), [[0, 8], [-16, 16], [128, 4]], -16 * (first + 1), 1)
+    iota(("mx", 0, 512), [[0, 8], [1, 16], [-100, 4]], 0, 0)
+    iota(("ct", 0, 512), [[1, 32], [0, 4], [-1, 4]], 0, 0)
+    iota(("mr", 0, 256), [[1, 256]], -256, 0)
+    iota(("mt", 0, 128), [[0, 8], [1, 4], [0, 4]], 0, 0)
+    order("p", [("su", 0, 128)], [])
+    dma("y", [(T.qw[:, :].bitcast(dt.uint8), T.wc[:, :])], [], [("qw", 0, 512)], "dwc")
+    dma("y", [(T.sw[:, :], T.ws[:, :])], [], [("sw", 0, 512)], "dws")
+
+    later += unpacking[1:] + [
+        (kquant, "tot"),
+        (ts, slot("tri"), ("ct2", 0, 512), cf(8), A.is_ge),
+        (kquant, "aa"), (kquant, "oa"), (counts_ready,), (kquant, "ab"), (flags_ready,),
+        (kquant, "tri"),
+        (ts, slot("kw"), ("ct2", 0, 512), cf(10), A.is_equal, 8.0, A.mult),
+        (kquant, "ob"), (marks_ready,),
+        (ts, slot("ra"), ("mx", 0, 512), cf(1), A.is_lt),
+        (kquant, "all"), (digits_ready,),
+        (ts, slot("kn"), ("ct", 0, 512), cf(8), A.is_equal),
+        (ts, cf(11), pc(8), 7.0, A.is_equal, -8192.0, A.mult),
+        (kquant, "ra"), (first_ready,),
+        (ts, slot("rb"), ("mx", 0, 512), 100.0, A.add, cf(1), A.is_lt),
+        (ts, cf(15), cf(3), 2.0, A.min, 8.0, A.mult),
+        (kquant, "rb"), (last_ready,),
+        (ts, ("go", 0, 8), ("r16", 0, 8), cf(15), A.add),
+        (ts, ("zmask", 0, 128), ("mt", 0, 128), cf(4), A.is_equal),
+        (kquant, "kd"), (kquant, "kj"), (weights_ready,),
+        (kquant, "kw"), (lists_ready,),
+        (ts, cf(14), pc(9), 1024.0, A.mult, cf(7), A.add)]
+
+    def fills():
+        by_group("ob", ("m64", 128, 192))
+        sfill(("fl", DG, DG + 264), 0.0)
+        sfill(slot("all"), 1.0)
+        act(cf(6), cf(1), F.Identity, bias=0.5 - 256.0)
+        sfill(("inj", 0, SEG * NV), BIG)
+        act(("kb", 0, 16), ("i16", 0, 16), F.Identity, bias=cf(6))
+        act(cf(7), cf(3), F.Identity, bias=1024.0)
+        act(("kb", 16, 24), ("kb", 8, 16), F.Identity, bias=-4096.0)
+
+    def more_fills():
+        sfill(("wb", 64, SEG * NV, SEG), -64.0)
+        sfill(("wb", 65, SEG * NV, SEG), 1000.0)
+
+    def window(a, n, kind):
+        copied = BY_DMA[kind]
+
+        def step(d, b, name):
+            mm(name, "eq", "es", LW * b + 16 * d, "qx", "sx", a, n)
+            act(("win", 1024 * d + 4 * a + b, 1024 * d + 4 * (a + n), 4), (name, 0, n))
+            if d == 0 and b == 3:
+                lo, hi, pairs = 4 * a, 4 * (a + n), []
+                for k in range(8 - copied, 8):
+                    pairs.append((T.win[0:128 - 16 * k, 1024 * k + lo:1024 * k + hi], T.win[16 * k:128, lo:hi]))
+                    pairs.append((T.win[128 - 16 * k:128, 1024 * k + lo:1024 * k + hi], T.win[0:16 * k, lo:hi]))
+                dma("y", pairs, [("win", lo, hi)], [("win", 1024 * k + lo, 1024 * k + hi) for k in range(8 - copied, 8)],
+                    "turn%d" % (a // 128))
+        return [(step, d, b) for d in range(8 - copied) for b in range(4)]
+
+    def pump(steps, n, last="w0"):
+        for step, d, b in steps[:n]:
+            step(d, b, ("w3", "w2", "w1", last)[b])
+        del steps[:n]
+
+    def choices(name, a, n):
+        return [(turn, ("st", a, a + n), (name, 0, n)),
+                (scan, ("rm", a, a + n), ("rst", 0, n), ("st", a, a + n), A.min, A.max),
+                (tt, ("fl", FB + a, FB + a + n - 8), ("rm", a, a + n - 8), ("rm", a + 8, a + n), A.is_ge),
+                (turn, ("fl", FT + a, FT + a + n), ("fl", FB + a, FB + a + n))]
+
+    def signs(h, k, first, n, junk, total):
+        act(("jk", junk, junk + n), run(first, n), F.Sign, bias=("kb", 8 * h + k, 8 * h + k + 1), scale=-1.0, accum_out=total)
+
+    def words(h, ks):
+        for k in ks:
+            signs(h, k, 0, 128, 1024 * h + 128 * k, ("ac%d" % h, SEG * k + 64, SEG * k + 65))
+
+    def places(h, out):
+        li, wd, at = "li%d" % h, "wd%d" % h, 384 * h
+        acc, k = ("ac%d" % h, 64, 8 * SEG, SEG), ("mr", 128 * h, 128 * h + 128)
+
+        def in_word():
+            quant("q2", "c2", 160 * h, 160, "fl", at + 128)
+            for i, (name, b) in enumerate((("kd", 0), ("kd", 32), ("kj", 0), ("kj", 32))):
+                kmm(out, name, "q2", "c2", 160 * h + b, 128, i == 0, False)
+
+        def of_word():
+            quant("q3", "c3", 128 * h, 128, "fl", at)
+            kmm(out, "kw", "q3", "c3", 128 * h, 128, False, True)
+        return [(ts, (li, 0, 8), acc, 0.5, A.mult, 64.0, A.add),
+                (ts, (wd, 0, 8), acc, M32, A.add, -M32, A.add),
+                (tt, ("fl", at + 128, at + 256), run(FIRST, 128), k, A.is_le, (li, 0, 8)),
+                (tt, ("fl", at + 256, at + 384), run(LAST, 128), k, A.is_le, (li, 0, 8)),
+                (tt, (wd, 8, 16), acc, (wd, 0, 8), A.subtract),
+                (in_word,),
+                (tt, ("fl", at, at + 128), (wd, 0, 24), ("zmask", 0, 128), A.mult, ("go", 0, 8)),
+                (of_word,),
+                (ts, ("lf", 32 * h, 32 * h + 32), (out, 0, 32), cf(14), A.add)]
+
+    def gather(h, dst):
+        act((dst, 256, 512), ("win", 0, 8192), by=("lf", 32 * h + 16, 32 * h + 32))
+        copy((dst, 0, 256), ("win", 0, 8192), by=("lf", 32 * h, 32 * h + 16))
+
+    def numbers():
         for h in range(2):
-            fill("s2%d" % h, 0, 1024, 0.0)
-        o, w = slot("w", 0)
-        tt(o, T.mm[:, 128:256], T.sg[:, :], A.mult, [("mm", 128, 256), ("sg", 0, 128)], w)
-        for h in range(2):
-            quant("q2%d" % h, "c2%d" % h, 0, 256, "s2%d" % h, 0)
-        quant("kq", "kqs", 128 * 6, 256, "ks", 512 * 6)
-
-    def layer_constants():
-        a = 512 * KN["z0"]
-        fill("ks", a, a + 2048, 0.0)
-        for b in range(4):
-            o, w = slot("z%d" % b, b)
-            copy(o, T.i64[:, :], [("i64", 0, 128)], w)
-        quant("kq", "kqs", 128 * KN["z0"], 512, "ks", a)
-
-    def om_constants():
-        a = 512 * KN["o0"]
-        fill("ks", a, a + 4096, 0.0)
-        for t in range(4):
-            o, w = slot("o%d" % t, t)
-            copy(o, T.sg[:, :], [("sg", 0, 128)], w)
-            o, w = slot("n%d" % t, 0)
-            ts(o, T.sg[:, :], T.zm[:, 4 + t:5 + t], 32.0, A.mult, A.mult, [("sg", 0, 128), ("zm", 0, 8)], w)
-        quant("kq", "kqs", 128 * KN["o0"], 512, "ks", a)
-        quant("kq", "kqs", 128 * KN["n0"], 512, "ks", a + 2048)
-        quant("qv", "sv", 0, 128, "vb", 0)
-
-    def one_round(t):
-        steps = [(gr, b) for gr in range(8) for b in range(4)]
-        at = [0]
-
-        def pump(n, who="s"):
-            for gr, b in steps[at[0]:at[0] + n]:
-                bank = "w%d" % (at[0] % 4)
-                mm(bank, "eq", "es", 512 * gr + 128 * b, "qx", "sx", 0, 256)
-                a = 2048 * b + gr
-                o, i, w = T.win[:, a:2048 * b + 2048:8], T[bank][:, 0:256], [("win", a, 2048 * b + 2048, 8)]
-                if who == "s":
-                    act(o, i, F.Copy, [(bank, 0, 512)], w)
-                else:
-                    copy(o, i, [(bank, 0, 512)], w)
-                at[0] += 1
-
-        order("p", [("su2", 0, 128)], [])
-        mm("p0", "qu2", "su2", 0, "qx", "sx", 0, 256)
-        if t == 0:
-            e_tiles(2)
-        pump(8)
-        op("v", lambda e: e.transpose(T.st[:, :], T.p0[:, 0:256]), [("p0", 0, 512)], [("st", 0, 256)])
-        op("v", lambda e: e.tensor_tensor_scan(T.rm[:, :], T.rst[:, :], T.st[:, :], 0.0, A.min, A.max),
-           [("rst", 0, 256), ("st", 0, 256)], [("rm", 0, 256)])
-        tt(T.fb[:, 0:248], T.rm[:, 0:248], T.rm[:, 8:256], A.is_ge, [("rm", 0, 256)], [("fb", 0, 248)])
-        op("v", lambda e: e.transpose(T.ft[:, 0:256], T.fb[:, :]), [("fb", 0, 256)], [("ft", 0, 256)])
-        quant("qf", "sf", 0, 128, "ft", 0)
-        kmm("p1", "tot", "qf", "sf", 0)
-        kmm("p2", "aa", "qf", "sf", 0)
-        kmm("p3", "ab", "qf", "sf", 0)
-        if t == 0:
-            for gr in (3, 4):
-                e_tiles(gr)
-            more_constants()
-        pump(8)
-        op("v", lambda e: e.tensor_tensor_scan(T.pw[:, 0:64], T.zz[:, :], T.p1[:, 0:64], 0.0, A.add, A.add),
-           [("zz", 0, 64), ("p1", 0, 512)], [("pw", 0, 64)])
-        tt(T.tt[:, 0:64], T.p2[:, 0:64], T.pw[:, 0:64], A.add, [("p2", 0, 512), ("pw", 0, 64)], [("tt", 0, 64)])
-        tt(T.tt[:, 128:192], T.p3[:, 0:64], T.pw[:, 0:64], A.add, [("p3", 0, 512), ("pw", 0, 64)], [("tt", 128, 192)])
-        ts(T.vv[:, 128:129], T.pw[:, 63:64], 256.0, None, A.min, None, [("pw", 0, 64)], [("vv", 128, 129)])
-        ts(T.vv[:, 0:64], T.tt[:, 0:64], -256.0, 0.0, A.add, A.max, [("tt", 0, 64)], [("vv", 0, 64)])
-        ts(T.vv[:, 64:128], T.tt[:, 128:192], -256.0, 0.0, A.add, A.max, [("tt", 128, 192)], [("vv", 64, 128)])
-        V = [("vv", 0, 130)]
-        ts(T.r1[:, :], T.vv[:, :], M16, -M16, A.add, A.add, V, [("r1", 0, 130)])
-        ts(T.dg[:, 2:520:4], T.vv[:, :], M256, -M256, A.add, A.add, V, [("dg", 2, 520, 4)])
-        tt(T.dg[:, 0:520:4], T.vv[:, :], T.r1[:, :], A.subtract, V + [("r1", 0, 130)], [("dg", 0, 520, 4)])
-        tt(T.dg[:, 1:520:4], T.r1[:, :], T.dg[:, 2:520:4], A.subtract, [("r1", 0, 130), ("dg", 2, 520, 4)], [("dg", 1, 520, 4)])
-        quant("qd", "sd", 0, 130, "dg", 0)
-        kmm("p0", "tri", "qd", "sd", 128)
-        kmm("p1", "x15", "qd", "sd", 64)
-        kmm("p2", "rc", "qd", "sd", 0)
-        if t == 0:
-            for gr in (5, 6, 7):
-                e_tiles(gr)
-            list_constants()
-        pump(8)
-        N = T.pw[:, 63:64]
-        ts(T.xi[:, 0:1], T.p0[:, 0:1], N, T.cf[:, 7:8], A.add, A.subtract, CF + [("p0", 0, 512), ("pw", 0, 64)], [("xi", 0, 1)])
-        XI = [("xi", 0, 1), ("pw", 0, 64)]
-        ts(T.pw[:, 64:128], T.p1[:, 0:64], T.xi[:, 0:1], N, A.add, A.max, XI + [("p1", 0, 512)], [("pw", 64, 128)])
-        ts(T.tt[:, 64:128], T.p2[:, 0:64], T.xi[:, 0:1], N, A.add, A.max, XI + [("p2", 0, 512)], [("tt", 64, 128)])
-        ts(T.tt[:, 192:256], T.p2[:, 64:128], T.xi[:, 0:1], N, A.add, A.max, XI + [("p2", 0, 512)], [("tt", 192, 256)])
-
-        def words(h):
-            for k in range(8 * h, 8 * h + 8):
-                act(T.jk[:, 128 * k:128 * k + 128], T.pw[:, 0:128], F.Sign, [("pw", 0, 128), ("kb", 0, 16)],
-                    [("ac", k, k + 1), ("jk", 128 * k, 128 * k + 128)], bias=T.kb[:, k:k + 1], scale=-1.0, accum_out=T.ac[:, k:k + 1])
-
-        def places(h, bank):
-            li, wi, wd, s2, q2, c2, lf = ["%s%d" % (n, h) for n in ("li", "wi", "wd", "s2", "q2", "c2", "lf")]
-            acc, R = T.ac[:, 8 * h:8 * h + 8], [("ac", 8 * h, 8 * h + 8)]
-            ts(T[li][:, 0:8], acc, 0.5, 64.0, A.mult, A.add, R, [(li, 0, 8)])
-            ts(T[wi][:, 0:8], acc, 0.5, 64.0, A.mult, A.add, R, [(wi, 0, 8)])
+            name = "p%d" % (1 + h)
+            kmm(name, "kn", "q2", "c2", 160 * h, 128, True, False)
+            kmm(name, "kn", "q2", "c2", 160 * h + 32, 128, False, False)
             for i in range(2):
-                tt(T[s2][:, 128 * i:128 * i + 128], T.tt[:, 128 * i:128 * i + 128].indirect(T[li][:, 0:8]), T.mr[:, 128 * h:128 * h + 128],
-                   A.is_le, [("tt", 128 * i, 128 * i + 128), (li, 0, 8), ("mr", 0, 256)], [(s2, 128 * i, 128 * i + 128)])
-                ts(T[wd][:, 8 * i:8 * i + 8], T[wi][:, 0:8], (48, 15)[i], None, A.bitwise_and, None, [(wi, 0, 8)], [(wd, 8 * i, 8 * i + 8)])
-            for z in range(4):
-                ts(T[s2][:, 256 + 4 * z:512:16], T[wd][:, 0:16], T.zm[:, z:z + 1], None, A.mult, None, [(wd, 0, 16), ("zm", 0, 4)],
-                   [(s2, 256 + 4 * z, 512, 16)])
-            quant(q2, c2, 0, 128, s2, 0)
-            for i in range(4):
-                kmm(bank, "ssww"[i], q2, c2, 32 * i, 128, i == 0, i == 3)
-            ts(T[lf][:, 0:32], T[bank][:, 0:32], T.cf[:, 8:9], None, A.add, None, CF + [(bank, 0, 512)], [(lf, 0, 32)])
+                kmm(name, "kw", "q3", "c3", 128 * h, 128, False, i == 1)
+            act(("omf", 32 * h, 32 * h + 32), (name, 0, 32), F.Identity, bias=2048.0)
+        return [(turn, ("omf", 64, 128), ("omf", 0, 64)), (numbers_out,)]
 
-        def gather(h, dst):
-            lf = "lf%d" % h
-            R = [("win", 0, 8192), (lf, 0, 32)]
-            copy(T[dst][:, 0:256], T.win[:, 0:8192].indirect(T[lf][:, 0:16]), R, [(dst, 0, 256)])
-            act(T[dst][:, 256:512], T.win[:, 0:8192].indirect(T[lf][:, 16:32]), F.Copy, R, [(dst, 256, 512)])
+    def numbers_out():
+        copy(("omf", 128, 144), ("omf", 64, 128, 4))
+        dma("y", [(T.om[c:8:2, 128 * h:128 * h + 128], T.omf[:, 128 + 8 * h + 4 * c:132 + 8 * h + 4 * c]) for h in range(2) for c in range(2)],
+            [("omf", 128, 144)], [], "dst")
 
-        def om_half(h):
-            for i in range(4):
-                bank = "w%d" % i
-                for j in range(4):
-                    kmm(bank, ("o%d" if j < 2 else "n%d") % i, "q2%d" % h, "c2%d" % h, 32 * j, 128, j == 0, j == 3)
-                act(T.omf[:, 128 * h + i:128 * h + 128:4], T[bank][:, 0:32], F.Copy, [(bank, 0, 512)], [("omf", 128 * h + i, 128 * h + 128, 4)])
+    def codes_out(h):
+        a = 128 * h
+        dma("y", [(T.oc[:, 4 * a:4 * a + 512], T.qx[:, a:a + 128].bitcast(dt.uint8))], [("qx", a, a + 128)], [], "dst")
 
-        words(1)
-        pump(8, "v")
-        words(0)
-        places(1, "p3")
-        gather(1, "hc")
+    def product_out(h):
+        a, name = 128 * h, "w%d" % h
+        mm(name, "qv", "sv", 0, "qx", "sx", a, 128)
+        copy(("yt", a, a + 128), (name, 0, 128))
+        dma("y", [(T.y[:, a:a + 128], T.yt[:, a:a + 128])], [("yt", a, a + 128)], [], "dst")
+
+    def send(t):
         qy, sy = "qy%d" % t, "sy%d" % t
-        quant(qy, sy, 0, 128, "hc", 0)
-        partner = T.cores[rank ^ XOR[t]]
-        rel = relays(topo, core, partner)
+        rel = relays(topo, core, T.cores[rank ^ XOR[t]])
         order("g", [(qy, 0, 128)], [])
         moves = []
-        for i, c in enumerate(rel):
+        for i, c in enumerate(rel[:NREL]):
             rid, pid = topo.addr(c, core)
             es = topo.engines(core, c)
             k = len(es) // NREL
@@ -453,55 +483,170 @@ def rank_program(g, core, T, topo):
                                            remote_sem=T.sem["in%d" % t], src=T[qy][:, PC * i:PC * i + PC].bitcast(dt.uint8),
                                            dst=T["rq%d" % t][:, 0:PC].bitcast(dt.uint8)))
         g.remote_dma_fused(moves, local_sem=T.sem.loc)
-        c = rel[-1]
-        rid, pid = topo.addr(c, core)
+        rid, pid = topo.addr(rel[NREL], core)
         g.remote_dma(out_ap=T["rs%d" % t][:, 0:128], in_ap=T[sy][:, 0:128], remote_sem=T.sem["in%d" % t], local_sem=T.sem.loc,
-                     pid=pid, routing_id=rid, dma_engine_mask=topo.mask(core, c))
-        places(0, "p0")
-        gather(0, "hk")
-        quant("qz", "sz", 0, 128, "hk", 0)
-        act(T.z64[:, :], T.hk[:, :], F.Identity, [("hk", 0, 512)], [("z64", 0, 512)], scale=64.0)
-        if t == 0:
-            layer_constants()
-            order("p", [("sw", 0, 512)], [])
-        for b in range(4):
-            mm("w%d" % b, "qw", "sw", 128 * b, "qz", "sz", 0, 128)
-        for b in range(4):
-            r = [("r64", 128 * b, 128 * b + 128)]
-            tt(T.r64[:, 128 * b:128 * b + 128], T["w%d" % b][:, 0:128], T.z64[:, b:512:4], A.add, [("w%d" % b, 0, 512), ("z64", 0, 512)], r)
-            act(T.xt[:, b:512:4], T.r64[:, 128 * b:128 * b + 128], F.Identity, r, [("xt", b, 512, 4)], scale=0.015625)
-        quant("qx", "sx", 0, 128, "xt", 0)
-        if t == 1:
-            om_constants()
-        if t == 2:
-            om_half(1)
-            om_half(0)
+                     pid=pid, routing_id=rid, dma_engine_mask=topo.mask(core, rel[NREL]))
+
+    def arrived(t, who):
         lq, ls = "lq%d" % t, "ls%d" % t
-        far = [len(topo.engines(c, core)) for c in relays(topo, partner, core)]
-        arrive("arr%d" % t, sum(far) + far[-1], [(lq, 0, 128)])
+        arrive("arr%d" % t, sum(len(topo.engines(c, core)) for c in relays(topo, T.cores[rank ^ XOR[t]], core)), [(lq, 0, 128)])
         for b in range(4):
-            bank = "p%d" % b
-            mm(bank, "qw", "sw", 128 * b, lq, ls, 0, 128, True, False)
-            kmm(bank, "z%d" % b, lq, ls, 0, 128, False, True)
-            o, i, w = T.xt[:, 512 + b:1024:4], T[bank][:, 0:128], [("xt", 512 + b, 1024, 4)]
-            if b % 2 == 0:
-                act(o, i, F.Identity, [(bank, 0, 512)], w, scale=0.015625)
-            else:
-                ts(o, i, 0.015625, None, A.mult, None, [(bank, 0, 512)], w)
+            name = "p%d" % (3 - b)
+            mm(name, "qw", "sw", 128 * b, lq, ls, 0, 128, True, False)
+            mm(name, "zq", "zs", 128 * b, lq, ls, 0, 128, False, True)
+            if who[b] == "s":
+                act(("xt", 512 + b, 1024, 4), (name, 0, 128), F.Identity, scale=0.015625)
+            elif who[b] == "v":
+                scaled(b)
+
+    def scaled(b):
+        ts(("xt", 512 + b, 1024, 4), ("p%d" % (3 - b), 0, 128), 0.015625, A.mult)
+
+    def taken(N, h):
+        ts(("wd%d" % h, 16, 24), ("kb", 8 * h, 8 * h + 8), N, A.is_gt, -64.0, A.mult)
+
+    def one_round(t):
+        a, n = (0, 256) if t == 0 else (128, 128)
+        mm("p0", "qu", "su", 0, "qx", "sx", a, n)
+        steps = window(a, n, "came" if t else "both")
+        gap(1 if t else 2)
+        calls = choices("p0", a, n)
+        if t == 0:
+            now(calls[:1])
+            del calls[:1]
+            gap(2)
+        pump(steps, (4, 8, 4)[t])
+        gap(1 if t == 1 else 0)
+        if t == 0:
+            fills()
+        for call in calls:
+            now([call])
+            gap()
+        quant("qf", "sf", 0, 128, "fl", FT)
+        until(counts_ready)
+        kmm("p1", "tot", "qf", "sf", 0)
+        kmm("p2", "aa", "qf", "sf", 0)
+        until(flags_ready)
+        kmm("p3", "ab", "qf", "sf", 0)
+        kmm("p0", "oa", "qf", "sf", 0)
+        gap(2)
+        N = run(CHOSEN + 63, 1)
+        scan(run(CHOSEN), ("one", 0, 64), ("p1", 0, 64), A.mult, A.add, -256.0)
+        until(marks_ready)
+        kmm("w0", "ob", "qf", "sf", 0)
+        pump(steps, 4, "w3")
+        for k in range(NV):
+            signs(1, k, CHOSEN, 64, 2048 + 64 * k, ("inj", SEG * k, SEG * k + 1))
+        if t == 0:
+            more_fills()
+        tt(run(FIRST), run(CHOSEN), ("p2", 0, 64), A.subtract)
+        tt(run(LAST), run(CHOSEN), ("p3", 0, 64), A.subtract)
+        ts(("free", 0, 1), N, cf(16), A.add, 0.0, A.min)
+        scan(("fl", DG + 8, DG + 264, 4), run(FIRST), ("p0", 0, 64), A.max, A.min)
+        scan(("fl", DG + 9, DG + 264, 4), run(LAST), ("w0", 0, 64), A.max, A.min)
+        ts(("fl", DG, DG + 1), ("free", 0, 1), -16.0, A.max)
+        gap()
+        quant("qd", "sd", 0, 130, "fl", DG)
+        until(digits_ready)
+        kmm("p0", "tri", "qd", "sd", 0)
+        kmm("p1", "all", "qd", "sd", 2)
+        ts(("kv", 0, 8), ("kb", 8, 16), N, A.is_gt, 4096.0, A.mult)
+        gap(1)
+        tt(("kv", 8, 16), ("kv", 0, 8), ("kb", 16, 24), A.add)
+        taken(N, 1)
+        if t:
+            taken(N, 0)
+        op("v", lambda e: e.tensor_tensor_scan(ap(run(RAW)), T.one[:, 0:64], T.p1[:, 0:64], T.p0[:, 0:1], A.mult, A.add),
+           [("one", 0, 64), ("p0", 0, 512), ("p1", 0, 512)], [run(RAW)])
+        until(first_ready)
+        kmm("p2", "ra", "qd", "sd", 2)
+        ts(run(REFUSED), run(RAW), N, A.max)
+        words(1, range(NV, 8))
+        if t == 0:
+            weights()
+        for k in range(NV):
+            ts(("wb", SEG * k, SEG * k + 64), run(RAW), ("kv", 8 + k, 9 + k), A.is_le, 2.0, A.mult)
+        gap(0 if t else 1)
+        scan(("ac1", 0, SEG * NV), ("inj", 0, SEG * NV), ("wb", 0, SEG * NV), A.min, A.add, 1000.0)
+        until(last_ready)
+        kmm("p3", "rb", "qd", "sd", 2)
+        tt(run(FIRST + 64), run(RAW), ("p2", 0, 64), A.subtract)
+        words(0, range(8))
+        go, stay = places(1, "w0"), places(0, "p0")
+        now(go[:2])
+        gap(2)
+        tt(run(LAST + 64), run(RAW), ("p3", 0, 64), A.subtract)
+        pump(steps, 32, "p3")
+        if t:
+            later.extend([stay[0], stay[1], stay[2], stay[4], stay[3]])
+            del stay[:5]
+        now([go[2], go[4], go[3], go[6]])
+        until(weights_ready)
+        now(go[5:6])
+        until(lists_ready)
+        now(go[7:8])
+        gap(3)
+        now(go[8:])
+        gap()
+        gather(1, "hc")
+        gap()
+        quant("qy%d" % t, "sy%d" % t, 0, 128, "hc", 0)
+        send(t)
+        if t == 0:
+            act(("zz64", 0, 516), ("z1", 0, 516), F.Identity, scale=64.0)
+            later.extend((quant, "zq", "zs", 128 * b, 128, "zz64", 3 - b) for b in range(4))
+            order("p", [("sw", 0, 512)], [])
+            taken(N, 0)
+        now(stay[:-1])
+        gap(2)
+        now(stay[-1:])
+        gap()
+        gather(0, "hk")
+        gap(2)
+        quant("qz", "sz", 0, 128, "hk", 0)
+        if t == 2:
+            later.extend(numbers())
+        for b in range(4):
+            act(("z64", b, 512, 4), ("hk", b, 512, 4), F.Identity, scale=64.0)
+            mm("w%d" % b, "qw", "sw", 128 * b, "qz", "sz", 0, 128)
+        if t > 0:
+            arrived(t, "sss-")
+        gap()
+        for b in range(4):
+            tt(("x64", b, 512, 4), ("w%d" % b, 0, 128), ("z64", b, 512, 4), A.add)
+        gap()
+        ts(("xt", 0, 512), ("x64", 0, 512), 0.015625, A.mult)
+        gap()
+        quant("qx", "sx", 0, 128, "xt", 0)
+        if t < 2:
+            mm("w0", "qu", "su", 0, "qx", "sx", 0, 128)
+            later.extend(choices("w0", 0, 128))
+        if t == 0:
+            gap(1)
+            pump(window(0, 128, "kept"), 32)
+            dma("y", [(T.vb[:, :], T.v[:, :])], [], [("vb", 0, 512)], "dv")
+            gap(3)
+            kquant("kn")
+            arrived(t, "svsv")
+        if t == 1:
+            later.append((quant, "qv", "sv", 0, 128, "vb", 0))
+        if t == 2:
+            codes_out(0)
+        if t > 0:
+            scaled(3)
+        if t == 1:
+            pump(window(0, 128, "kept"), 32, "p3")
         quant("qx", "sx", 128, 128, "xt", 512)
 
     for t in range(3):
         one_round(t)
 
-    mm("w0", "qv", "sv", 0, "qx", "sx", 0, 256)
-    copy(T.yt[:, 0:256], T.w0[:, 0:256], [("w0", 0, 512)], [("yt", 0, 256)])
-    dma("y", lambda e: e.dma_start(T.om[:, :], T.omf[0:128:16, :]), [("omf", 0, 256)], [], "dst")
-    dma("y", lambda e: e.dma_start(T.oc[:, :], T.qx[:, 0:256].bitcast(dt.uint8)), [("qx", 0, 256)], [], "dst")
-    for k in range(4):
-        dma("s", lambda e: e.dma_start(T.osc[4 * k:4 * k + 4, :], T.sx[32 * k:32 * k + 4, 0:256]), [("qx", 0, 256)], [], "dst")
-    dma("y", lambda e: e.dma_start(T.y[:, :], T.yt[:, :]), [("yt", 0, 256)], [], "dst")
+    codes_out(1)
+    product_out(0)
+    dma("s", [(T.osc[4 * k:4 * k + 4, :], T.sx[32 * k:32 * k + 4, 0:256]) for k in range(4)], [("qx", 0, 256)], [], "dst")
+    product_out(1)
     n = 0
     for t in range(3):
         rel = relays(topo, core, T.cores[rank ^ XOR[t]])
-        n += sum(len(topo.engines(core, c)) // NREL for c in rel) + len(topo.engines(core, rel[-1]))
+        n += sum(len(topo.engines(core, c)) // NREL for c in rel[:NREL]) + len(topo.engines(core, rel[NREL]))
     finish([("loc", n)])

@@ -8,12 +8,13 @@ F8 = "float8_e4m3fn_x4"
 BIG = 2.0 ** 90
 M32 = 1.5 * 2.0 ** 28
 LW = 160
-BY_DMA = {"both": 7, "kept": 7, "came": 5}
+BY_DMA = [6, 5, 5]
 NV = 5
+EARLY = 4
 SEG = 66
 
-KN = {n: i for i, n in enumerate(["tot", "aa", "ab", "oa", "ob", "tri", "all", "ra", "rb", "kd", "kj", "kw", "kn"])}
-REFUSED, CHOSEN, FIRST, LAST, RAW = 0, 64, 128, 256, 384
+KN = {n: i for i, n in enumerate(["tot", "aa", "ab", "oa", "ob", "all", "ra", "rb", "kd", "kj", "kw", "kn"])}
+REFUSED, CHOSEN, FIRST, LAST, RAW = 0, 64, 128, 256, 392
 DG, FT, FB = 768, 1032, 1288
 
 
@@ -27,13 +28,13 @@ SCRATCH = {
     "qw": sb(512, F8), "sw": sb(512, "uint8"), "qx": sb(256, F8), "sx": sb(256, "uint8"),
     "eq": sb(4 * LW, F8), "es": sb(4 * LW, "uint8"), "zq": sb(512, F8), "zs": sb(512, "uint8"),
     "kq": sb(128 * len(KN), F8), "kqs": sb(128 * len(KN), "uint8"), "ks": sb(512 * len(KN)),
-    "jj": sb(512), "z1": sb(1024), "zz64": sb(528), "one": sb(64),
+    "jj": sb(512), "z1": sb(1024), "zz64": sb(528), "one": sb(72),
     "mx": sb(512), "ct": sb(512), "ct2": sb(512), "mt": sb(128), "mr": sb(256), "i16": sb(16), "zmask": sb(128),
-    "pc": sb(16, "int32"), "cf": sb(24, "float32"), "nk": sb(32, "float32"), "kb": sb(24, "float32"),
+    "pc": sb(16, "int32"), "cf": sb(24, "float32"), "nk": sb(40, "float32"), "kb": sb(24, "float32"),
     "qu1": sb(128, F8), "su1": sb(128, "uint8"), "uo": sb(8, "uint16"), "go": sb(8, "uint16"),
     "rst": sb(256, "float32"), "inj": sb(SEG * NV, "float32"),
     "st": sb(256, "float32"), "rm": sb(256, "float32"), "fl": sb(1544), "qf": sb(128, F8), "sf": sb(128, "uint8"),
-    "tt": sb(448, "float32"), "free": sb(8, "float32"), "kv": sb(16, "float32"), "m64": sb(192),
+    "tt": sb(456, "float32"), "free": sb(64, "float32"), "kv": sb(16, "float32"), "m64": sb(192),
     "qd": sb(130, F8), "sd": sb(130, "uint8"), "r16": sb(16),
     "jk": sb(2688), "wb": sb(SEG * NV), "q2": sb(320, F8), "c2": sb(320, "uint8"), "q3": sb(256, F8), "c3": sb(256, "uint8"), "lf": sb(64, "uint16"),
     "win": sb(8192), "hk": sb(512), "hc": sb(512), "z64": sb(512), "x64": sb(512), "xt": sb(1024),
@@ -48,7 +49,7 @@ for _t in range(3):
 PSUM = ["w0", "w1", "w2", "w3", "p0", "p1", "p2", "p3"]
 for _b in PSUM:
     SCRATCH[_b] = ("psum", [128, 512], "float32")
-SEMAPHORES = ["qg", "qv", "qs", "qp", "dx", "du", "dv", "dwc", "dws", "dst", "loc", "turn0", "turn1"] + \
+SEMAPHORES = ["qg", "qv", "qs", "qp", "dx", "du", "dv", "dwc", "dws", "dst", "loc", "turn"] + \
     ["%s%d" % (n, t) for n in ("arr", "in") for t in range(3)]
 
 
@@ -210,7 +211,9 @@ def rank_program(g, core, T, topo):
         op("v", lambda e: e.tensor_copy(ap(out), src), reads, [out])
 
     def scan(out, d0, d1, o0, o1, first=0.0):
-        op("v", lambda e: e.tensor_tensor_scan(ap(out), ap(d0), ap(d1), first, o0, o1), [bank(d0), bank(d1)], [out])
+        column = isinstance(first, tuple)
+        op("v", lambda e: e.tensor_tensor_scan(ap(out), ap(d0), ap(d1), ap(first) if column else first, o0, o1),
+           [bank(d0), bank(d1)] + ([bank(first)] if column else []), [out])
 
     def turn(out, in_):
         op("v", lambda e: e.transpose(ap(out), ap(in_)), [bank(in_)], [out])
@@ -276,16 +279,7 @@ def rank_program(g, core, T, topo):
     def last_ready():
         pass
 
-    def weights():
-        act(cf(13), cf(11), F.Identity, bias=1024.0)
-        act(cf(12), cf(9), F.Identity, scale=4.0)
-        act(slot("kd"), slot("kn"), F.Identity, scale=cf(13))
-        act(slot("kj"), slot("kn"), F.Identity, scale=cf(12))
-
     def digits_ready():
-        pass
-
-    def lists_ready():
         pass
 
     def weights_ready():
@@ -299,7 +293,8 @@ def rank_program(g, core, T, topo):
     iota(("jj", 0, 512), [[1, 512]], 0, -4)
     iota(("i16", 0, 16), [[16, 16]], 0, 0)
     iota(("m64", 0, 64), [[1, 16], [-8, 4]], 0, 0)
-    fill(("one", 0, 64), 1.0)
+    fill(("one", 0, 72), 1.0)
+    fill(("fl", DG, DG + 264), 0.0)
     ts(pc(1), pc(0), 15, A.bitwise_and)
     ts(pc(2), pc(0), 4, A.arith_shift_right)
     ts(pc(3), pc(0), 3, A.bitwise_and)
@@ -321,23 +316,25 @@ def rank_program(g, core, T, topo):
     unpacking = [(quant, "eq", "es", LW * b, LW, "z1", 3 - b) for b in range(4)]
     now(unpacking[:1])
     act(cf(8), cf(2), F.Identity, scale=4.0)
-    act(cf(16), cf(1), F.Identity, scale=16.0)
+    act(cf(16), cf(1), F.Identity, scale=16.0, bias=-256.0)
+    act(cf(6), cf(1), F.Identity, bias=0.5 - 256.0)
+    act(cf(7), cf(3), F.Identity, bias=1024.0)
     act(cf(10), cf(3), F.Identity, bias=cf(8))
 
-    def by_group(name, pattern):
+    def by_group(name, pattern, first=32):
         a = slot(name)[1]
         for c in range(8):
-            act(("ks", a + 64 * c, a + 64 * c + 64), pattern, F.Identity, scale=("nk", 24 + c, 25 + c))
+            act(("ks", a + 64 * c, a + 64 * c + 64), pattern, F.Identity, scale=("nk", first + c, first + c + 1))
 
-    by_group("tot", ("one", 0, 64))
+    by_group("tot", ("one", 0, 64), 24)
     op("v", lambda e: e.tensor_copy(T.qu[:, 0:128].bitcast(dt.uint32), T.qu1[:, 0:128].bitcast(dt.uint32).indirect(T.uo[:, 0:8])),
        [("qu1", 0, 128), ("uo", 0, 8)], [("qu", 0, 128)])
     op("s", lambda e: e.activation(T.su[:, 0:128], T.su1[:, 0:128].indirect(T.uo[:, 0:8]), F.Copy), [("qu1", 0, 128), ("uo", 0, 8)], [("su", 0, 128)])
+    ts(("nk", 32, 40), ("nk", 24, 32), ("nk", 7, 8), A.subtract, -4096.0, A.mult)
     ts(("m64", 64, 128), ("m64", 0, 64), cf(2), A.is_equal)
     quant("qx", "sx", 0, 256, "x0", 0)
     ts(("m64", 128, 192), ("m64", 0, 64), 16.0, A.add, cf(2), A.is_equal)
     ts(("pc", 8, 10), ("pc", 6, 8), 7, A.bitwise_and)
-    act(cf(9), ("nk", 7, 8), F.Identity, bias=("nk", 15, 16))
     act(("rst", 128, 256), ("rst", 0, 128))
     by_group("oa", ("m64", 64, 128))
     iota(("ct2", 0, 512), [[1, 32], [0, 16]], 0, 0)
@@ -353,52 +350,48 @@ def rank_program(g, core, T, topo):
 
     later += unpacking[1:] + [
         (kquant, "tot"),
-        (ts, slot("tri"), ("ct2", 0, 512), cf(8), A.is_ge),
-        (kquant, "aa"), (kquant, "oa"), (counts_ready,), (kquant, "ab"), (flags_ready,),
-        (kquant, "tri"),
         (ts, slot("kw"), ("ct2", 0, 512), cf(10), A.is_equal, 8.0, A.mult),
-        (kquant, "ob"), (marks_ready,),
-        (ts, slot("ra"), ("mx", 0, 512), cf(1), A.is_lt),
-        (kquant, "all"), (digits_ready,),
-        (ts, slot("kn"), ("ct", 0, 512), cf(8), A.is_equal),
+        (kquant, "aa"), (kquant, "oa"), (counts_ready,), (kquant, "ab"), (flags_ready,),
+        (kquant, "kw"),
         (ts, cf(11), pc(8), 7.0, A.is_equal, -8192.0, A.mult),
-        (kquant, "ra"), (first_ready,),
-        (ts, slot("rb"), ("mx", 0, 512), 100.0, A.add, cf(1), A.is_lt),
         (ts, cf(15), cf(3), 2.0, A.min, 8.0, A.mult),
-        (kquant, "rb"), (last_ready,),
-        (ts, ("go", 0, 8), ("r16", 0, 8), cf(15), A.add),
+        (kquant, "ob"), (marks_ready,),
+        (ts, ("ks", slot("all")[1] + 2, slot("all")[2], 4), ("ct2", 2, 512, 4), cf(8), A.is_ge),
+        (kquant, "all"), (digits_ready,),
+        (ts, slot("ra"), ("mx", 0, 512), cf(1), A.is_lt),
+        (ts, slot("rb"), ("mx", 0, 512), 100.0, A.add, cf(1), A.is_lt),
+        (kquant, "ra"), (kquant, "rb"), (first_ready,),
+        (ts, slot("kd"), ("ct", 0, 512), cf(8), A.is_equal, cf(13), A.mult),
+        (ts, ("go", 0, 8), ("r16", 0, 8), cf(15), A.add), (last_ready,),
         (ts, ("zmask", 0, 128), ("mt", 0, 128), cf(4), A.is_equal),
-        (kquant, "kd"), (kquant, "kj"), (weights_ready,),
-        (kquant, "kw"), (lists_ready,),
-        (ts, cf(14), pc(9), 1024.0, A.mult, cf(7), A.add)]
+        (kquant, "kd"),
+        (ts, cf(14), pc(9), 1024.0, A.mult, cf(7), A.add),
+        (kquant, "kj"), (weights_ready,)]
 
     def fills():
         by_group("ob", ("m64", 128, 192))
-        sfill(("fl", DG, DG + 264), 0.0)
         sfill(slot("all"), 1.0)
-        act(cf(6), cf(1), F.Identity, bias=0.5 - 256.0)
-        sfill(("inj", 0, SEG * NV), BIG)
         act(("kb", 0, 16), ("i16", 0, 16), F.Identity, bias=cf(6))
-        act(cf(7), cf(3), F.Identity, bias=1024.0)
+        sfill(("inj", 0, SEG * NV), BIG)
         act(("kb", 16, 24), ("kb", 8, 16), F.Identity, bias=-4096.0)
+        act(cf(9), ("nk", 7, 8), F.Identity, bias=("nk", 15, 16))
 
     def more_fills():
-        sfill(("wb", 64, SEG * NV, SEG), -64.0)
-        sfill(("wb", 65, SEG * NV, SEG), 1000.0)
+        act(cf(13), cf(11), F.Identity, bias=1024.0)
+        act(cf(17), cf(11), F.Identity, scale=(1 / 1792 + 1 / 256) / 8192, bias=1 / 256)
+        iota(("wb", 64, SEG * NV, SEG), [[0, NV]], -64, 0)
+        iota(("wb", 65, SEG * NV, SEG), [[0, NV]], 1000, 0)
 
-    def window(a, n, kind):
-        copied = BY_DMA[kind]
-
+    def window(copied):
         def step(d, b, name):
-            mm(name, "eq", "es", LW * b + 16 * d, "qx", "sx", a, n)
-            act(("win", 1024 * d + 4 * a + b, 1024 * d + 4 * (a + n), 4), (name, 0, n))
+            mm(name, "eq", "es", LW * b + 16 * d, "qx", "sx", 0, 256)
+            act(("win", 1024 * d + b, 1024 * d + 1024, 4), (name, 0, 256))
             if d == 0 and b == 3:
-                lo, hi, pairs = 4 * a, 4 * (a + n), []
+                pairs = []
                 for k in range(8 - copied, 8):
-                    pairs.append((T.win[0:128 - 16 * k, 1024 * k + lo:1024 * k + hi], T.win[16 * k:128, lo:hi]))
-                    pairs.append((T.win[128 - 16 * k:128, 1024 * k + lo:1024 * k + hi], T.win[0:16 * k, lo:hi]))
-                dma("y", pairs, [("win", lo, hi)], [("win", 1024 * k + lo, 1024 * k + hi) for k in range(8 - copied, 8)],
-                    "turn%d" % (a // 128))
+                    pairs.append((T.win[0:128 - 16 * k, 1024 * k:1024 * k + 1024], T.win[16 * k:128, 0:1024]))
+                    pairs.append((T.win[128 - 16 * k:128, 1024 * k:1024 * k + 1024], T.win[0:16 * k, 0:1024]))
+                dma("y", pairs, [("win", 0, 1024)], [("win", 1024 * (8 - copied), 8192)], "turn")
         return [(step, d, b) for d in range(8 - copied) for b in range(4)]
 
     def pump(steps, n, last="w0"):
@@ -425,11 +418,13 @@ def rank_program(g, core, T, topo):
 
         def in_word():
             quant("q2", "c2", 160 * h, 160, "fl", at + 128)
-            for i, (name, b) in enumerate((("kd", 0), ("kd", 32), ("kj", 0), ("kj", 32))):
-                kmm(out, name, "q2", "c2", 160 * h + b, 128, i == 0, False)
+            for b in (0, 32):
+                kmm(out, "kd", "q2", "c2", 160 * h + b, 128, b == 0, False)
 
         def of_word():
             quant("q3", "c3", 128 * h, 128, "fl", at)
+            for b in (0, 32):
+                kmm(out, "kj", "q2", "c2", 160 * h + b, 128, False, False)
             kmm(out, "kw", "q3", "c3", 128 * h, 128, False, True)
         return [(ts, (li, 0, 8), acc, 0.5, A.mult, 64.0, A.add),
                 (ts, (wd, 0, 8), acc, M32, A.add, -M32, A.add),
@@ -487,20 +482,15 @@ def rank_program(g, core, T, topo):
         g.remote_dma(out_ap=T["rs%d" % t][:, 0:128], in_ap=T[sy][:, 0:128], remote_sem=T.sem["in%d" % t], local_sem=T.sem.loc,
                      pid=pid, routing_id=rid, dma_engine_mask=topo.mask(core, rel[NREL]))
 
-    def arrived(t, who):
+    def arrived(t):
         lq, ls = "lq%d" % t, "ls%d" % t
         arrive("arr%d" % t, sum(len(topo.engines(c, core)) for c in relays(topo, T.cores[rank ^ XOR[t]], core)), [(lq, 0, 128)])
         for b in range(4):
             name = "p%d" % (3 - b)
             mm(name, "qw", "sw", 128 * b, lq, ls, 0, 128, True, False)
             mm(name, "zq", "zs", 128 * b, lq, ls, 0, 128, False, True)
-            if who[b] == "s":
+            if b < 3:
                 act(("xt", 512 + b, 1024, 4), (name, 0, 128), F.Identity, scale=0.015625)
-            elif who[b] == "v":
-                scaled(b)
-
-    def scaled(b):
-        ts(("xt", 512 + b, 1024, 4), ("p%d" % (3 - b), 0, 128), 0.015625, A.mult)
 
     def taken(N, h):
         ts(("wd%d" % h, 16, 24), ("kb", 8 * h, 8 * h + 8), N, A.is_gt, -64.0, A.mult)
@@ -508,15 +498,15 @@ def rank_program(g, core, T, topo):
     def one_round(t):
         a, n = (0, 256) if t == 0 else (128, 128)
         mm("p0", "qu", "su", 0, "qx", "sx", a, n)
-        steps = window(a, n, "came" if t else "both")
+        steps = window(BY_DMA[t])
         gap(1 if t else 2)
         calls = choices("p0", a, n)
         if t == 0:
             now(calls[:1])
             del calls[:1]
             gap(2)
-        pump(steps, (4, 8, 4)[t])
-        gap(1 if t == 1 else 0)
+        pump(steps, 4)
+        pump(steps, 4 if t else 0, "p3")
         if t == 0:
             fills()
         for call in calls:
@@ -525,78 +515,83 @@ def rank_program(g, core, T, topo):
         quant("qf", "sf", 0, 128, "fl", FT)
         until(counts_ready)
         kmm("p1", "tot", "qf", "sf", 0)
-        kmm("p2", "aa", "qf", "sf", 0)
+        kmm("p0", "aa", "qf", "sf", 0, 128, True, False)
+        kmm("p0", "oa", "qf", "sf", 0, 128, False, True)
         until(flags_ready)
-        kmm("p3", "ab", "qf", "sf", 0)
-        kmm("p0", "oa", "qf", "sf", 0)
-        gap(2)
+        kmm("w0", "ab", "qf", "sf", 0, 128, True, False)
+        gap(4)
         N = run(CHOSEN + 63, 1)
         scan(run(CHOSEN), ("one", 0, 64), ("p1", 0, 64), A.mult, A.add, -256.0)
         until(marks_ready)
-        kmm("w0", "ob", "qf", "sf", 0)
-        pump(steps, 4, "w3")
+        kmm("w0", "ob", "qf", "sf", 0, 128, False, True)
+        kmm("p2", "aa", "qf", "sf", 0)
+        kmm("p3", "ab", "qf", "sf", 0)
+        scan(("free", 0, 64), ("one", 0, 64), ("p1", 0, 64), A.mult, A.add, cf(16))
         for k in range(NV):
             signs(1, k, CHOSEN, 64, 2048 + 64 * k, ("inj", SEG * k, SEG * k + 1))
         if t == 0:
             more_fills()
-        tt(run(FIRST), run(CHOSEN), ("p2", 0, 64), A.subtract)
-        tt(run(LAST), run(CHOSEN), ("p3", 0, 64), A.subtract)
-        ts(("free", 0, 1), N, cf(16), A.add, 0.0, A.min)
-        scan(("fl", DG + 8, DG + 264, 4), run(FIRST), ("p0", 0, 64), A.max, A.min)
-        scan(("fl", DG + 9, DG + 264, 4), run(LAST), ("w0", 0, 64), A.max, A.min)
-        ts(("fl", DG, DG + 1), ("free", 0, 1), -16.0, A.max)
+        pump(steps, 2)
+        if t == 0:
+            act(cf(12), cf(17), F.Identity, scale=cf(9))
+        tt(("fl", DG + 8, DG + 264, 4), run(CHOSEN), ("p0", 0, 64), A.is_gt)
+        ts(("fl", DG + 2, DG + 3), ("free", 63, 64), 0.0, A.min, -16.0, A.max)
+        gap()
+        tt(("fl", DG + 9, DG + 264, 4), run(CHOSEN), ("w0", 0, 64), A.is_gt)
         gap()
         quant("qd", "sd", 0, 130, "fl", DG)
         until(digits_ready)
-        kmm("p0", "tri", "qd", "sd", 0)
-        kmm("p1", "all", "qd", "sd", 2)
+        kmm("p1", "all", "qd", "sd", 0)
         ts(("kv", 0, 8), ("kb", 8, 16), N, A.is_gt, 4096.0, A.mult)
-        gap(1)
+        tt(run(FIRST), run(CHOSEN), ("p2", 0, 64), A.subtract)
+        tt(run(LAST), run(CHOSEN), ("p3", 0, 64), A.subtract)
+        gap()
         tt(("kv", 8, 16), ("kv", 0, 8), ("kb", 16, 24), A.add)
+        gap()
+        scan(run(RAW - 2, 66), ("one", 0, 66), ("p1", 0, 66), A.mult, A.add)
+        until(first_ready)
+        kmm("p2", "ra", "qd", "sd", 2)
         taken(N, 1)
         if t:
             taken(N, 0)
-        op("v", lambda e: e.tensor_tensor_scan(ap(run(RAW)), T.one[:, 0:64], T.p1[:, 0:64], T.p0[:, 0:1], A.mult, A.add),
-           [("one", 0, 64), ("p0", 0, 512), ("p1", 0, 512)], [run(RAW)])
-        until(first_ready)
-        kmm("p2", "ra", "qd", "sd", 2)
         ts(run(REFUSED), run(RAW), N, A.max)
         words(1, range(NV, 8))
-        if t == 0:
-            weights()
         for k in range(NV):
             ts(("wb", SEG * k, SEG * k + 64), run(RAW), ("kv", 8 + k, 9 + k), A.is_le, 2.0, A.mult)
-        gap(0 if t else 1)
+        if t == 0:
+            gap()
+            act(slot("kj"), slot("kd"), F.Identity, scale=cf(12))
         scan(("ac1", 0, SEG * NV), ("inj", 0, SEG * NV), ("wb", 0, SEG * NV), A.min, A.add, 1000.0)
         until(last_ready)
         kmm("p3", "rb", "qd", "sd", 2)
         tt(run(FIRST + 64), run(RAW), ("p2", 0, 64), A.subtract)
         words(0, range(8))
         go, stay = places(1, "w0"), places(0, "p0")
-        now(go[:2])
-        gap(2)
-        tt(run(LAST + 64), run(RAW), ("p3", 0, 64), A.subtract)
-        pump(steps, 32, "p3")
-        if t:
-            later.extend([stay[0], stay[1], stay[2], stay[4], stay[3]])
-            del stay[:5]
-        now([go[2], go[4], go[3], go[6]])
-        until(weights_ready)
-        now(go[5:6])
-        until(lists_ready)
-        now(go[7:8])
-        gap(3)
-        now(go[8:])
         gap()
+        now(go[:2])
+        last = (tt, run(LAST + 64), run(RAW), ("p3", 0, 64), A.subtract)
+        gap()
+        now([last, go[2]])
+        pump(steps, 2, "p3")
+        now([go[4], go[3], go[6], go[5]])
+        until(weights_ready)
+        later.extend([(taken, N, 0)] * (t == 0) + [stay[0], stay[1], stay[2], stay[4], stay[3], stay[6], stay[5]])
+        del stay[:7]
+        now(go[7:8])
+        gap(EARLY if t else 1)
+        now(go[8:])
+        gap(1 if t else 2)
         gather(1, "hc")
         gap()
         quant("qy%d" % t, "sy%d" % t, 0, 128, "hc", 0)
         send(t)
+        gap(7)
         if t == 0:
             act(("zz64", 0, 516), ("z1", 0, 516), F.Identity, scale=64.0)
             later.extend((quant, "zq", "zs", 128 * b, 128, "zz64", 3 - b) for b in range(4))
             order("p", [("sw", 0, 512)], [])
-            taken(N, 0)
+        if t == 1:
+            later.extend([(ts, slot("kn"), ("ct", 0, 512), cf(8), A.is_equal), (quant, "qv", "sv", 0, 128, "vb", 0), (kquant, "kn")])
         now(stay[:-1])
         gap(2)
         now(stay[-1:])
@@ -609,8 +604,7 @@ def rank_program(g, core, T, topo):
         for b in range(4):
             act(("z64", b, 512, 4), ("hk", b, 512, 4), F.Identity, scale=64.0)
             mm("w%d" % b, "qw", "sw", 128 * b, "qz", "sz", 0, 128)
-        if t > 0:
-            arrived(t, "sss-")
+        arrived(t)
         gap()
         for b in range(4):
             tt(("x64", b, 512, 4), ("w%d" % b, 0, 128), ("z64", b, 512, 4), A.add)
@@ -622,20 +616,11 @@ def rank_program(g, core, T, topo):
             mm("w0", "qu", "su", 0, "qx", "sx", 0, 128)
             later.extend(choices("w0", 0, 128))
         if t == 0:
-            gap(1)
-            pump(window(0, 128, "kept"), 32)
+            order("y", [("qz", 0, 128)], [])
             dma("y", [(T.vb[:, :], T.v[:, :])], [], [("vb", 0, 512)], "dv")
-            gap(3)
-            kquant("kn")
-            arrived(t, "svsv")
-        if t == 1:
-            later.append((quant, "qv", "sv", 0, 128, "vb", 0))
         if t == 2:
             codes_out(0)
-        if t > 0:
-            scaled(3)
-        if t == 1:
-            pump(window(0, 128, "kept"), 32, "p3")
+        ts(("xt", 515, 1024, 4), ("p0", 0, 128), 0.015625, A.mult)
         quant("qx", "sx", 128, 128, "xt", 512)
 
     for t in range(3):

@@ -6,16 +6,33 @@ NREL = 2
 PC = 128 // NREL
 F8 = "float8_e4m3fn_x4"
 BIG = 2.0 ** 90
-M32 = 1.5 * 2.0 ** 28
+M32 = 1.5 * 2.0 ** 31
 LW = 160
-BY_DMA = [6, 5, 5]
-NV = 5
-EARLY = 4
+BY_DMA = [(2, 3, 5, 6, 7), (3, 5, 6, 7), (3, 5, 6, 7)]
+BY_G = [(4,), (4,), (4,)]
+NV = 3
 SEG = 66
+OWN = 2048.0
+LESS = 256.0 + OWN
+SC, HALF = 2, 1
+MID, AHEAD_OF, BEHIND_OF = [4, 4, 4], "", ""
+KE = [0, 0, 0]
+GV = [16, 16]
+RA, RB, AB = ["p0", "p2", "p2"], ["p3", "p0", "p0"], ["p1", "p3", "p3"]
+ROUND = ("scores TURN AHEAD turn block0 BEHIND ahead behind u0 l0 u1 FLAGS flags BACK u3 u2 back count aa u4 l1 v3 ob chosen free l2 u6 marks room ab "
+         "marks2 table u5 count2 early v4 table2 floor refused ra compare u7 rb table4 l5 late sum LATE table3 LATE2 list mask first l7 high last taken low "
+         "in_word of_word numbers MASK LIST HIGH FIRST l6 offsets LAST gather LOW TAKEN cross IN_WORD OF_WORD OFFSETS")
+FIRST_ROUND = ("tot= all= scores turn block0 ct= zeros= behind ob= u2 mx0= mt= ahead qoa odd= flags turn0= aa= turn= u0 fills= kn0= back go= qtot u1 count ab= "
+               "rb0= turns= gcopy kn1= slots= kn3= qob ob wrap= chosen step= free rb1= kn2= early marks room marks2 start= column= qall count2 vfloor rb2= kw1= "
+               "vwb= qaa aa rb3= refused vwb2= kw2= qrb l1 rb compare qra kd= kj= mask= kw0= late ra sum qab l2 table3 l0 table mask list table4 ab qkd high "
+               "table2 LATE2 first kw3= u3 LATE last taken low l3 qkj in_word qkw of_word GO= offsets gather MASK cross HIGH TAKEN ZEROS= SLOTS= LIST LAST LOW "
+               "FIRST IN_WORD OF_WORD OFFSETS")
 
-KN = {n: i for i, n in enumerate(["tot", "aa", "ab", "oa", "ob", "all", "ra", "rb", "kd", "kj", "kw", "kn"])}
-REFUSED, CHOSEN, FIRST, LAST, RAW = 0, 64, 128, 256, 392
-DG, FT, FB = 768, 1032, 1288
+KN = {n: i for i, n in enumerate(["tot", "rb", "all", "oa", "ob", "aa", "ab", "kn", "kd", "kj", "kw", "ra"])}
+REFUSED, CHOSEN, FIRST, LAST, FLOOR = 8, 72, 136, 264, 392
+DG, FT, FB = 640, 1032, 1288
+CMP, DIG = (0, 384), (256, 904)
+QL, QD, QF = (256, 0), 128, 384
 
 
 def sb(n, kind="bfloat16"):
@@ -26,23 +43,22 @@ SCRATCH = {
     "ub": sb(512), "vb": sb(512), "x0": sb(1024),
     "qu": sb(128, F8), "su": sb(128, "uint8"), "qv": sb(128, F8), "sv": sb(128, "uint8"),
     "qw": sb(512, F8), "sw": sb(512, "uint8"), "qx": sb(256, F8), "sx": sb(256, "uint8"),
-    "eq": sb(4 * LW, F8), "es": sb(4 * LW, "uint8"), "zq": sb(512, F8), "zs": sb(512, "uint8"),
+    "eq": sb(4 * LW, F8), "es": sb(4 * LW, "uint8"),
     "kq": sb(128 * len(KN), F8), "kqs": sb(128 * len(KN), "uint8"), "ks": sb(512 * len(KN)),
-    "jj": sb(512), "z1": sb(1024), "zz64": sb(528), "one": sb(72),
-    "mx": sb(512), "ct": sb(512), "ct2": sb(512), "mt": sb(128), "mr": sb(256), "i16": sb(16), "zmask": sb(128),
+    "jj": sb(512), "z1": sb(1024), "one": sb(72),
+    "mx": sb(512), "ct": sb(512), "ct2": sb(512), "mt": sb(128), "mr": sb(256, "float32"), "i16": sb(16), "zmask": sb(128),
     "pc": sb(16, "int32"), "cf": sb(24, "float32"), "nk": sb(40, "float32"), "kb": sb(24, "float32"),
     "qu1": sb(128, F8), "su1": sb(128, "uint8"), "uo": sb(8, "uint16"), "go": sb(8, "uint16"),
     "rst": sb(256, "float32"), "inj": sb(SEG * NV, "float32"),
-    "st": sb(256, "float32"), "rm": sb(256, "float32"), "fl": sb(1544), "qf": sb(128, F8), "sf": sb(128, "uint8"),
-    "tt": sb(456, "float32"), "free": sb(64, "float32"), "kv": sb(16, "float32"), "m64": sb(192),
-    "qd": sb(130, F8), "sd": sb(130, "uint8"), "r16": sb(16),
-    "jk": sb(2688), "wb": sb(SEG * NV), "q2": sb(320, F8), "c2": sb(320, "uint8"), "q3": sb(256, F8), "c3": sb(256, "uint8"), "lf": sb(64, "uint16"),
+    "st": sb(260, "float32"), "rm": sb(256, "float32"), "fl": sb(1544),
+    "tt": sb(456, "float32"), "free": sb(64, "float32"), "kv": sb(16, "float32"), "m64": sb(384), "r16": sb(16),
+    "jk": sb(2688), "wb": sb(SEG * NV), "q2": sb(514, F8), "c2": sb(514, "uint8"), "q3": sb(128, F8), "c3": sb(128, "uint8"), "lf": sb(64, "uint16"),
     "win": sb(8192), "hk": sb(512), "hc": sb(512), "z64": sb(512), "x64": sb(512), "xt": sb(1024),
     "qz": sb(128, F8), "sz": sb(128, "uint8"), "yt": sb(256, "float32"),
     "omf": sb(144, "float32"),
 }
 for _h in range(2):
-    SCRATCH.update({"ac%d" % _h: sb(8 * SEG, "float32"), "li%d" % _h: sb(8, "uint16"), "wd%d" % _h: sb(24, "float32")})
+    SCRATCH.update({"ac%d" % _h: sb(8 * SEG, "float32"), "li%d" % _h: sb(8, "uint16"), "wd%d" % _h: sb(32, "float32")})
 for _t in range(3):
     SCRATCH.update({"qy%d" % _t: sb(128, F8), "sy%d" % _t: sb(128, "uint8"), "lq%d" % _t: sb(128, F8), "ls%d" % _t: sb(128, "uint8"),
                     "rq%d" % _t: sb(PC, F8), "rs%d" % _t: sb(128, "uint8")})
@@ -221,8 +237,12 @@ def rank_program(g, core, T, topo):
     def fill(r, val):
         op("v", lambda e: e.memset(ap(r), val), [], [r])
 
-    def act(out, in_, func=F.Copy, by=None, **kw):
+    def act(out, in_, func=F.Copy, by=None, scale=1.0, bias=0.0, **kw):
         src, reads = source(in_, by)
+        if scale != 1.0:
+            kw["scale"] = scale
+        if bias != 0.0:
+            kw["bias"] = bias
         reads += [kw[k] for k in ("scale", "bias") if isinstance(kw.get(k), tuple)]
         writes = [out] + ([kw["accum_out"]] if "accum_out" in kw else [])
         args = {k: ap(v) if isinstance(v, tuple) else v for k, v in kw.items()}
@@ -235,8 +255,8 @@ def rank_program(g, core, T, topo):
         kw = {} if r[0] == "pc" else {"allow_small_or_imprecise_dtypes": True}
         op("g", lambda e: e.iota(ap(r), pattern, base, cmul, **kw), [], [r])
 
-    def keep(out, in_, pattern, base, cmul):
-        op("g", lambda e: e.affine_select(ap(out), ap(in_), pattern, A.is_ge, 0.0, base, cmul), [in_], [out])
+    def keep(out, in_, pattern, base, cmul, other=0.0):
+        op("g", lambda e: e.affine_select(ap(out), ap(in_), pattern, A.is_ge, other, base, cmul), [in_], [out])
 
     def slot(name):
         return ("ks", 512 * KN[name], 512 * KN[name] + 512)
@@ -260,194 +280,183 @@ def rank_program(g, core, T, topo):
         now(later[:n])
         del later[:n]
 
-    def until(mark):
-        if (mark,) in later:
-            gap(later.index((mark,)) + 1)
-
-    def counts_ready():
-        pass
-
-    def flags_ready():
-        pass
-
-    def marks_ready():
-        pass
-
-    def first_ready():
-        pass
-
-    def last_ready():
-        pass
-
-    def digits_ready():
-        pass
-
-    def weights_ready():
-        pass
-
     dma("s", [(T.ub[:, :], T.u[:, :])], [], [("ub", 0, 512)], "du")
     dma("y", [(T.x0[:, :], T.x[:, :])], [], [("x0", 0, 1024)], "dx")
 
     iota(pc(0), [[0, 1]], 0, 1)
-    iota(("r16", 0, 16), [[1, 16]], 0, 0)
-    iota(("jj", 0, 512), [[1, 512]], 0, -4)
-    iota(("i16", 0, 16), [[16, 16]], 0, 0)
-    iota(("m64", 0, 64), [[1, 16], [-8, 4]], 0, 0)
-    fill(("one", 0, 72), 1.0)
-    fill(("fl", DG, DG + 264), 0.0)
+    iota(("jj", 0, 128), [[1, 128]], 0, 0)
+    fill(("m64", 0, 64), -OWN)
+    keep(("m64", 64, 128), ("m64", 0, 64), [[-16, 16], [128, 4]], 0, 1)
+    keep(("m64", 128, 192), ("m64", 64, 128), [[16, 16], [-128, 4]], 15, -1, 1.0)
+    fill(("z1", 0, 4 * LW + 4), 0.0)
     ts(pc(1), pc(0), 15, A.bitwise_and)
     ts(pc(2), pc(0), 4, A.arith_shift_right)
     ts(pc(3), pc(0), 3, A.bitwise_and)
     ts(pc(4), pc(0), 2, A.arith_shift_right, 3, A.bitwise_and)
-    ts(pc(5), pc(0), 7, A.bitwise_and)
-    fill(("fl", FB + 248, FB + 256), 0.0)
+    ts(pc(5), pc(0), 1, A.arith_shift_right, 7, A.bitwise_and)
+    fill(("one", 0, 72), 1.0)
     copy(("cf", 0, 6), ("pc", 0, 6))
     fill(("rst", 0, 128), BIG)
-    ts(("nk", 0, 16), ("r16", 0, 16), cf(1), A.is_equal)
-    ts(("nk", 16, 24), ("r16", 0, 8), -1.0, A.add, cf(1), A.is_equal)
-    fill(("rst", 0, 128, 16), -BIG)
-    tt(("nk", 24, 32), ("nk", 0, 8), ("nk", 16, 24), A.subtract)
-    ts(pc(6), pc(0), cf(2), A.subtract)
-    ts(pc(7), pc(2), -1.0, A.mult, 8.0, A.add)
-    ts(("uo", 0, 8), ("i16", 0, 8), cf(5), A.add)
-    ts(("z1", 0, 512), ("jj", 0, 512), 3.0, A.is_equal)
-    ts(("z1", 512, 4 * LW + 4), ("jj", 0, 4 * LW + 4 - 512), 3.0, A.is_equal)
+    ts(("nk", 0, 18), ("jj", 0, 18), -2.0, A.add, cf(1), A.is_equal)
+    ts(("z1", 3, 512, 4), ("jj", 0, 128), cf(0), A.is_equal, 64.0, A.mult)
+    ts(("z1", 515, 4 * LW + 4, 4), ("jj", 0, LW - 127), cf(0), A.is_equal, 64.0, A.mult)
+    tt(("nk", 24, 32), ("nk", 2, 18, 2), ("nk", 0, 16, 2), A.subtract)
     quant("qu1", "su1", 0, 128, "ub", 0)
+    ts(("uo", 0, 8), ("jj", 0, 8), 16.0, A.mult, cf(5), A.add)
     unpacking = [(quant, "eq", "es", LW * b, LW, "z1", 3 - b) for b in range(4)]
     now(unpacking[:1])
-    act(cf(8), cf(2), F.Identity, scale=4.0)
-    act(cf(16), cf(1), F.Identity, scale=16.0, bias=-256.0)
-    act(cf(6), cf(1), F.Identity, bias=0.5 - 256.0)
-    act(cf(7), cf(3), F.Identity, bias=1024.0)
-    act(cf(10), cf(3), F.Identity, bias=cf(8))
-
-    def by_group(name, pattern, first=32):
-        a = slot(name)[1]
-        for c in range(8):
-            act(("ks", a + 64 * c, a + 64 * c + 64), pattern, F.Identity, scale=("nk", first + c, first + c + 1))
-
-    by_group("tot", ("one", 0, 64), 24)
     op("v", lambda e: e.tensor_copy(T.qu[:, 0:128].bitcast(dt.uint32), T.qu1[:, 0:128].bitcast(dt.uint32).indirect(T.uo[:, 0:8])),
        [("qu1", 0, 128), ("uo", 0, 8)], [("qu", 0, 128)])
+    act(cf(6), cf(1), F.Identity, bias=0.5 - LESS)
+    act(cf(8), cf(2), F.Identity, scale=4.0)
+    act(cf(16), cf(1), F.Identity, scale=16.0, bias=-256.0)
+    act(("kb", 0, 16), ("jj", 0, 16), F.Identity, scale=16.0, bias=cf(6))
+
+    def by_group(name, pattern, groups=range(8)):
+        a = slot(name)[1]
+        for c in groups:
+            act(("ks", a + 64 * c, a + 64 * c + 64), pattern, F.Identity, scale=("nk", 24 + c, 25 + c))
+
+    by_group("oa", ("m64", 128, 192), range(2))
     op("s", lambda e: e.activation(T.su[:, 0:128], T.su1[:, 0:128].indirect(T.uo[:, 0:8]), F.Copy), [("qu1", 0, 128), ("uo", 0, 8)], [("su", 0, 128)])
-    ts(("nk", 32, 40), ("nk", 24, 32), ("nk", 7, 8), A.subtract, -4096.0, A.mult)
-    ts(("m64", 64, 128), ("m64", 0, 64), cf(2), A.is_equal)
-    quant("qx", "sx", 0, 256, "x0", 0)
-    ts(("m64", 128, 192), ("m64", 0, 64), 16.0, A.add, cf(2), A.is_equal)
-    ts(("pc", 8, 10), ("pc", 6, 8), 7, A.bitwise_and)
-    act(("rst", 128, 256), ("rst", 0, 128))
-    by_group("oa", ("m64", 64, 128))
-    iota(("ct2", 0, 512), [[1, 32], [0, 16]], 0, 0)
-    for name, first in (("aa", 0), ("ab", 16)):
-        keep(slot(name), slot("tot"), [[0, 8], [-16, 16], [128, 4]], -16 * (first + 1), 1)
-    iota(("mx", 0, 512), [[0, 8], [1, 16], [-100, 4]], 0, 0)
-    iota(("ct", 0, 512), [[1, 32], [0, 4], [-1, 4]], 0, 0)
-    iota(("mr", 0, 256), [[1, 256]], -256, 0)
-    iota(("mt", 0, 128), [[0, 8], [1, 4], [0, 4]], 0, 0)
     order("p", [("su", 0, 128)], [])
+    by_group("oa", ("m64", 128, 192), range(2, 8))
+    quant("qx", "sx", 0, 256, "x0", 0)
+    fill(("rst", 0, 128, 8), -BIG)
+    now(unpacking[1:])
+
+    def behind(name, first):
+        keep(slot(name), slot("tot"), [[0, 8], [-16, 16], [128, 4]], -16 * (first + 1), 1)
+
     dma("y", [(T.qw[:, :].bitcast(dt.uint8), T.wc[:, :])], [], [("qw", 0, 512)], "dwc")
     dma("y", [(T.sw[:, :], T.ws[:, :])], [], [("sw", 0, 512)], "dws")
 
-    later += unpacking[1:] + [
-        (kquant, "tot"),
-        (ts, slot("kw"), ("ct2", 0, 512), cf(10), A.is_equal, 8.0, A.mult),
-        (kquant, "aa"), (kquant, "oa"), (counts_ready,), (kquant, "ab"), (flags_ready,),
-        (kquant, "kw"),
-        (ts, cf(11), pc(8), 7.0, A.is_equal, -8192.0, A.mult),
-        (ts, cf(15), cf(3), 2.0, A.min, 8.0, A.mult),
-        (kquant, "ob"), (marks_ready,),
-        (ts, ("ks", slot("all")[1] + 2, slot("all")[2], 4), ("ct2", 2, 512, 4), cf(8), A.is_ge),
-        (kquant, "all"), (digits_ready,),
-        (ts, slot("ra"), ("mx", 0, 512), cf(1), A.is_lt),
-        (ts, slot("rb"), ("mx", 0, 512), 100.0, A.add, cf(1), A.is_lt),
-        (kquant, "ra"), (kquant, "rb"), (first_ready,),
-        (ts, slot("kd"), ("ct", 0, 512), cf(8), A.is_equal, cf(13), A.mult),
-        (ts, ("go", 0, 8), ("r16", 0, 8), cf(15), A.add), (last_ready,),
-        (ts, ("zmask", 0, 128), ("mt", 0, 128), cf(4), A.is_equal),
-        (kquant, "kd"),
-        (ts, cf(14), pc(9), 1024.0, A.mult, cf(7), A.add),
-        (kquant, "kj"), (weights_ready,)]
+    def turned(k):
+        return [(T.win[0:128 - 16 * k, 1024 * k:1024 * k + 1024], T.win[16 * k:128, 0:1024]),
+                (T.win[128 - 16 * k:128, 1024 * k:1024 * k + 1024], T.win[0:16 * k, 0:1024])]
+
+    def g_copies(t):
+        order("g", [slot("ab")], [])
+        for k in BY_G[t]:
+            for i, (out, in_) in enumerate(turned(k)[:2 if t else 1]):
+                op("g", lambda e: e.affine_select(out, in_, [[0, 1024]], A.is_ge, 0.0, 0, 0), [("win", 0, 1024)],
+                   [("win", 1024 * k + 512 * i, 1024 * k + 512 * i + 512)])
 
     def fills():
-        by_group("ob", ("m64", 128, 192))
-        sfill(slot("all"), 1.0)
-        act(("kb", 0, 16), ("i16", 0, 16), F.Identity, bias=cf(6))
         sfill(("inj", 0, SEG * NV), BIG)
-        act(("kb", 16, 24), ("kb", 8, 16), F.Identity, bias=-4096.0)
-        act(cf(9), ("nk", 7, 8), F.Identity, bias=("nk", 15, 16))
+        sfill(("ac1", SEG * NV, SEG * 8), 0.0)
 
-    def more_fills():
-        act(cf(13), cf(11), F.Identity, bias=1024.0)
-        act(cf(17), cf(11), F.Identity, scale=(1 / 1792 + 1 / 256) / 8192, bias=1 / 256)
-        iota(("wb", 64, SEG * NV, SEG), [[0, NV]], -64, 0)
-        iota(("wb", 65, SEG * NV, SEG), [[0, NV]], 1000, 0)
+    def slots(h):
+        act(("mr", 128 * h, 128 * h + 128), ("jj", 0, 128), F.Identity, bias=128.0 * h - LESS)
 
-    def window(copied):
-        def step(d, b, name):
-            mm(name, "eq", "es", LW * b + 16 * d, "qx", "sx", 0, 256)
-            act(("win", 1024 * d + b, 1024 * d + 1024, 4), (name, 0, 256))
-            if d == 0 and b == 3:
-                pairs = []
-                for k in range(8 - copied, 8):
-                    pairs.append((T.win[0:128 - 16 * k, 1024 * k:1024 * k + 1024], T.win[16 * k:128, 0:1024]))
-                    pairs.append((T.win[128 - 16 * k:128, 1024 * k:1024 * k + 1024], T.win[0:16 * k, 0:1024]))
-                dma("y", pairs, [("win", 0, 1024)], [("win", 1024 * (8 - copied), 8192)], "turn")
-        return [(step, d, b) for d in range(8 - copied) for b in range(4)]
+    made = {
+        "odd=": (fill, ("fl", FB + 1, FB + 256, 2), 0.0),
+        "zeros=": (fill, ("fl", DG, FT), 0.0),
+        "ZEROS=": (fill, ("fl", DIG[0] + 3, DIG[0] + 128, 4), 0.0),
+        "turn=": (ts, pc(6), pc(0), cf(2), A.subtract),
+        "turn0=": (ts, pc(7), pc(2), -1.0, A.mult, 8.0, A.add),
+        "turns=": (ts, ("pc", 8, 10), ("pc", 6, 8), 7, A.bitwise_and),
+        "wrap=": (ts, cf(11), pc(8), 7.0, A.is_equal, -8192.0, A.mult),
+        "step=": (act, cf(13), cf(11), F.Identity, None, 1.0, 1024.0),
+        "column=": (ts, cf(12), ("nk", 9, 10), ("nk", 17, 18), A.add, 4.0, A.mult),
+        "start=": (ts, cf(14), pc(9), 1024.0, A.mult, cf(3), A.add),
+        "go=": (ts, ("go", 2, 4), ("jj", 0, 8, 4), cf(4), A.add, float(SEG), A.mult),
+        "GO=": (ts, ("go", 0, 2), ("jj", 0, 8, 4), cf(4), A.add),
+        "mask=": (ts, ("zmask", 0, 32), ("mt", 0, 32), cf(4), A.is_equal, 8.0, A.mult),
+        "rb=": (ts, slot("rb"), ("mx", 0, 512), cf(1), A.is_lt),
+        "rb0=": (ts, ("ks", slot("rb")[1], slot("rb")[1] + 64), ("mx", 0, 64), cf(1), A.is_lt),
+        "mx0=": (iota, ("mx", 0, 64), [[1, 16], [-100, 4]], 100, 0),
+        "kd=": (act, slot("kd"), slot("kn"), F.Identity, None, cf(13)), "kj=": (act, slot("kj"), slot("kn"), F.Identity, None, cf(12)),
+        "fills=": (fills,), "slots=": (slots, 1), "SLOTS=": (slots, 0),
+        "ob=": (keep, slot("ob"), ("ks", slot("oa")[1] - 2, slot("oa")[2] - 2), [[0, 128], [1, 4]], -2, 0),
+        "tot=": (by_group, "tot", ("one", 0, 64)), "aa=": (behind, "aa", 0), "ab=": (behind, "ab", 16),
+        "ct=": (iota, ("ct", 0, 128), [[1, 32], [0, 4]], 0, 0), "mt=": (iota, ("mt", 0, 32), [[0, 8], [1, 4]], 0, 0),
+        "wb=": (now, [(iota, ("wb", 64, SEG * NV, SEG), [[0, NV]], -64, 0), (iota, ("wb", 65, SEG * NV, SEG), [[0, NV]], 1000, 0)]),
+        "vwb=": (fill, ("wb", 64, SEG * NV, SEG), -64.0), "vwb2=": (fill, ("wb", 65, SEG * NV, SEG), 1000.0),
+        "all=": (keep, slot("all"), ("z1", 1, 513), [[16, 8], [0, 16], [128, 4]], 15 - 384, -1, -1.0),
+        "mx=": (iota, ("mx", 0, 512), [[0, 8], [1, 16], [-100, 4]], 100, 0), "gcopy": (g_copies, 0),
+    }
+    for i in range(3):
+        a = slot("rb")[1]
+        made["rb%d=" % (i + 1)] = (copy, ("ks", a + (64 << i), a + (128 << i)), ("ks", a, a + (64 << i)))
+    for b in range(4):
+        made["kw%d=" % b] = (ts, ("ks", slot("kw")[1] + b, slot("kw")[2], 4), ("ct", 0, 128), cf(3), A.subtract, cf(8), A.is_equal)
+        made["kn%d=" % b] = (ts, ("ks", slot("kn")[1] + b, slot("kn")[2], 4), ("ct", 0, 128), -float(b), A.add, cf(8), A.is_equal)
+    made.update({"q" + name: (kquant, name) for name in KN})
+    made["qra"] = (quant, "kq", "kqs", 128 * KN["ra"], 128, "ks", 512 * KN["rb"] + 1)
 
-    def pump(steps, n, last="w0"):
-        for step, d, b in steps[:n]:
-            step(d, b, ("w3", "w2", "w1", last)[b])
-        del steps[:n]
+    def unpack(d, b, name, a=0, n=256):
+        mm(name, "eq", "es", LW * b + 16 * d, "qx", "sx", a, n)
+
+    def lay(d, b, name, a=0, n=256):
+        act(("win", 1024 * d + 4 * a + b, 1024 * d + 4 * (a + n), 4), (name, 0, n), F.Identity, scale=0.015625)
+
+    def copies(t):
+        rest = [] if t else BY_G[t]
+        dma("y", [pair for k in BY_DMA[t] for pair in turned(k)] + [turned(k)[1] for k in rest], [("win", 0, 1024)],
+            [("win", 1024 * k, 1024 * k + 1024) for k in BY_DMA[t]] + [("win", 1024 * k + 512, 1024 * k + 1024) for k in rest], "turn")
+        if t:
+            g_copies(t)
 
     def choices(name, a, n):
+        ahead, behind = ("rm", a, a + n // 2), ("rm", a + n // 2, a + n)
+
+        def backwards():
+            op("v", lambda e: e.tensor_tensor_scan(T.rm[:, a + n - 1:a + n // 2 - 1:-1], T.rst[:, 0:n // 2], T.st[:, a + n - 2:a - 2 if a else None:-2],
+                                                   0.0, A.min, A.max), [("rst", 0, n // 2), ("st", a, a + n)], [behind])
         return [(turn, ("st", a, a + n), (name, 0, n)),
-                (scan, ("rm", a, a + n), ("rst", 0, n), ("st", a, a + n), A.min, A.max),
-                (tt, ("fl", FB + a, FB + a + n - 8), ("rm", a, a + n - 8), ("rm", a + 8, a + n), A.is_ge),
+                (scan, ahead, ("rst", 0, n // 2), ("st", a, a + n, 2), A.min, A.max), (backwards,),
+                (tt, ("fl", FB + a, FB + a + n, 2), ahead, behind, A.is_ge),
                 (turn, ("fl", FT + a, FT + a + n), ("fl", FB + a, FB + a + n))]
 
     def signs(h, k, first, n, junk, total):
         act(("jk", junk, junk + n), run(first, n), F.Sign, bias=("kb", 8 * h + k, 8 * h + k + 1), scale=-1.0, accum_out=total)
 
-    def words(h, ks):
-        for k in ks:
-            signs(h, k, 0, 128, 1024 * h + 128 * k, ("ac%d" % h, SEG * k + 64, SEG * k + 65))
+    def digits(h):
+        return ("q3", "c3", 0) if h else ("q2", "c2", QL[0] + 64)
 
     def places(h, out):
-        li, wd, at = "li%d" % h, "wd%d" % h, 384 * h
-        acc, k = ("ac%d" % h, 64, 8 * SEG, SEG), ("mr", 128 * h, 128 * h + 128)
+        li, wd, at = "li%d" % h, ("wd%d" % h, 0, 32), CMP[h]
+        acc, k = ("ac1", 64, 8 * SEG, SEG) if h else ("ac0", 16, 24), ("mr", 128 * h, 128 * h + 128)
+
+        def digit(b):
+            return ("fl", DIG[h] + b, DIG[h] + 128, 4)
 
         def in_word():
-            quant("q2", "c2", 160 * h, 160, "fl", at + 128)
-            for b in (0, 32):
-                kmm(out, "kd", "q2", "c2", 160 * h + b, 128, b == 0, False)
+            quant("q2", "c2", QL[h], 128, "fl", at)
+            for name in ("kd", "kj"):
+                for b in (0, 32):
+                    kmm(out, name, "q2", "c2", QL[h] + b, 128, (name, b) == ("kd", 0), False)
 
         def of_word():
-            quant("q3", "c3", 128 * h, 128, "fl", at)
-            for b in (0, 32):
-                kmm(out, "kj", "q2", "c2", 160 * h + b, 128, False, False)
-            kmm(out, "kw", "q3", "c3", 128 * h, 128, False, True)
-        return [(ts, (li, 0, 8), acc, 0.5, A.mult, 64.0, A.add),
-                (ts, (wd, 0, 8), acc, M32, A.add, -M32, A.add),
-                (tt, ("fl", at + 128, at + 256), run(FIRST, 128), k, A.is_le, (li, 0, 8)),
-                (tt, ("fl", at + 256, at + 384), run(LAST, 128), k, A.is_le, (li, 0, 8)),
-                (tt, (wd, 8, 16), acc, (wd, 0, 8), A.subtract),
-                (in_word,),
-                (tt, ("fl", at, at + 128), (wd, 0, 24), ("zmask", 0, 128), A.mult, ("go", 0, 8)),
-                (of_word,),
-                (ts, ("lf", 32 * h, 32 * h + 32), (out, 0, 32), cf(14), A.add)]
+            if h:
+                quant("q3", "c3", 0, 128, "fl", DIG[h])
+            kmm(out, "kw", *digits(h), 128, False, True)
+        return {"list": (ts, (li, 0, 8), acc, 0.5, A.mult, 64.0, A.add),
+                "mask": (tt, wd, acc[:3], ("zmask", 0, 32), A.mult, ("go", 2 * h, 2 * h + 2)),
+                "high": (ts, digit(0), wd, M32, A.add, -M32, A.add),
+                "low": (tt, digit(1), wd, digit(0), A.subtract),
+                "taken": (ts, digit(2), wd, 0.0, A.is_gt, -1024.0, A.mult),
+                "first": (tt, ("fl", at, at + 128), run(FIRST, 128), k, A.is_le, (li, 0, 8)),
+                "last": (tt, ("fl", at + 128, at + 256), run(LAST, 128), k, A.is_le, (li, 0, 8)),
+                "in_word": (in_word,), "of_word": (of_word,),
+                "offsets": (ts, ("lf", 32 * h, 32 * h + 32), (out, 0, 32), cf(14), A.add, 1024.0, A.add)}
 
     def gather(h, dst):
-        act((dst, 256, 512), ("win", 0, 8192), by=("lf", 32 * h + 16, 32 * h + 32))
-        copy((dst, 0, 256), ("win", 0, 8192), by=("lf", 32 * h, 32 * h + 16))
+        k = GV[h]
+        act((dst, 16 * k, 512), ("win", 0, 8192), by=("lf", 32 * h + k, 32 * h + 32))
+        copy((dst, 0, 16 * k), ("win", 0, 8192), by=("lf", 32 * h, 32 * h + k))
 
-    def numbers():
+    def numbers(h):
+        name = "p%d" % (1 + h)
+        kmm(name, "kn", "q2", "c2", QL[h], 128, True, False)
+        kmm(name, "kn", "q2", "c2", QL[h] + 32, 128, False, False)
+        for i in range(2):
+            kmm(name, "kw", *digits(h), 128, False, i == 1)
+
+    def numbers_laid():
         for h in range(2):
-            name = "p%d" % (1 + h)
-            kmm(name, "kn", "q2", "c2", 160 * h, 128, True, False)
-            kmm(name, "kn", "q2", "c2", 160 * h + 32, 128, False, False)
-            for i in range(2):
-                kmm(name, "kw", "q3", "c3", 128 * h, 128, False, i == 1)
-            act(("omf", 32 * h, 32 * h + 32), (name, 0, 32), F.Identity, bias=2048.0)
+            act(("omf", 32 * h, 32 * h + 32), ("p%d" % (1 + h), 0, 32), F.Identity, bias=2048.0)
         return [(turn, ("omf", 64, 128), ("omf", 0, 64)), (numbers_out,)]
 
     def numbers_out():
@@ -462,8 +471,8 @@ def rank_program(g, core, T, topo):
     def product_out(h):
         a, name = 128 * h, "w%d" % h
         mm(name, "qv", "sv", 0, "qx", "sx", a, 128)
-        copy(("yt", a, a + 128), (name, 0, 128))
-        dma("y", [(T.y[:, a:a + 128], T.yt[:, a:a + 128])], [("yt", a, a + 128)], [], "dst")
+        (copy if h else act)(("yt", a, a + 128), (name, 0, 128))
+        dma("y" if h else "s", [(T.y[:, a:a + 128], T.yt[:, a:a + 128])], [("yt", a, a + 128)], [], "dst")
 
     def send(t):
         qy, sy = "qy%d" % t, "sy%d" % t
@@ -482,152 +491,136 @@ def rank_program(g, core, T, topo):
         g.remote_dma(out_ap=T["rs%d" % t][:, 0:128], in_ap=T[sy][:, 0:128], remote_sem=T.sem["in%d" % t], local_sem=T.sem.loc,
                      pid=pid, routing_id=rid, dma_engine_mask=topo.mask(core, rel[NREL]))
 
-    def arrived(t):
+    def arrived(t, bs):
         lq, ls = "lq%d" % t, "ls%d" % t
-        arrive("arr%d" % t, sum(len(topo.engines(c, core)) for c in relays(topo, T.cores[rank ^ XOR[t]], core)), [(lq, 0, 128)])
-        for b in range(4):
+        for b in bs:
             name = "p%d" % (3 - b)
             mm(name, "qw", "sw", 128 * b, lq, ls, 0, 128, True, False)
-            mm(name, "zq", "zs", 128 * b, lq, ls, 0, 128, False, True)
+            mm(name, "eq", "es", LW * b, lq, ls, 0, 128, False, True)
             if b < 3:
                 act(("xt", 512 + b, 1024, 4), (name, 0, 128), F.Identity, scale=0.015625)
 
-    def taken(N, h):
-        ts(("wd%d" % h, 16, 24), ("kb", 8 * h, 8 * h + 8), N, A.is_gt, -64.0, A.mult)
-
     def one_round(t):
         a, n = (0, 256) if t == 0 else (128, 128)
-        mm("p0", "qu", "su", 0, "qx", "sx", a, n)
-        steps = window(BY_DMA[t])
-        gap(1 if t else 2)
-        calls = choices("p0", a, n)
+
+        def block0():
+            for b in range(4):
+                unpack(0, b, "w%d" % (3 - b), *((a, n) if HALF else (0, 256)))
+                lay(0, b, "w%d" % (3 - b), *((a, n) if HALF else (0, 256)))
+            copies(t)
+
+        def count():
+            quant("q2", "c2", QF, 128, "fl", FT)
+            kmm("p1", "tot", "q2", "c2", QF)
+            kmm("p0", "oa", "q2", "c2", QF)
+
+        def count2():
+            quant("q2", "c2", QD, 128, "fl", DG)
+            kmm("p1", "all", "q2", "c2", QD)
+
+        def refused():
+            op("v", lambda e: e.tensor_tensor_scan(T.tt[:, REFUSED + 63:REFUSED - 1:-1], T.p1[:, 64:0:-1], ap(run(FLOOR)), -OWN, A.add, A.max),
+               [bank(("p1",)), run(FLOOR)], [run(REFUSED)])
+
+        early = KE[t]
+
+        def kept_late(k):
+            if k < early:
+                return (signs, 0, k, REFUSED, 64, 128 * k, ("ac0", 8 + k, 9 + k))
+            return (signs, 0, k, REFUSED, 128, 128 * k, ("ac0", 16 + k, 17 + k))
+
+        def cross():
+            quant("qy%d" % t, "sy%d" % t, 0, 128, "hc", 0)
+            send(t)
+
+        def table(a, counts, name):
+            return (tt, run(a), run(counts), (name, 0, 64), A.subtract)
+
+        steps = dict(made)
+        steps.update(places(1, "w0"))
+        steps.update({k.upper(): v for k, v in places(0, "p0").items()})
+        steps.update(zip(["turn", "ahead", "behind", "flags", "back"], choices("p0", a, n)))
+        steps.update(zip(["TURN", "AHEAD", "BEHIND", "FLAGS", "BACK"], choices("w0", 0, 128)))
+        for i, name in enumerate(["w3", "w2", "w1", "p3"] * 2 if t else ["w3", "w2", "w1"] * 3):
+            steps.update({"u%d" % i: (unpack, 1 + i // 4, i % 4, name), "l%d" % i: (lay, 1 + i // 4, i % 4, name),
+                          "v%d" % i: (ts, ("win", 1024 * (1 + i // 4) + i % 4, 1024 * (2 + i // 4), 4), (name, 0, 256), 0.015625, A.mult)})
+        steps.update({
+            "scores": (mm, "p0", "qu", "su", 0, "qx", "sx", a, n), "block0": (block0,), "count": (count,), "count2": (count2,),
+            "ob": (kmm, "w0", "ob", "q2", "c2", QF), "aa": (kmm, "p2", "aa", "q2", "c2", QF), "ab": (kmm, AB[t], "ab", "q2", "c2", QF),
+            "ra": (kmm, RA[t], "ra", "q2", "c2", QD), "rb": (kmm, RB[t], "rb", "q2", "c2", QD),
+            "chosen": (scan, run(CHOSEN), ("one", 0, 64), ("p1", 0, 64), A.mult, A.add, -LESS),
+            "marks": (tt, ("fl", DG, DG + 256, 4), run(CHOSEN), ("p0", 0, 64), A.is_gt),
+            "marks2": (tt, ("fl", DG + 1, DG + 256, 4), run(CHOSEN), ("w0", 0, 64), A.is_gt),
+            "free": (scan, ("free", 0, 64), ("one", 0, 64), ("p1", 0, 64), A.mult, A.add, cf(16)),
+            "room": (ts, ("fl", DG + 259, DG + 260), ("free", 63, 64), 0.0, A.min, -16.0, A.max),
+            "vfloor": (ts, run(FLOOR), ("one", 0, 64), run(CHOSEN + 63, 1), A.mult),
+            "floor": (act, run(FLOOR), ("one", 0, 64), F.Identity, None, run(CHOSEN + 63, 1)), "refused": (refused,),
+            "table": table(FIRST, CHOSEN, "p2"), "table2": table(LAST, CHOSEN, AB[t]),
+            "table3": table(FIRST + 64, REFUSED, RA[t]), "table4": table(LAST + 64, REFUSED, RB[t]),
+            "early": (now, [(signs, 1, k, CHOSEN, 64, 2048 + 64 * k, ("inj", SEG * k, SEG * k + 1)) for k in range(NV)]),
+            "late": (now, [(signs, 1, k, REFUSED, 128, 1024 + 128 * k, ("ac1", SEG * k + 64, SEG * k + 65)) for k in range(NV, 8)]),
+            "compare": (now, [(ts, ("wb", SEG * k, SEG * k + 64), run(REFUSED), ("kb", 8 + k, 9 + k), A.is_le, 2.0, A.mult) for k in range(NV)]),
+            "sum": (scan, ("ac1", 0, SEG * NV), ("inj", 0, SEG * NV), ("wb", 0, SEG * NV), A.min, A.add, 1000.0),
+            "EARLY": (now, [(signs, 0, k, CHOSEN, 64, 128 * k + 64, ("ac0", k, k + 1)) for k in range(early)]),
+            "LATE": (now, [kept_late(k) for k in range(4)]), "LATE2": (now, [kept_late(k) for k in range(4, 8)]),
+            "SUM": (tt, ("ac0", 16, 16 + early), ("ac0", 0, early), ("ac0", 8, 8 + early), A.add) if early else (now, []),
+            "gather": (gather, 1, "hc"), "cross": (cross,), "numbers": (numbers, 1) if t == 2 else (now, [])})
+        now([steps[k] for k in (ROUND if t else FIRST_ROUND).split()])
         if t == 0:
-            now(calls[:1])
-            del calls[:1]
-            gap(2)
-        pump(steps, 4)
-        pump(steps, 4 if t else 0, "p3")
-        if t == 0:
-            fills()
-        for call in calls:
-            now([call])
-            gap()
-        quant("qf", "sf", 0, 128, "fl", FT)
-        until(counts_ready)
-        kmm("p1", "tot", "qf", "sf", 0)
-        kmm("p0", "aa", "qf", "sf", 0, 128, True, False)
-        kmm("p0", "oa", "qf", "sf", 0, 128, False, True)
-        until(flags_ready)
-        kmm("w0", "ab", "qf", "sf", 0, 128, True, False)
-        gap(4)
-        N = run(CHOSEN + 63, 1)
-        scan(run(CHOSEN), ("one", 0, 64), ("p1", 0, 64), A.mult, A.add, -256.0)
-        until(marks_ready)
-        kmm("w0", "ob", "qf", "sf", 0, 128, False, True)
-        kmm("p2", "aa", "qf", "sf", 0)
-        kmm("p3", "ab", "qf", "sf", 0)
-        scan(("free", 0, 64), ("one", 0, 64), ("p1", 0, 64), A.mult, A.add, cf(16))
-        for k in range(NV):
-            signs(1, k, CHOSEN, 64, 2048 + 64 * k, ("inj", SEG * k, SEG * k + 1))
-        if t == 0:
-            more_fills()
-        pump(steps, 2)
-        if t == 0:
-            act(cf(12), cf(17), F.Identity, scale=cf(9))
-        tt(("fl", DG + 8, DG + 264, 4), run(CHOSEN), ("p0", 0, 64), A.is_gt)
-        ts(("fl", DG + 2, DG + 3), ("free", 63, 64), 0.0, A.min, -16.0, A.max)
-        gap()
-        tt(("fl", DG + 9, DG + 264, 4), run(CHOSEN), ("w0", 0, 64), A.is_gt)
-        gap()
-        quant("qd", "sd", 0, 130, "fl", DG)
-        until(digits_ready)
-        kmm("p1", "all", "qd", "sd", 0)
-        ts(("kv", 0, 8), ("kb", 8, 16), N, A.is_gt, 4096.0, A.mult)
-        tt(run(FIRST), run(CHOSEN), ("p2", 0, 64), A.subtract)
-        tt(run(LAST), run(CHOSEN), ("p3", 0, 64), A.subtract)
-        gap()
-        tt(("kv", 8, 16), ("kv", 0, 8), ("kb", 16, 24), A.add)
-        gap()
-        scan(run(RAW - 2, 66), ("one", 0, 66), ("p1", 0, 66), A.mult, A.add)
-        until(first_ready)
-        kmm("p2", "ra", "qd", "sd", 2)
-        taken(N, 1)
-        if t:
-            taken(N, 0)
-        ts(run(REFUSED), run(RAW), N, A.max)
-        words(1, range(NV, 8))
-        for k in range(NV):
-            ts(("wb", SEG * k, SEG * k + 64), run(RAW), ("kv", 8 + k, 9 + k), A.is_le, 2.0, A.mult)
-        if t == 0:
-            gap()
-            act(slot("kj"), slot("kd"), F.Identity, scale=cf(12))
-        scan(("ac1", 0, SEG * NV), ("inj", 0, SEG * NV), ("wb", 0, SEG * NV), A.min, A.add, 1000.0)
-        until(last_ready)
-        kmm("p3", "rb", "qd", "sd", 2)
-        tt(run(FIRST + 64), run(RAW), ("p2", 0, 64), A.subtract)
-        words(0, range(8))
-        go, stay = places(1, "w0"), places(0, "p0")
-        gap()
-        now(go[:2])
-        last = (tt, run(LAST + 64), run(RAW), ("p3", 0, 64), A.subtract)
-        gap()
-        now([last, go[2]])
-        pump(steps, 2, "p3")
-        now([go[4], go[3], go[6], go[5]])
-        until(weights_ready)
-        later.extend([(taken, N, 0)] * (t == 0) + [stay[0], stay[1], stay[2], stay[4], stay[3], stay[6], stay[5]])
-        del stay[:7]
-        now(go[7:8])
-        gap(EARLY if t else 1)
-        now(go[8:])
-        gap(1 if t else 2)
-        gather(1, "hc")
-        gap()
-        quant("qy%d" % t, "sy%d" % t, 0, 128, "hc", 0)
-        send(t)
-        gap(7)
-        if t == 0:
-            act(("zz64", 0, 516), ("z1", 0, 516), F.Identity, scale=64.0)
-            later.extend((quant, "zq", "zs", 128 * b, 128, "zz64", 3 - b) for b in range(4))
             order("p", [("sw", 0, 512)], [])
         if t == 1:
-            later.extend([(ts, slot("kn"), ("ct", 0, 512), cf(8), A.is_equal), (quant, "qv", "sv", 0, 128, "vb", 0), (kquant, "kn")])
-        now(stay[:-1])
-        gap(2)
-        now(stay[-1:])
+            later.extend([(quant, "qv", "sv", 0, 128, "vb", 0), (kquant, "kn")])
+        if t == 2:
+            numbers(0)
         gap()
         gather(0, "hk")
-        gap(2)
-        quant("qz", "sz", 0, 128, "hk", 0)
+        gap()
         if t == 2:
-            later.extend(numbers())
+            later.extend(numbers_laid())
+        quant("qz", "sz", 0, 128, "hk", 0)
+        gap()
         for b in range(4):
             act(("z64", b, 512, 4), ("hk", b, 512, 4), F.Identity, scale=64.0)
             mm("w%d" % b, "qw", "sw", 128 * b, "qz", "sz", 0, 128)
-        arrived(t)
+        arrive("arr%d" % t, sum(len(topo.engines(c, core)) for c in relays(topo, T.cores[rank ^ XOR[t]], core)), [("lq%d" % t, 0, 128)])
         gap()
         for b in range(4):
             tt(("x64", b, 512, 4), ("w%d" % b, 0, 128), ("z64", b, 512, 4), A.add)
+            if SC == 1:
+                act(("xt", b, 512, 4), ("x64", b, 512, 4), F.Identity, scale=0.015625)
         gap()
-        ts(("xt", 0, 512), ("x64", 0, 512), 0.015625, A.mult)
-        gap()
+        if SC == 0:
+            ts(("xt", 0, 512), ("x64", 0, 512), 0.015625, A.mult)
+        if SC == 2:
+            for b in range(4):
+                ts(("xt", b, 512, 4), ("x64", b, 512, 4), 0.015625, A.mult)
+        last_bank = (ts, ("xt", 515, 1024, 4), ("p0", 0, 128), 0.015625, A.mult)
         quant("qx", "sx", 0, 128, "xt", 0)
+        mid = MID[t]
+        arrived(t, range(mid))
         if t < 2:
             mm("w0", "qu", "su", 0, "qx", "sx", 0, 128)
-            later.extend(choices("w0", 0, 128))
+        arrived(t, range(mid, 4))
+        if t < 2:
+            for b, name in enumerate(["w3", "w2", "w1", "p3"] * HALF):
+                unpack(0, b, name, 0, 128)
+                lay(0, b, name, 0, 128)
+            now([steps[k] for k in AHEAD_OF.split()])
         if t == 0:
             order("y", [("qz", 0, 128)], [])
             dma("y", [(T.vb[:, :], T.v[:, :])], [], [("vb", 0, 512)], "dv")
         if t == 2:
             codes_out(0)
-        ts(("xt", 515, 1024, 4), ("p0", 0, 128), 0.015625, A.mult)
+            product_out(0)
+        now([last_bank])
+        if t < 2:
+            now([steps[k] for k in BEHIND_OF.split()])
         quant("qx", "sx", 128, 128, "xt", 512)
 
     for t in range(3):
         one_round(t)
 
     codes_out(1)
-    product_out(0)
     dma("s", [(T.osc[4 * k:4 * k + 4, :], T.sx[32 * k:32 * k + 4, 0:256]) for k in range(4)], [("qx", 0, 256)], [], "dst")
     product_out(1)
     n = 0

from concourse.bass import DstId, RemoteDMATransfer
from concourse.mybir import dt, AluOpType as A, ActivationFunctionType as F

XOR = [1, 2, 4]
NREL = 2
PC = 128 // NREL
F8 = "float8_e4m3fn_x4"
BIG = 2.0 ** 90
M32 = 1.5 * 2.0 ** 31
LW = 160
BY_DMA = [(2, 3, 5, 6, 7), (3, 5, 6, 7), (3, 5, 6, 7)]
BY_G = [(4,), (4,), (4,)]
NV = 3
SEG = 66
OWN = 2048.0
LESS = 256.0 + OWN
SC, HALF = 2, 1
MID, AHEAD_OF, BEHIND_OF = [4, 4, 4], "", ""
KE = [0, 0, 0]
GV = [16, 16]
RA, RB, AB = ["p0", "p2", "p2"], ["p3", "p0", "p0"], ["p1", "p3", "p3"]
ROUND = ("scores TURN AHEAD turn block0 BEHIND ahead behind u0 l0 u1 FLAGS flags BACK u3 u2 back count aa u4 l1 v3 ob chosen free l2 u6 marks room ab "
         "marks2 table u5 count2 early v4 table2 floor refused ra compare u7 rb table4 l5 late sum LATE table3 LATE2 list mask first l7 high last taken low "
         "in_word of_word numbers MASK LIST HIGH FIRST l6 offsets LAST gather LOW TAKEN cross IN_WORD OF_WORD OFFSETS")
FIRST_ROUND = ("tot= all= scores turn block0 ct= zeros= behind ob= u2 mx0= mt= ahead qoa odd= flags turn0= aa= turn= u0 fills= kn0= back go= qtot u1 count ab= "
               "rb0= turns= gcopy kn1= slots= kn3= qob ob wrap= chosen step= free rb1= kn2= early marks room marks2 start= column= qall count2 vfloor rb2= kw1= "
               "vwb= qaa aa rb3= refused vwb2= kw2= qrb l1 rb compare qra kd= kj= mask= kw0= late ra sum qab l2 table3 l0 table mask list table4 ab qkd high "
               "table2 LATE2 first kw3= u3 LATE last taken low l3 qkj in_word qkw of_word GO= offsets gather MASK cross HIGH TAKEN ZEROS= SLOTS= LIST LAST LOW "
               "FIRST IN_WORD OF_WORD OFFSETS")

KN = {n: i for i, n in enumerate(["tot", "rb", "all", "oa", "ob", "aa", "ab", "kn", "kd", "kj", "kw", "ra"])}
REFUSED, CHOSEN, FIRST, LAST, FLOOR = 8, 72, 136, 264, 392
DG, FT, FB = 640, 1032, 1288
CMP, DIG = (0, 384), (256, 904)
QL, QD, QF = (256, 0), 128, 384


def sb(n, kind="bfloat16"):
    return ("sbuf", [128, n], kind)


SCRATCH = {
    "ub": sb(512), "vb": sb(512), "x0": sb(1024),
    "qu": sb(128, F8), "su": sb(128, "uint8"), "qv": sb(128, F8), "sv": sb(128, "uint8"),
    "qw": sb(512, F8), "sw": sb(512, "uint8"), "qx": sb(256, F8), "sx": sb(256, "uint8"),
    "eq": sb(4 * LW, F8), "es": sb(4 * LW, "uint8"),
    "kq": sb(128 * len(KN), F8), "kqs": sb(128 * len(KN), "uint8"), "ks": sb(512 * len(KN)),
    "jj": sb(512), "z1": sb(1024), "one": sb(72),
    "mx": sb(512), "ct": sb(512), "ct2": sb(512), "mt": sb(128), "mr": sb(256, "float32"), "i16": sb(16), "zmask": sb(128),
    "pc": sb(16, "int32"), "cf": sb(24, "float32"), "nk": sb(40, "float32"), "kb": sb(24, "float32"),
    "qu1": sb(128, F8), "su1": sb(128, "uint8"), "uo": sb(8, "uint16"), "go": sb(8, "uint16"),
    "rst": sb(256, "float32"), "inj": sb(SEG * NV, "float32"),
    "st": sb(260, "float32"), "rm": sb(256, "float32"), "fl": sb(1544),
    "tt": sb(456, "float32"), "free": sb(64, "float32"), "kv": sb(16, "float32"), "m64": sb(384), "r16": sb(16),
    "jk": sb(2688), "wb": sb(SEG * NV), "q2": sb(514, F8), "c2": sb(514, "uint8"), "q3": sb(128, F8), "c3": sb(128, "uint8"), "lf": sb(64, "uint16"),
    "win": sb(8192), "hk": sb(512), "hc": sb(512), "z64": sb(512), "x64": sb(512), "xt": sb(1024),
    "qz": sb(128, F8), "sz": sb(128, "uint8"), "yt": sb(256, "float32"),
    "omf": sb(144, "float32"),
}
for _h in range(2):
    SCRATCH.update({"ac%d" % _h: sb(8 * SEG, "float32"), "li%d" % _h: sb(8, "uint16"), "wd%d" % _h: sb(32, "float32")})
for _t in range(3):
    SCRATCH.update({"qy%d" % _t: sb(128, F8), "sy%d" % _t: sb(128, "uint8"), "lq%d" % _t: sb(128, F8), "ls%d" % _t: sb(128, "uint8"),
                    "rq%d" % _t: sb(PC, F8), "rs%d" % _t: sb(128, "uint8")})
PSUM = ["w0", "w1", "w2", "w3", "p0", "p1", "p2", "p3"]
for _b in PSUM:
    SCRATCH[_b] = ("psum", [128, 512], "float32")
SEMAPHORES = ["qg", "qv", "qs", "qp", "dx", "du", "dv", "dwc", "dws", "dst", "loc", "turn"] + \
    ["%s%d" % (n, t) for n in ("arr", "in") for t in range(3)]


def relays(topo, core, partner):
    able = [c for c in topo.cores_of(core) if c != core and topo.may_write(c, partner)]
    near = [c for c in able if topo.die(c) == topo.die(core)]
    far = [c for c in able if topo.die(c) != topo.die(core)]
    return [near[0], far[0], near[1]]


def bits(es):
    return sum(1 << e for e in es)


def hand_on(g, core, T, topo):
    mine = [c for c in topo.cores_of(core) if T.rank_of(c) is not None]
    if not mine:
        return
    home, sent = mine[0], 0
    for t in range(3):
        partner = T.cores[T.rank_of(home) ^ XOR[t]]
        rel = relays(topo, home, partner)
        if core not in rel:
            continue
        i = rel.index(core)
        rid, pid = topo.addr(partner, core)
        m, n = topo.mask(core, partner), len(topo.engines(core, partner))
        es = len(topo.engines(home, core))
        if i < NREL:
            out, in_, landed = T["lq%d" % t][:, PC * i:PC * i + PC].bitcast(dt.uint8), T["rq%d" % t][:, 0:PC].bitcast(dt.uint8), es // NREL
        else:
            out, in_, landed = T["ls%d" % t][:, 0:128], T["rs%d" % t][:, 0:128], es
        g.wait_ge(T.sem["in%d" % t], landed)
        g.remote_dma(out_ap=out, in_ap=in_, remote_sem=T.sem["arr%d" % t], local_sem=T.sem.loc, pid=pid, routing_id=rid, dma_engine_mask=m)
        sent += n
    if sent:
        g.wait_ge(T.sem.loc, sent)


def machine(g, T):
    eng = {"g": g, "v": g.vector, "s": g.scalar, "p": g.tensor, "y": g.sync}
    own = {"g": "qg", "v": "qv", "s": "qs", "p": "qp"}
    clock = {q: {} for q in eng}
    count, regs = {}, {}

    def wait(q, tok):
        sem, n, clk = tok
        if clock[q].get(sem, 0) < n:
            eng[q].wait_ge(T.sem[sem], n)
            clock[q][sem] = n
            for k in clk:
                if clk[k] > clock[q].get(k, 0):
                    clock[q][k] = clk[k]

    def full(r):
        return r if len(r) == 4 else (r[0], r[1], r[2], 1)

    def meet(lo, hi, st, r):
        if st == 1 and r[5] > 1:
            return any(lo <= c < hi for c in range(r[0], r[1], r[5]))
        if r[5] == 1 and st > 1:
            return any(r[0] <= c < r[1] for c in range(lo, hi, st))
        return r[0] < hi and lo < r[1] and not (st == r[5] and (lo - r[0]) % st)

    def inside(r, lo, hi, st):
        return lo <= r[0] and r[1] <= hi and (st == 1 or (st == r[5] and (lo - r[0]) % st == 0))

    def order(q, reads, writes):
        toks = []
        for n, lo, hi, st in map(full, reads):
            toks += [r[4] for r in regs.get(n, []) if (r[2] or (n in PSUM and r[3] != q)) and meet(lo, hi, st, r)]
        for n, lo, hi, st in map(full, writes):
            toks += [r[4] for r in regs.get(n, []) if (r[3] != q or q != "p") and meet(lo, hi, st, r)]
        best = {}
        for tok in toks:
            if tok[0] not in best or best[tok[0]][1] < tok[1]:
                best[tok[0]] = tok
        for tok in sorted(best.values(), key=lambda k: -len(k[2])):
            wait(q, tok)

    def note(q, tok, reads, writes):
        for n, lo, hi, st in map(full, reads):
            regs[n] = [r for r in regs.get(n, []) if not (r[3] == q and not r[2] and inside(r, lo, hi, st))]
            regs[n].append((lo, hi, False, q, tok, st))
        for n, lo, hi, st in map(full, writes):
            regs[n] = [r for r in regs.get(n, []) if not inside(r, lo, hi, st)]
            regs[n].append((lo, hi, True, q, tok, st))

    def op(q, call, reads, writes):
        order(q, reads, writes)
        sem = own[q]
        count[sem] = count.get(sem, 0) + 1
        call(eng[q]).then_inc(T.sem[sem], 1)
        note(q, (sem, count[sem], dict(clock[q])), reads, writes)

    def dma(q, pairs, reads, writes, sem):
        order(q, reads, writes)
        for out, in_ in pairs:
            count[sem] = count.get(sem, 0) + 16
            eng[q].dma_start(out, in_).then_inc(T.sem[sem], 16)
        note(q + sem, (sem, count[sem], dict(clock[q])), reads, writes)

    def arrive(sem, n, writes):
        note("far", (sem, n, {}), [], writes)

    def finish(extra):
        for sem in count:
            wait("y", (sem, count[sem], {}))
        for sem, n in extra:
            wait("y", (sem, n, {}))

    return op, dma, arrive, finish, order


def rank_program(g, core, T, topo):
    rank = T.rank_of(core)
    if rank is None:
        hand_on(g, core, T, topo)
        return
    op, dma, arrive, finish, order = machine(g, T)

    def ap(r):
        return T[r[0]][:, r[1]:r[2]:r[3]] if len(r) == 4 else T[r[0]][:, r[1]:r[2]]

    def bank(r):
        return (r[0], 0, 512) if r[0] in PSUM else r

    def mm(out, k, ks, a, q, s, b, n, start=True, stop=True):
        op("p", lambda e: e.matmul_mx(T[out][:, 0:n], T[k][:, a:a + 128], T[ks][:, a:a + 128], T[q][:, b:b + n], T[s][:, b:b + n], start, stop),
           [(k, a, a + 128), (q, b, b + n)], [(out, 0, 512)])

    def kmm(out, name, q, s, b, n=128, start=True, stop=True):
        mm(out, "kq", "kqs", 128 * KN[name], q, s, b, n, start, stop)

    def quant(q, s, a, n, src, b):
        op("v", lambda e: e.quantize_mx(T[q][:, a:a + n], T[s][:, a:a + n], T[src][:, b:b + 4 * n]),
           [(src, b, b + 4 * n)], [(q, a, a + n)])

    def kquant(name):
        quant("kq", "kqs", 128 * KN[name], 128, "ks", 512 * KN[name])

    def source(r, by):
        return (ap(r), [bank(r)]) if by is None else (ap(r).indirect(ap(by)), [r, by])

    def ts(out, in0, s1, o0, s2=None, o1=None):
        reads = [bank(r) for r in (in0, s1, s2) if isinstance(r, tuple)]
        a, b = [ap(r) if isinstance(r, tuple) else r for r in (s1, s2)]
        if o1 is None:
            op("v", lambda e: e.tensor_scalar(ap(out), ap(in0), a, None, o0), reads, [out])
        else:
            op("v", lambda e: e.tensor_scalar(ap(out), ap(in0), a, b, o0, o1), reads, [out])

    def tt(out, a, b, o, by=None):
        src, reads = source(a, by)
        op("v", lambda e: e.tensor_tensor(ap(out), src, ap(b), o), reads + [bank(b)], [out])

    def copy(out, in_, by=None):
        src, reads = source(in_, by)
        op("v", lambda e: e.tensor_copy(ap(out), src), reads, [out])

    def scan(out, d0, d1, o0, o1, first=0.0):
        column = isinstance(first, tuple)
        op("v", lambda e: e.tensor_tensor_scan(ap(out), ap(d0), ap(d1), ap(first) if column else first, o0, o1),
           [bank(d0), bank(d1)] + ([bank(first)] if column else []), [out])

    def turn(out, in_):
        op("v", lambda e: e.transpose(ap(out), ap(in_)), [bank(in_)], [out])

    def fill(r, val):
        op("v", lambda e: e.memset(ap(r), val), [], [r])

    def act(out, in_, func=F.Copy, by=None, scale=1.0, bias=0.0, **kw):
        src, reads = source(in_, by)
        if scale != 1.0:
            kw["scale"] = scale
        if bias != 0.0:
            kw["bias"] = bias
        reads += [kw[k] for k in ("scale", "bias") if isinstance(kw.get(k), tuple)]
        writes = [out] + ([kw["accum_out"]] if "accum_out" in kw else [])
        args = {k: ap(v) if isinstance(v, tuple) else v for k, v in kw.items()}
        op("s", lambda e: e.activation(ap(out), src, func, **args), reads, writes)

    def sfill(r, val):
        act(r, ("z1", 0, len(range(*r[1:]))), F.Identity, scale=0.0, bias=val)

    def iota(r, pattern, base, cmul):
        kw = {} if r[0] == "pc" else {"allow_small_or_imprecise_dtypes": True}
        op("g", lambda e: e.iota(ap(r), pattern, base, cmul, **kw), [], [r])

    def keep(out, in_, pattern, base, cmul, other=0.0):
        op("g", lambda e: e.affine_select(ap(out), ap(in_), pattern, A.is_ge, other, base, cmul), [in_], [out])

    def slot(name):
        return ("ks", 512 * KN[name], 512 * KN[name] + 512)

    def pc(i):
        return ("pc", i, i + 1)

    def cf(i):
        return ("cf", i, i + 1)

    def run(a, n=64):
        return ("tt", a, a + n)

    later = []

    def now(calls):
        for call in calls:
            call[0](*call[1:])

    def gap(n=1):
        now(later[:n])
        del later[:n]

    dma("s", [(T.ub[:, :], T.u[:, :])], [], [("ub", 0, 512)], "du")
    dma("y", [(T.x0[:, :], T.x[:, :])], [], [("x0", 0, 1024)], "dx")

    iota(pc(0), [[0, 1]], 0, 1)
    iota(("jj", 0, 128), [[1, 128]], 0, 0)
    fill(("m64", 0, 64), -OWN)
    keep(("m64", 64, 128), ("m64", 0, 64), [[-16, 16], [128, 4]], 0, 1)
    keep(("m64", 128, 192), ("m64", 64, 128), [[16, 16], [-128, 4]], 15, -1, 1.0)
    fill(("z1", 0, 4 * LW + 4), 0.0)
    ts(pc(1), pc(0), 15, A.bitwise_and)
    ts(pc(2), pc(0), 4, A.arith_shift_right)
    ts(pc(3), pc(0), 3, A.bitwise_and)
    ts(pc(4), pc(0), 2, A.arith_shift_right, 3, A.bitwise_and)
    ts(pc(5), pc(0), 1, A.arith_shift_right, 7, A.bitwise_and)
    fill(("one", 0, 72), 1.0)
    copy(("cf", 0, 6), ("pc", 0, 6))
    fill(("rst", 0, 128), BIG)
    ts(("nk", 0, 18), ("jj", 0, 18), -2.0, A.add, cf(1), A.is_equal)
    ts(("z1", 3, 512, 4), ("jj", 0, 128), cf(0), A.is_equal, 64.0, A.mult)
    ts(("z1", 515, 4 * LW + 4, 4), ("jj", 0, LW - 127), cf(0), A.is_equal, 64.0, A.mult)
    tt(("nk", 24, 32), ("nk", 2, 18, 2), ("nk", 0, 16, 2), A.subtract)
    quant("qu1", "su1", 0, 128, "ub", 0)
    ts(("uo", 0, 8), ("jj", 0, 8), 16.0, A.mult, cf(5), A.add)
    unpacking = [(quant, "eq", "es", LW * b, LW, "z1", 3 - b) for b in range(4)]
    now(unpacking[:1])
    op("v", lambda e: e.tensor_copy(T.qu[:, 0:128].bitcast(dt.uint32), T.qu1[:, 0:128].bitcast(dt.uint32).indirect(T.uo[:, 0:8])),
       [("qu1", 0, 128), ("uo", 0, 8)], [("qu", 0, 128)])
    act(cf(6), cf(1), F.Identity, bias=0.5 - LESS)
    act(cf(8), cf(2), F.Identity, scale=4.0)
    act(cf(16), cf(1), F.Identity, scale=16.0, bias=-256.0)
    act(("kb", 0, 16), ("jj", 0, 16), F.Identity, scale=16.0, bias=cf(6))

    def by_group(name, pattern, groups=range(8)):
        a = slot(name)[1]
        for c in groups:
            act(("ks", a + 64 * c, a + 64 * c + 64), pattern, F.Identity, scale=("nk", 24 + c, 25 + c))

    by_group("oa", ("m64", 128, 192), range(2))
    op("s", lambda e: e.activation(T.su[:, 0:128], T.su1[:, 0:128].indirect(T.uo[:, 0:8]), F.Copy), [("qu1", 0, 128), ("uo", 0, 8)], [("su", 0, 128)])
    order("p", [("su", 0, 128)], [])
    by_group("oa", ("m64", 128, 192), range(2, 8))
    quant("qx", "sx", 0, 256, "x0", 0)
    fill(("rst", 0, 128, 8), -BIG)
    now(unpacking[1:])

    def behind(name, first):
        keep(slot(name), slot("tot"), [[0, 8], [-16, 16], [128, 4]], -16 * (first + 1), 1)

    dma("y", [(T.qw[:, :].bitcast(dt.uint8), T.wc[:, :])], [], [("qw", 0, 512)], "dwc")
    dma("y", [(T.sw[:, :], T.ws[:, :])], [], [("sw", 0, 512)], "dws")

    def turned(k):
        return [(T.win[0:128 - 16 * k, 1024 * k:1024 * k + 1024], T.win[16 * k:128, 0:1024]),
                (T.win[128 - 16 * k:128, 1024 * k:1024 * k + 1024], T.win[0:16 * k, 0:1024])]

    def g_copies(t):
        order("g", [slot("ab")], [])
        for k in BY_G[t]:
            for i, (out, in_) in enumerate(turned(k)[:2 if t else 1]):
                op("g", lambda e: e.affine_select(out, in_, [[0, 1024]], A.is_ge, 0.0, 0, 0), [("win", 0, 1024)],
                   [("win", 1024 * k + 512 * i, 1024 * k + 512 * i + 512)])

    def fills():
        sfill(("inj", 0, SEG * NV), BIG)
        sfill(("ac1", SEG * NV, SEG * 8), 0.0)

    def slots(h):
        act(("mr", 128 * h, 128 * h + 128), ("jj", 0, 128), F.Identity, bias=128.0 * h - LESS)

    made = {
        "odd=": (fill, ("fl", FB + 1, FB + 256, 2), 0.0),
        "zeros=": (fill, ("fl", DG, FT), 0.0),
        "ZEROS=": (fill, ("fl", DIG[0] + 3, DIG[0] + 128, 4), 0.0),
        "turn=": (ts, pc(6), pc(0), cf(2), A.subtract),
        "turn0=": (ts, pc(7), pc(2), -1.0, A.mult, 8.0, A.add),
        "turns=": (ts, ("pc", 8, 10), ("pc", 6, 8), 7, A.bitwise_and),
        "wrap=": (ts, cf(11), pc(8), 7.0, A.is_equal, -8192.0, A.mult),
        "step=": (act, cf(13), cf(11), F.Identity, None, 1.0, 1024.0),
        "column=": (ts, cf(12), ("nk", 9, 10), ("nk", 17, 18), A.add, 4.0, A.mult),
        "start=": (ts, cf(14), pc(9), 1024.0, A.mult, cf(3), A.add),
        "go=": (ts, ("go", 2, 4), ("jj", 0, 8, 4), cf(4), A.add, float(SEG), A.mult),
        "GO=": (ts, ("go", 0, 2), ("jj", 0, 8, 4), cf(4), A.add),
        "mask=": (ts, ("zmask", 0, 32), ("mt", 0, 32), cf(4), A.is_equal, 8.0, A.mult),
        "rb=": (ts, slot("rb"), ("mx", 0, 512), cf(1), A.is_lt),
        "rb0=": (ts, ("ks", slot("rb")[1], slot("rb")[1] + 64), ("mx", 0, 64), cf(1), A.is_lt),
        "mx0=": (iota, ("mx", 0, 64), [[1, 16], [-100, 4]], 100, 0),
        "kd=": (act, slot("kd"), slot("kn"), F.Identity, None, cf(13)), "kj=": (act, slot("kj"), slot("kn"), F.Identity, None, cf(12)),
        "fills=": (fills,), "slots=": (slots, 1), "SLOTS=": (slots, 0),
        "ob=": (keep, slot("ob"), ("ks", slot("oa")[1] - 2, slot("oa")[2] - 2), [[0, 128], [1, 4]], -2, 0),
        "tot=": (by_group, "tot", ("one", 0, 64)), "aa=": (behind, "aa", 0), "ab=": (behind, "ab", 16),
        "ct=": (iota, ("ct", 0, 128), [[1, 32], [0, 4]], 0, 0), "mt=": (iota, ("mt", 0, 32), [[0, 8], [1, 4]], 0, 0),
        "wb=": (now, [(iota, ("wb", 64, SEG * NV, SEG), [[0, NV]], -64, 0), (iota, ("wb", 65, SEG * NV, SEG), [[0, NV]], 1000, 0)]),
        "vwb=": (fill, ("wb", 64, SEG * NV, SEG), -64.0), "vwb2=": (fill, ("wb", 65, SEG * NV, SEG), 1000.0),
        "all=": (keep, slot("all"), ("z1", 1, 513), [[16, 8], [0, 16], [128, 4]], 15 - 384, -1, -1.0),
        "mx=": (iota, ("mx", 0, 512), [[0, 8], [1, 16], [-100, 4]], 100, 0), "gcopy": (g_copies, 0),
    }
    for i in range(3):
        a = slot("rb")[1]
        made["rb%d=" % (i + 1)] = (copy, ("ks", a + (64 << i), a + (128 << i)), ("ks", a, a + (64 << i)))
    for b in range(4):
        made["kw%d=" % b] = (ts, ("ks", slot("kw")[1] + b, slot("kw")[2], 4), ("ct", 0, 128), cf(3), A.subtract, cf(8), A.is_equal)
        made["kn%d=" % b] = (ts, ("ks", slot("kn")[1] + b, slot("kn")[2], 4), ("ct", 0, 128), -float(b), A.add, cf(8), A.is_equal)
    made.update({"q" + name: (kquant, name) for name in KN})
    made["qra"] = (quant, "kq", "kqs", 128 * KN["ra"], 128, "ks", 512 * KN["rb"] + 1)

    def unpack(d, b, name, a=0, n=256):
        mm(name, "eq", "es", LW * b + 16 * d, "qx", "sx", a, n)

    def lay(d, b, name, a=0, n=256):
        act(("win", 1024 * d + 4 * a + b, 1024 * d + 4 * (a + n), 4), (name, 0, n), F.Identity, scale=0.015625)

    def copies(t):
        rest = [] if t else BY_G[t]
        dma("y", [pair for k in BY_DMA[t] for pair in turned(k)] + [turned(k)[1] for k in rest], [("win", 0, 1024)],
            [("win", 1024 * k, 1024 * k + 1024) for k in BY_DMA[t]] + [("win", 1024 * k + 512, 1024 * k + 1024) for k in rest], "turn")
        if t:
            g_copies(t)

    def choices(name, a, n):
        ahead, behind = ("rm", a, a + n // 2), ("rm", a + n // 2, a + n)

        def backwards():
            op("v", lambda e: e.tensor_tensor_scan(T.rm[:, a + n - 1:a + n // 2 - 1:-1], T.rst[:, 0:n // 2], T.st[:, a + n - 2:a - 2 if a else None:-2],
                                                   0.0, A.min, A.max), [("rst", 0, n // 2), ("st", a, a + n)], [behind])
        return [(turn, ("st", a, a + n), (name, 0, n)),
                (scan, ahead, ("rst", 0, n // 2), ("st", a, a + n, 2), A.min, A.max), (backwards,),
                (tt, ("fl", FB + a, FB + a + n, 2), ahead, behind, A.is_ge),
                (turn, ("fl", FT + a, FT + a + n), ("fl", FB + a, FB + a + n))]

    def signs(h, k, first, n, junk, total):
        act(("jk", junk, junk + n), run(first, n), F.Sign, bias=("kb", 8 * h + k, 8 * h + k + 1), scale=-1.0, accum_out=total)

    def digits(h):
        return ("q3", "c3", 0) if h else ("q2", "c2", QL[0] + 64)

    def places(h, out):
        li, wd, at = "li%d" % h, ("wd%d" % h, 0, 32), CMP[h]
        acc, k = ("ac1", 64, 8 * SEG, SEG) if h else ("ac0", 16, 24), ("mr", 128 * h, 128 * h + 128)

        def digit(b):
            return ("fl", DIG[h] + b, DIG[h] + 128, 4)

        def in_word():
            quant("q2", "c2", QL[h], 128, "fl", at)
            for name in ("kd", "kj"):
                for b in (0, 32):
                    kmm(out, name, "q2", "c2", QL[h] + b, 128, (name, b) == ("kd", 0), False)

        def of_word():
            if h:
                quant("q3", "c3", 0, 128, "fl", DIG[h])
            kmm(out, "kw", *digits(h), 128, False, True)
        return {"list": (ts, (li, 0, 8), acc, 0.5, A.mult, 64.0, A.add),
                "mask": (tt, wd, acc[:3], ("zmask", 0, 32), A.mult, ("go", 2 * h, 2 * h + 2)),
                "high": (ts, digit(0), wd, M32, A.add, -M32, A.add),
                "low": (tt, digit(1), wd, digit(0), A.subtract),
                "taken": (ts, digit(2), wd, 0.0, A.is_gt, -1024.0, A.mult),
                "first": (tt, ("fl", at, at + 128), run(FIRST, 128), k, A.is_le, (li, 0, 8)),
                "last": (tt, ("fl", at + 128, at + 256), run(LAST, 128), k, A.is_le, (li, 0, 8)),
                "in_word": (in_word,), "of_word": (of_word,),
                "offsets": (ts, ("lf", 32 * h, 32 * h + 32), (out, 0, 32), cf(14), A.add, 1024.0, A.add)}

    def gather(h, dst):
        k = GV[h]
        act((dst, 16 * k, 512), ("win", 0, 8192), by=("lf", 32 * h + k, 32 * h + 32))
        copy((dst, 0, 16 * k), ("win", 0, 8192), by=("lf", 32 * h, 32 * h + k))

    def numbers(h):
        name = "p%d" % (1 + h)
        kmm(name, "kn", "q2", "c2", QL[h], 128, True, False)
        kmm(name, "kn", "q2", "c2", QL[h] + 32, 128, False, False)
        for i in range(2):
            kmm(name, "kw", *digits(h), 128, False, i == 1)

    def numbers_laid():
        for h in range(2):
            act(("omf", 32 * h, 32 * h + 32), ("p%d" % (1 + h), 0, 32), F.Identity, bias=2048.0)
        return [(turn, ("omf", 64, 128), ("omf", 0, 64)), (numbers_out,)]

    def numbers_out():
        copy(("omf", 128, 144), ("omf", 64, 128, 4))
        dma("y", [(T.om[c:8:2, 128 * h:128 * h + 128], T.omf[:, 128 + 8 * h + 4 * c:132 + 8 * h + 4 * c]) for h in range(2) for c in range(2)],
            [("omf", 128, 144)], [], "dst")

    def codes_out(h):
        a = 128 * h
        dma("y", [(T.oc[:, 4 * a:4 * a + 512], T.qx[:, a:a + 128].bitcast(dt.uint8))], [("qx", a, a + 128)], [], "dst")

    def product_out(h):
        a, name = 128 * h, "w%d" % h
        mm(name, "qv", "sv", 0, "qx", "sx", a, 128)
        (copy if h else act)(("yt", a, a + 128), (name, 0, 128))
        dma("y" if h else "s", [(T.y[:, a:a + 128], T.yt[:, a:a + 128])], [("yt", a, a + 128)], [], "dst")

    def send(t):
        qy, sy = "qy%d" % t, "sy%d" % t
        rel = relays(topo, core, T.cores[rank ^ XOR[t]])
        order("g", [(qy, 0, 128)], [])
        moves = []
        for i, c in enumerate(rel[:NREL]):
            rid, pid = topo.addr(c, core)
            es = topo.engines(core, c)
            k = len(es) // NREL
            moves.append(RemoteDMATransfer(dst_ids=[DstId(rid=rid, pnc=pid)], dma_engine_mask=bits(es[k * i:k * i + k]),
                                           remote_sem=T.sem["in%d" % t], src=T[qy][:, PC * i:PC * i + PC].bitcast(dt.uint8),
                                           dst=T["rq%d" % t][:, 0:PC].bitcast(dt.uint8)))
        g.remote_dma_fused(moves, local_sem=T.sem.loc)
        rid, pid = topo.addr(rel[NREL], core)
        g.remote_dma(out_ap=T["rs%d" % t][:, 0:128], in_ap=T[sy][:, 0:128], remote_sem=T.sem["in%d" % t], local_sem=T.sem.loc,
                     pid=pid, routing_id=rid, dma_engine_mask=topo.mask(core, rel[NREL]))

    def arrived(t, bs):
        lq, ls = "lq%d" % t, "ls%d" % t
        for b in bs:
            name = "p%d" % (3 - b)
            mm(name, "qw", "sw", 128 * b, lq, ls, 0, 128, True, False)
            mm(name, "eq", "es", LW * b, lq, ls, 0, 128, False, True)
            if b < 3:
                act(("xt", 512 + b, 1024, 4), (name, 0, 128), F.Identity, scale=0.015625)

    def one_round(t):
        a, n = (0, 256) if t == 0 else (128, 128)

        def block0():
            for b in range(4):
                unpack(0, b, "w%d" % (3 - b), *((a, n) if HALF else (0, 256)))
                lay(0, b, "w%d" % (3 - b), *((a, n) if HALF else (0, 256)))
            copies(t)

        def count():
            quant("q2", "c2", QF, 128, "fl", FT)
            kmm("p1", "tot", "q2", "c2", QF)
            kmm("p0", "oa", "q2", "c2", QF)

        def count2():
            quant("q2", "c2", QD, 128, "fl", DG)
            kmm("p1", "all", "q2", "c2", QD)

        def refused():
            op("v", lambda e: e.tensor_tensor_scan(T.tt[:, REFUSED + 63:REFUSED - 1:-1], T.p1[:, 64:0:-1], ap(run(FLOOR)), -OWN, A.add, A.max),
               [bank(("p1",)), run(FLOOR)], [run(REFUSED)])

        early = KE[t]

        def kept_late(k):
            if k < early:
                return (signs, 0, k, REFUSED, 64, 128 * k, ("ac0", 8 + k, 9 + k))
            return (signs, 0, k, REFUSED, 128, 128 * k, ("ac0", 16 + k, 17 + k))

        def cross():
            quant("qy%d" % t, "sy%d" % t, 0, 128, "hc", 0)
            send(t)

        def table(a, counts, name):
            return (tt, run(a), run(counts), (name, 0, 64), A.subtract)

        steps = dict(made)
        steps.update(places(1, "w0"))
        steps.update({k.upper(): v for k, v in places(0, "p0").items()})
        steps.update(zip(["turn", "ahead", "behind", "flags", "back"], choices("p0", a, n)))
        steps.update(zip(["TURN", "AHEAD", "BEHIND", "FLAGS", "BACK"], choices("w0", 0, 128)))
        for i, name in enumerate(["w3", "w2", "w1", "p3"] * 2 if t else ["w3", "w2", "w1"] * 3):
            steps.update({"u%d" % i: (unpack, 1 + i // 4, i % 4, name), "l%d" % i: (lay, 1 + i // 4, i % 4, name),
                          "v%d" % i: (ts, ("win", 1024 * (1 + i // 4) + i % 4, 1024 * (2 + i // 4), 4), (name, 0, 256), 0.015625, A.mult)})
        steps.update({
            "scores": (mm, "p0", "qu", "su", 0, "qx", "sx", a, n), "block0": (block0,), "count": (count,), "count2": (count2,),
            "ob": (kmm, "w0", "ob", "q2", "c2", QF), "aa": (kmm, "p2", "aa", "q2", "c2", QF), "ab": (kmm, AB[t], "ab", "q2", "c2", QF),
            "ra": (kmm, RA[t], "ra", "q2", "c2", QD), "rb": (kmm, RB[t], "rb", "q2", "c2", QD),
            "chosen": (scan, run(CHOSEN), ("one", 0, 64), ("p1", 0, 64), A.mult, A.add, -LESS),
            "marks": (tt, ("fl", DG, DG + 256, 4), run(CHOSEN), ("p0", 0, 64), A.is_gt),
            "marks2": (tt, ("fl", DG + 1, DG + 256, 4), run(CHOSEN), ("w0", 0, 64), A.is_gt),
            "free": (scan, ("free", 0, 64), ("one", 0, 64), ("p1", 0, 64), A.mult, A.add, cf(16)),
            "room": (ts, ("fl", DG + 259, DG + 260), ("free", 63, 64), 0.0, A.min, -16.0, A.max),
            "vfloor": (ts, run(FLOOR), ("one", 0, 64), run(CHOSEN + 63, 1), A.mult),
            "floor": (act, run(FLOOR), ("one", 0, 64), F.Identity, None, run(CHOSEN + 63, 1)), "refused": (refused,),
            "table": table(FIRST, CHOSEN, "p2"), "table2": table(LAST, CHOSEN, AB[t]),
            "table3": table(FIRST + 64, REFUSED, RA[t]), "table4": table(LAST + 64, REFUSED, RB[t]),
            "early": (now, [(signs, 1, k, CHOSEN, 64, 2048 + 64 * k, ("inj", SEG * k, SEG * k + 1)) for k in range(NV)]),
            "late": (now, [(signs, 1, k, REFUSED, 128, 1024 + 128 * k, ("ac1", SEG * k + 64, SEG * k + 65)) for k in range(NV, 8)]),
            "compare": (now, [(ts, ("wb", SEG * k, SEG * k + 64), run(REFUSED), ("kb", 8 + k, 9 + k), A.is_le, 2.0, A.mult) for k in range(NV)]),
            "sum": (scan, ("ac1", 0, SEG * NV), ("inj", 0, SEG * NV), ("wb", 0, SEG * NV), A.min, A.add, 1000.0),
            "EARLY": (now, [(signs, 0, k, CHOSEN, 64, 128 * k + 64, ("ac0", k, k + 1)) for k in range(early)]),
            "LATE": (now, [kept_late(k) for k in range(4)]), "LATE2": (now, [kept_late(k) for k in range(4, 8)]),
            "SUM": (tt, ("ac0", 16, 16 + early), ("ac0", 0, early), ("ac0", 8, 8 + early), A.add) if early else (now, []),
            "gather": (gather, 1, "hc"), "cross": (cross,), "numbers": (numbers, 1) if t == 2 else (now, [])})
        now([steps[k] for k in (ROUND if t else FIRST_ROUND).split()])
        if t == 0:
            order("p", [("sw", 0, 512)], [])
        if t == 1:
            later.extend([(quant, "qv", "sv", 0, 128, "vb", 0), (kquant, "kn")])
        if t == 2:
            numbers(0)
        gap()
        gather(0, "hk")
        gap()
        if t == 2:
            later.extend(numbers_laid())
        quant("qz", "sz", 0, 128, "hk", 0)
        gap()
        for b in range(4):
            act(("z64", b, 512, 4), ("hk", b, 512, 4), F.Identity, scale=64.0)
            mm("w%d" % b, "qw", "sw", 128 * b, "qz", "sz", 0, 128)
        arrive("arr%d" % t, sum(len(topo.engines(c, core)) for c in relays(topo, T.cores[rank ^ XOR[t]], core)), [("lq%d" % t, 0, 128)])
        gap()
        for b in range(4):
            tt(("x64", b, 512, 4), ("w%d" % b, 0, 128), ("z64", b, 512, 4), A.add)
            if SC == 1:
                act(("xt", b, 512, 4), ("x64", b, 512, 4), F.Identity, scale=0.015625)
        gap()
        if SC == 0:
            ts(("xt", 0, 512), ("x64", 0, 512), 0.015625, A.mult)
        if SC == 2:
            for b in range(4):
                ts(("xt", b, 512, 4), ("x64", b, 512, 4), 0.015625, A.mult)
        last_bank = (ts, ("xt", 515, 1024, 4), ("p0", 0, 128), 0.015625, A.mult)
        quant("qx", "sx", 0, 128, "xt", 0)
        mid = MID[t]
        arrived(t, range(mid))
        if t < 2:
            mm("w0", "qu", "su", 0, "qx", "sx", 0, 128)
        arrived(t, range(mid, 4))
        if t < 2:
            for b, name in enumerate(["w3", "w2", "w1", "p3"] * HALF):
                unpack(0, b, name, 0, 128)
                lay(0, b, name, 0, 128)
            now([steps[k] for k in AHEAD_OF.split()])
        if t == 0:
            order("y", [("qz", 0, 128)], [])
            dma("y", [(T.vb[:, :], T.v[:, :])], [], [("vb", 0, 512)], "dv")
        if t == 2:
            codes_out(0)
            product_out(0)
        now([last_bank])
        if t < 2:
            now([steps[k] for k in BEHIND_OF.split()])
        quant("qx", "sx", 128, 128, "xt", 512)

    for t in range(3):
        one_round(t)

    codes_out(1)
    dma("s", [(T.osc[4 * k:4 * k + 4, :], T.sx[32 * k:32 * k + 4, 0:256]) for k in range(4)], [("qx", 0, 256)], [], "dst")
    product_out(1)
    n = 0
    for t in range(3):
        rel = relays(topo, core, T.cores[rank ^ XOR[t]])
        n += sum(len(topo.engines(core, c)) // NREL for c in rel[:NREL]) + len(topo.engines(core, rel[NREL]))
    finish([("loc", n)])
